import numpy as np
import ml_dtypes


def mxq(x, axis, fmt="e4m3"):
    dtype, down = {"e4m3": (ml_dtypes.float8_e4m3fn, 7), "e5m2": (ml_dtypes.float8_e5m2, 14)}[fmt]
    v = np.moveaxis(np.asarray(x, np.float32).astype(ml_dtypes.bfloat16).astype(np.float64), axis, -1)
    blocks = v.reshape(v.shape[:-1] + (-1, 32))
    amax = np.abs(blocks).max(-1, keepdims=True)
    byte = np.maximum(np.where(amax > 0, np.frexp(amax)[1] - 1 + 127, 0) - down, 1)
    scale = np.exp2(byte - 127.0)
    codes = (blocks / scale).astype(np.float32).astype(dtype).astype(np.float64)
    return np.moveaxis((codes * scale).reshape(v.shape), -1, axis)


WIDE = False


def mx_kscale(k):
    if not WIDE:
        return np.ones(k)
    levels = np.array([10, -10, 5, -5, 0])
    if k % 512:
        return np.exp2(np.random.permutation(np.resize(levels, k // 32))).repeat(32)
    a = np.empty((k // 512, 16))
    for p in range(k // 512):
        a[p, :8] = np.random.permutation(np.resize(levels, 8))
        for g in range(8):
            far = levels[np.abs(levels - a[p, g]) >= 10]
            a[p, g + 8] = far[np.random.randint(len(far))]
    return np.exp2(a.ravel()).repeat(32)


BF16 = ml_dtypes.bfloat16


def bf(x):
    return np.asarray(x, np.float32).astype(BF16)


def f64(x):
    return np.asarray(x).astype(np.float64)

E4M3FN = np.array([(-1.0 if i & 128 else 1.0) * ((1.0 + (i & 7) / 8.0) * 2.0 ** (((i >> 3) & 15) - 7) if i & 120 else (i & 7) * 2.0 ** -9) for i in range(256)])


def e4m3fn_bytes(y):
    return np.clip(np.asarray(y, np.float64), -448.0, 448.0).astype(np.float32).astype(ml_dtypes.float8_e4m3fn).view(np.uint8)


def e4m3fn_values(b):
    return E4M3FN[b]


Q, T, K = 512, 4096, 2048


def setup_inputs():
    s = mx_kscale(K)
    length = np.random.uniform(0.5, 1.5, (T, 1))
    keys = np.random.standard_normal((T, K)) * length * s
    scale = (np.abs(keys).max(axis=1, keepdims=True) / 448).astype(np.float32)
    return {"query": bf(np.random.standard_normal((Q, K)) / np.sqrt(K) / s),
            "keys_bytes": e4m3fn_bytes(keys / f64(scale)),
            "keys_scale": scale,
            "age": bf(np.random.exponential(2.0, T)),
            "rate": bf(0.2 + 0.3 * np.abs(np.random.standard_normal(Q)))}


def reference(query, keys_bytes, keys_scale, age, rate):
    keys = e4m3fn_values(keys_bytes) * np.repeat(f64(keys_scale), K, axis=1)
    match = mxq(f64(query), 1, "e4m3") @ mxq(keys, 1, "e4m3").T
    staleness = np.log(1.0 + f64(age))
    return match - f64(rate)[:, None] * staleness[None, :]

@@ -1,0 +1,274 @@
+from contextlib import ExitStack
+
+import concourse.mybir as mybir
+from concourse.masks import make_identity
+
+Q, T, K = 512, 4096, 2048
+FLOPS = 2 * Q * T * K
+
+F32 = mybir.dt.float32
+BF16 = mybir.dt.bfloat16
+U32 = mybir.dt.uint32
+U8 = mybir.dt.uint8
+FP8 = mybir.dt.float8_e4m3fn
+FP8X4 = mybir.dt.float8_e4m3fn_x4
+MULT = mybir.AluOpType.mult
+ADD = mybir.AluOpType.add
+COPY = mybir.ActivationFunctionType.Copy
+LN = mybir.ActivationFunctionType.Ln
+
+P = 128
+PASS = 512
+G = K // PASS
+PAIRS = PASS // 2
+CHUNK = 512
+NT = CHUNK // P
+NC = T // CHUNK
+M = Q // P
+
+SCALAR_WIDTHS = (K, PASS)
+
+RAW_BUFS = 5
+WIDE_BUFS = 4
+TURN_BANKS = 5
+SUM_BANKS = 3
+WARM_UP_HEAD = 14
+
+
+def tile_aged_key_retrieval_d3_kernel(tc, query, keys_bytes, keys_scale, age, rate, out):
+    nc = tc.nc
+    with ExitStack() as ctx:
+        const = ctx.enter_context(tc.tile_pool(name="const", bufs=1))
+        raw_pool = ctx.enter_context(tc.tile_pool(name="raw", bufs=RAW_BUFS))
+        wide_pool = ctx.enter_context(tc.tile_pool(name="wide", bufs=WIDE_BUFS))
+        turned_pool = ctx.enter_context(tc.tile_pool(name="turned", bufs=2))
+        code_pool = ctx.enter_context(tc.tile_pool(name="code", bufs=2))
+        result_pool = ctx.enter_context(tc.tile_pool(name="result", bufs=6))
+        turn_psum = ctx.enter_context(tc.psum_pool(name="turn", bufs=TURN_BANKS))
+        sum_psum = ctx.enter_context(tc.psum_pool(name="sum", bufs=SUM_BANKS))
+
+        ident = const.tile([P, P], F32, name="ident")
+        zeros = const.tile([P, CHUNK], BF16, name="zeros")
+        scale_first = const.tile([P, NT], F32, name="scale_first")
+        scale_rest = const.tile([P, NC - 1, NT], F32, name="scale_rest")
+        age_sb = const.tile([P, T // P], BF16, name="age_sb")
+        stale_sb = const.tile([P, T // P], F32, name="stale_sb")
+        stale = const.tile([P, T], F32, name="stale")
+        rate_sb = const.tile([P, M], BF16, name="rate_sb")
+        neg_rate = const.tile([P, M], F32, name="neg_rate")
+        query_sb = const.tile([P, M, K], BF16, name="query_sb")
+        q_codes = const.tile([P, M, G, P], U32, name="q_codes", align_bytes=64)
+        q_scales = const.tile([P, M, G, P], U8, name="q_scales", align_bytes=64)
+
+        key_view = keys_bytes.rearrange("(c p i) k -> c p i k", p=P, i=NT)
+        scale_view = keys_scale.rearrange("(c p i) o -> p c (i o)", p=P, i=NT)
+        query_view = query.rearrange("(p m) k -> p m k", m=M)
+        out_view = out.rearrange("(p m) n -> p m n", m=M)
+        park = out[Q - 1 : Q, :]
+
+        raw, natural, split, turned, codes, banks, sums = {}, {}, {}, {}, {}, {}, {}
+
+        def load_keys(c, parts):
+            raw[c] = raw_pool.tile([P, NT, K], U8, name="raw_keys")
+            n = NT // parts
+            for i in range(0, NT, n):
+                nc.sync.dma_start(out=raw[c][:, i : i + n, :], in_=key_view[c][:, i : i + n, :])
+
+        def load_stale(c):
+            cols = slice(CHUNK * c, CHUNK * (c + 1))
+            nc.sync.dma_start(out=stale[:, cols], in_=park[0, cols].partition_broadcast(P))
+
+        def scale_col(c, i):
+            return scale_first[:, i : i + 1] if c == 0 else scale_rest[:, c - 1, i : i + 1]
+
+
+        def widen_scalar(c):
+            natural[c] = wide_pool.tile([P, sum(SCALAR_WIDTHS)], BF16, name="natural")
+            for i, width in enumerate(SCALAR_WIDTHS):
+                nc.scalar.activation(
+                    out=natural[c][:, K * i : K * i + width],
+                    in_=raw[c][:, i, :width].bitcast(FP8),
+                    func=COPY,
+                    scale=scale_col(c, i),
+                )
+
+        def widen_vector(c, i):
+            if i == 1:
+                split[c] = wide_pool.tile([P, NT - 1, 2, K // 4, 2], BF16, name="split")
+            k0 = SCALAR_WIDTHS[i] if i < len(SCALAR_WIDTHS) else 0
+            nc.vector.tensor_scalar(
+                out=split[c][:, i - 1, :, k0 // 4 :, :].rearrange("p u w e -> p w u e"),
+                in0=raw[c][:, i, k0:].bitcast(FP8).rearrange("p (w u e) -> p w u e", u=2, e=2),
+                scalar1=scale_col(c, i),
+                scalar2=None,
+                op0=MULT,
+            )
+
+
+        def natural_pairs(row, g, u):
+            return row.bitcast(F32)[:, PAIRS * g + u : PAIRS * (g + 1) : 2]
+
+        def key_pairs(c, i, g, u):
+            if i < len(SCALAR_WIDTHS) and PASS * g < SCALAR_WIDTHS[i]:
+                return natural_pairs(natural[c][:, K * i : K * i + SCALAR_WIDTHS[i]], g, u)
+            half = split[c][:, i - 1, u].rearrange("p w e -> p (w e)").bitcast(F32)
+            return half[:, P * g : P * (g + 1)]
+
+        def turn_keys(c, b):
+            g, h = divmod(b, 2)
+            bank = turn_psum.tile([P, 2, 2, P], F32, name="bank")
+            banks[c, b] = bank
+            for j in range(2):
+                for u in range(2):
+                    nc.tensor.transpose(bank[:, u, j, :], key_pairs(c, 2 * h + j, g, u), ident[:])
+
+        def empty_keys(c, b):
+            g, h = divmod(b, 2)
+            if b == 0:
+                turned[c] = turned_pool.tile([P, G, CHUNK, 4], BF16, name="turned_rows", align_bytes=64)
+            nc.scalar.copy(
+                out=turned[c][:, g, 2 * P * h : 2 * P * (h + 1), :].bitcast(F32),
+                in_=banks[c, b][:].rearrange("p u j r -> p (j r) u"),
+            )
+
+        def turn_query(m, h):
+            bank = turn_psum.tile([P, 2, 2, P], F32, name="bank")
+            banks["query", m, h] = bank
+            for j in range(2):
+                for u in range(2):
+                    nc.tensor.transpose(bank[:, j, u, :], natural_pairs(query_sb[:, m, :], 2 * h + j, u), ident[:])
+
+        def empty_query(m, h):
+            if m == 0 and h == 0:
+                turned["query"] = turned_pool.tile([P, M, G * P, 4], BF16, name="turned_rows", align_bytes=64)
+            dst = turned["query"][:, m, 2 * P * h : 2 * P * (h + 1), :].bitcast(F32)
+            nc.scalar.copy(
+                out=dst.rearrange("p (j r) u -> p j r u", j=2),
+                in_=banks["query", m, h][:].rearrange("p j u r -> p j r u"),
+            )
+
+
+        def quantize_keys(c, g):
+            if g == 0:
+                key_codes = code_pool.tile([P, G, CHUNK], U32, name="key_codes", align_bytes=64)
+                key_scales = code_pool.tile([P, G, CHUNK], U8, name="key_scales", align_bytes=64)
+                codes[c] = (key_codes, key_scales)
+            key_codes, key_scales = codes[c]
+            nc.vector.quantize_mx(
+                out=key_codes[:, g, :].bitcast(FP8X4),
+                scales=key_scales[:, g, :],
+                in_=turned[c][:, g].rearrange("p n t -> p (n t)"),
+            )
+
+        def quantize_query(m):
+            nc.vector.quantize_mx(
+                out=q_codes[:, m].rearrange("p g r -> p (g r)").bitcast(FP8X4),
+                scales=q_scales[:, m].rearrange("p g r -> p (g r)"),
+                in_=turned["query"][:, m].rearrange("p n t -> p (n t)"),
+            )
+
+
+        def multiply(c, m):
+            key_codes, key_scales = codes[c]
+            sums[c, m] = sum_psum.tile([P, CHUNK], F32, name="acc")
+            for g in range(G):
+                nc.tensor.matmul_mx(
+                    out=sums[c, m][:],
+                    lhsT=q_codes[:, m, g, :].bitcast(FP8X4),
+                    lhsT_scale=q_scales[:, m, g, :],
+                    rhs=key_codes[:, g, :].bitcast(FP8X4),
+                    rhs_scale=key_scales[:, g, :],
+                    start=(g == 0),
+                    stop=(g == G - 1),
+                )
+
+        def finish(c, m):
+            cols = slice(CHUNK * c, CHUNK * (c + 1))
+            result = result_pool.tile([P, CHUNK], F32, name="scores")
+            nc.vector.scalar_tensor_tensor(
+                out=result[:].rearrange("p (r i) -> p r i", i=NT),
+                in0=stale[:, cols].rearrange("p (r i) -> p r i", i=NT),
+                scalar=neg_rate[:, m : m + 1],
+                in1=sums[c, m][:].rearrange("p (i r) -> p r i", i=NT),
+                op0=MULT,
+                op1=ADD,
+            )
+            nc.sync.dma_start(out=out_view[:, m, cols], in_=result[:])
+
+        def warm_up(n):
+            for i in range(n):
+                nc.tensor.matmul(idle_bank[:], lhsT=zeros[:, :P], rhs=zeros[:], start=True, stop=True)
+
+        with tc.manual_schedule():
+            nc.scalar.dma_start(out=scale_first[:], in_=scale_view[:, 0, :])
+            nc.scalar.dma_start(out=age_sb[:], in_=age.rearrange("(p i) -> p i", p=P))
+            nc.scalar.dma_start(out=scale_rest[:], in_=scale_view[:, 1:, :])
+            nc.scalar.dma_start(out=rate_sb[:], in_=rate.rearrange("(p m) -> p m", m=M))
+            load_keys(0, parts=NT)
+            load_keys(1, parts=2)
+            for m in range(M):
+                nc.sync.dma_start(out=query_sb[:, m, :], in_=query_view[:, m, :])
+
+            nc.vector.memset(zeros[:], 0.0)
+            make_identity(nc, ident[:])
+            nc.scalar.activation(out=stale_sb[:], in_=age_sb[:], func=LN, bias=1.0)
+            nc.gpsimd.tensor_scalar(out=neg_rate[:], in0=rate_sb[:], scalar1=-1.0, scalar2=None, op0=MULT)
+            nc.sync.dma_start(out=park.rearrange("o (p i) -> p (o i)", p=P), in_=stale_sb[:])
+            load_keys(2, parts=2)
+            for c in range(3, RAW_BUFS):
+                load_stale(c - 3)
+                load_keys(c, parts=2)
+            load_stale(RAW_BUFS - 3)
+
+            for c in range(2):
+                widen_scalar(c)
+                for i in range(1, NT):
+                    widen_vector(c, i)
+            idle_bank = sum_psum.tile([P, CHUNK], F32, name="acc")
+            warm_up(WARM_UP_HEAD)
+            for b in range(2 * G):
+                turn_keys(0, b)
+                warm_up(1)
+                empty_keys(0, b)
+            for m in range(M):
+                for h in range(2):
+                    turn_query(m, h)
+                    warm_up(1)
+                    empty_query(m, h)
+            widen_scalar(2)
+            for g in range(G):
+                quantize_keys(0, g)
+            widen_vector(2, 1)
+            quantize_query(0)
+            quantize_query(1)
+            widen_vector(2, 2)
+            quantize_query(2)
+            quantize_query(3)
+            widen_vector(2, 3)
+
+            for c in range(NC):
+                turning, widening, loading = c + 1 < NC, c + 3 < NC, c + RAW_BUFS < NC
+                if c + 3 < NC:
+                    load_stale(c + 3)
+                if loading:
+                    load_keys(c + RAW_BUFS, parts=2)
+                for half in range(2):
+                    if turning:
+                        for b in range(4 * half, 4 * half + 4):
+                            turn_keys(c + 1, b)
+                            empty_keys(c + 1, b)
+                    if turning and half == 1:
+                        quantize_keys(c + 1, 2)
+                    multiply(c, 2 * half)
+                    multiply(c, 2 * half + 1)
+                    finish(c, 2 * half)
+                    if turning and half == 1:
+                        quantize_keys(c + 1, 3)
+                    finish(c, 2 * half + 1)
+                    if turning and half == 0:
+                        quantize_keys(c + 1, 0)
+                        quantize_keys(c + 1, 1)
+                if widening:
+                    widen_scalar(c + 3)
+                    for i in range(1, NT):
+                        widen_vector(c + 3, i)

@@ -21,254 +21,309 @@ P = 128
 PASS = 512
 G = K // PASS
 PAIRS = PASS // 2
-CHUNK = 512
-NT = CHUNK // P
-NC = T // CHUNK
 M = Q // P
 
-SCALAR_WIDTHS = (K, PASS)
-
-RAW_BUFS = 5
-WIDE_BUFS = 4
-TURN_BANKS = 5
-SUM_BANKS = 3
-WARM_UP_HEAD = 14
+NT = 2
+UNIT = NT * P
+NU = T // UNIT
+CAST = ((0, 0), (0, 0), (0, 0), (4, 2), (4, 2), (4, 2), (4, 2), (4, 2), (4, 2), (4, 2), (4, 2), (4, 2), (4, 2), (4, 2), (4, 2), (4, 2))
+TURN_BANKS = 4
+SUM_BANKS = 8 - TURN_BANKS
 
 
 def tile_aged_key_retrieval_d3_kernel(tc, query, keys_bytes, keys_scale, age, rate, out):
     nc = tc.nc
     with ExitStack() as ctx:
         const = ctx.enter_context(tc.tile_pool(name="const", bufs=1))
-        raw_pool = ctx.enter_context(tc.tile_pool(name="raw", bufs=RAW_BUFS))
-        wide_pool = ctx.enter_context(tc.tile_pool(name="wide", bufs=WIDE_BUFS))
-        turned_pool = ctx.enter_context(tc.tile_pool(name="turned", bufs=2))
-        code_pool = ctx.enter_context(tc.tile_pool(name="code", bufs=2))
-        result_pool = ctx.enter_context(tc.tile_pool(name="result", bufs=6))
+        raw_pool = ctx.enter_context(tc.tile_pool(name="raw", bufs=8))
+        cast_pool = ctx.enter_context(tc.tile_pool(name="cast", bufs=6))
+        split_pool = ctx.enter_context(tc.tile_pool(name="split", bufs=8))
+        turned_pool = ctx.enter_context(tc.tile_pool(name="turned", bufs=6))
+        code_pool = ctx.enter_context(tc.tile_pool(name="code", bufs=6))
+        result_pool = ctx.enter_context(tc.tile_pool(name="result", bufs=10))
         turn_psum = ctx.enter_context(tc.psum_pool(name="turn", bufs=TURN_BANKS))
         sum_psum = ctx.enter_context(tc.psum_pool(name="sum", bufs=SUM_BANKS))
 
         ident = const.tile([P, P], F32, name="ident")
-        zeros = const.tile([P, CHUNK], BF16, name="zeros")
         scale_first = const.tile([P, NT], F32, name="scale_first")
-        scale_rest = const.tile([P, NC - 1, NT], F32, name="scale_rest")
+        scale_rest = const.tile([P, NU - 1, NT], F32, name="scale_rest")
         age_sb = const.tile([P, T // P], BF16, name="age_sb")
         stale_sb = const.tile([P, T // P], F32, name="stale_sb")
-        stale = const.tile([P, T], F32, name="stale")
         rate_sb = const.tile([P, M], BF16, name="rate_sb")
         neg_rate = const.tile([P, M], F32, name="neg_rate")
-        query_sb = const.tile([P, M, K], BF16, name="query_sb")
-        q_codes = const.tile([P, M, G, P], U32, name="q_codes", align_bytes=64)
-        q_scales = const.tile([P, M, G, P], U8, name="q_scales", align_bytes=64)
+        query_sb = [const.tile([P, K], BF16, name="query_%d" % m) for m in range(M)]
+        q_codes = [const.tile([P, G * P], U32, name="q_codes_%d" % m, align_bytes=64) for m in range(M)]
+        q_scales = [const.tile([P, G * P], U8, name="q_scales_%d" % m, align_bytes=64) for m in range(M)]
+        stale = [const.tile([P, 2 * UNIT], F32, name="stale_%d" % c) for c in range(NU // 2)]
 
-        key_view = keys_bytes.rearrange("(c p i) k -> c p i k", p=P, i=NT)
-        scale_view = keys_scale.rearrange("(c p i) o -> p c (i o)", p=P, i=NT)
+        key_view = keys_bytes.rearrange("(v p j) k -> v p j k", p=P, j=NT)
+        scale_view = keys_scale.rearrange("(v p j) o -> p v (j o)", p=P, j=NT)
         query_view = query.rearrange("(p m) k -> p m k", m=M)
         out_view = out.rearrange("(p m) n -> p m n", m=M)
         park = out[Q - 1 : Q, :]
 
-        raw, natural, split, turned, codes, banks, sums = {}, {}, {}, {}, {}, {}, {}
+        raw, cast, split, turned, codes, banks, sums, results = {}, {}, {}, {}, {}, {}, {}, {}
 
-        def load_keys(c, parts):
-            raw[c] = raw_pool.tile([P, NT, K], U8, name="raw_keys")
-            n = NT // parts
-            for i in range(0, NT, n):
-                nc.sync.dma_start(out=raw[c][:, i : i + n, :], in_=key_view[c][:, i : i + n, :])
+        def load_keys(v, j=0, n=NT):
+            rows = raw_pool.tile([P, n, K], U8, name="raw_keys")
+            nc.sync.dma_start(out=rows[:], in_=key_view[v][:, j : j + n, :])
+            for i in range(n):
+                raw[v, j + i] = rows[:, i, :]
+
+        def load_query(m):
+            nc.sync.dma_start(out=query_sb[m][:], in_=query_view[:, m, :])
 
         def load_stale(c):
-            cols = slice(CHUNK * c, CHUNK * (c + 1))
-            nc.sync.dma_start(out=stale[:, cols], in_=park[0, cols].partition_broadcast(P))
+            nc.sync.dma_start(out=stale[c][:], in_=park[0, 2 * UNIT * c : 2 * UNIT * (c + 1)].partition_broadcast(P))
 
-        def scale_col(c, i):
-            return scale_first[:, i : i + 1] if c == 0 else scale_rest[:, c - 1, i : i + 1]
+        def scale_col(v, j):
+            return scale_first[:, j : j + 1] if v == 0 else scale_rest[:, v - 1, j : j + 1]
 
+        def halves(v, j, g0, g1):
+            if (v, j) not in split:
+                split[v, j] = split_pool.tile([P, 2, K // 4, 2], BF16, name="split_rows")
+            return split[v, j][:, :, P * g0 : P * g1, :]
 
-        def widen_scalar(c):
-            natural[c] = wide_pool.tile([P, sum(SCALAR_WIDTHS)], BF16, name="natural")
-            for i, width in enumerate(SCALAR_WIDTHS):
-                nc.scalar.activation(
-                    out=natural[c][:, K * i : K * i + width],
-                    in_=raw[c][:, i, :width].bitcast(FP8),
-                    func=COPY,
-                    scale=scale_col(c, i),
+        def cast_tile(v, j):
+            g = CAST[v][j]
+            if g > 0:
+                cast[v, j] = cast_pool.tile([P, K], BF16, name="cast_rows")
+                nc.scalar.copy(out=cast[v, j][:, : PASS * g], in_=raw[v, j][:, : PASS * g].bitcast(FP8))
+
+        def widen(v, j, g0=0, g1=G):
+            g = CAST[v][j]
+            if g > g0:
+                hi = min(g, g1)
+                nc.vector.tensor_scalar(
+                    out=halves(v, j, g0, hi),
+                    in0=cast[v, j][:, PASS * g0 : PASS * hi].rearrange("p (w u e) -> p u w e", u=2, e=2),
+                    scalar1=scale_col(v, j),
+                    scalar2=None,
+                    op0=MULT,
+                )
+            if g < g1:
+                lo = max(g, g0)
+                nc.vector.tensor_scalar(
+                    out=halves(v, j, lo, g1).rearrange("p u w e -> p w u e"),
+                    in0=raw[v, j][:, PASS * lo : PASS * g1].bitcast(FP8).rearrange("p (w u e) -> p w u e", u=2, e=2),
+                    scalar1=scale_col(v, j),
+                    scalar2=None,
+                    op0=MULT,
                 )
 
-        def widen_vector(c, i):
-            if i == 1:
-                split[c] = wide_pool.tile([P, NT - 1, 2, K // 4, 2], BF16, name="split")
-            k0 = SCALAR_WIDTHS[i] if i < len(SCALAR_WIDTHS) else 0
-            nc.vector.tensor_scalar(
-                out=split[c][:, i - 1, :, k0 // 4 :, :].rearrange("p u w e -> p w u e"),
-                in0=raw[c][:, i, k0:].bitcast(FP8).rearrange("p (w u e) -> p w u e", u=2, e=2),
-                scalar1=scale_col(c, i),
-                scalar2=None,
-                op0=MULT,
-            )
-
-
-        def natural_pairs(row, g, u):
-            return row.bitcast(F32)[:, PAIRS * g + u : PAIRS * (g + 1) : 2]
-
-        def key_pairs(c, i, g, u):
-            if i < len(SCALAR_WIDTHS) and PASS * g < SCALAR_WIDTHS[i]:
-                return natural_pairs(natural[c][:, K * i : K * i + SCALAR_WIDTHS[i]], g, u)
-            half = split[c][:, i - 1, u].rearrange("p w e -> p (w e)").bitcast(F32)
-            return half[:, P * g : P * (g + 1)]
-
-        def turn_keys(c, b):
-            g, h = divmod(b, 2)
-            bank = turn_psum.tile([P, 2, 2, P], F32, name="bank")
-            banks[c, b] = bank
-            for j in range(2):
+        def turn_keys(v, g):
+            bank = turn_psum.tile([P, 2, NT, P], F32, name="bank")
+            banks[v, g] = bank
+            for j in range(NT):
                 for u in range(2):
-                    nc.tensor.transpose(bank[:, u, j, :], key_pairs(c, 2 * h + j, g, u), ident[:])
-
-        def empty_keys(c, b):
-            g, h = divmod(b, 2)
-            if b == 0:
-                turned[c] = turned_pool.tile([P, G, CHUNK, 4], BF16, name="turned_rows", align_bytes=64)
-            nc.scalar.copy(
-                out=turned[c][:, g, 2 * P * h : 2 * P * (h + 1), :].bitcast(F32),
-                in_=banks[c, b][:].rearrange("p u j r -> p (j r) u"),
-            )
+                    half = split[v, j][:, u].rearrange("p w e -> p (w e)").bitcast(F32)
+                    nc.tensor.transpose(bank[:, u, j, :], half[:, P * g : P * (g + 1)], ident[:])
 
         def turn_query(m, h):
             bank = turn_psum.tile([P, 2, 2, P], F32, name="bank")
             banks["query", m, h] = bank
+            words = query_sb[m][:].bitcast(F32)
             for j in range(2):
+                g = 2 * h + j
                 for u in range(2):
-                    nc.tensor.transpose(bank[:, j, u, :], natural_pairs(query_sb[:, m, :], 2 * h + j, u), ident[:])
+                    nc.tensor.transpose(bank[:, u, j, :], words[:, PAIRS * g + u : PAIRS * (g + 1) : 2], ident[:])
 
-        def empty_query(m, h):
-            if m == 0 and h == 0:
-                turned["query"] = turned_pool.tile([P, M, G * P, 4], BF16, name="turned_rows", align_bytes=64)
-            dst = turned["query"][:, m, 2 * P * h : 2 * P * (h + 1), :].bitcast(F32)
-            nc.scalar.copy(
-                out=dst.rearrange("p (j r) u -> p j r u", j=2),
-                in_=banks["query", m, h][:].rearrange("p j u r -> p j r u"),
-            )
+        def empty(bank, key, half, engine):
+            if half == 0:
+                turned[key] = turned_pool.tile([P, PASS, 4], BF16, name="turned_rows", align_bytes=64)
+            dst = turned[key][:, 2 * P * half : 2 * P * (half + 1), :].bitcast(F32)
+            src = bank[:].rearrange("p u j r -> p (j r) u")
+            if engine == "scalar":
+                nc.scalar.copy(out=dst, in_=src)
+            else:
+                nc.vector.tensor_copy(out=dst, in_=src)
 
+        def empty_keys(v, g, engine="scalar"):
+            empty(banks[v, g], (v, g // 2), g % 2, engine)
 
-        def quantize_keys(c, g):
-            if g == 0:
-                key_codes = code_pool.tile([P, G, CHUNK], U32, name="key_codes", align_bytes=64)
-                key_scales = code_pool.tile([P, G, CHUNK], U8, name="key_scales", align_bytes=64)
-                codes[c] = (key_codes, key_scales)
-            key_codes, key_scales = codes[c]
+        def empty_query(m, h, engine="scalar"):
+            empty(banks["query", m, h], ("query", m), h, engine)
+
+        def quantize_keys(v, h):
+            key_codes = code_pool.tile([P, PASS], U32, name="key_codes", align_bytes=64)
+            key_scales = code_pool.tile([P, PASS], U8, name="key_scales", align_bytes=64)
+            codes[v, h] = (key_codes, key_scales)
             nc.vector.quantize_mx(
-                out=key_codes[:, g, :].bitcast(FP8X4),
-                scales=key_scales[:, g, :],
-                in_=turned[c][:, g].rearrange("p n t -> p (n t)"),
+                out=key_codes[:].bitcast(FP8X4),
+                scales=key_scales[:],
+                in_=turned[v, h][:].rearrange("p n t -> p (n t)"),
             )
 
         def quantize_query(m):
             nc.vector.quantize_mx(
-                out=q_codes[:, m].rearrange("p g r -> p (g r)").bitcast(FP8X4),
-                scales=q_scales[:, m].rearrange("p g r -> p (g r)"),
-                in_=turned["query"][:, m].rearrange("p n t -> p (n t)"),
+                out=q_codes[m][:].bitcast(FP8X4),
+                scales=q_scales[m][:],
+                in_=turned["query", m][:].rearrange("p n t -> p (n t)"),
             )
 
-
-        def multiply(c, m):
-            key_codes, key_scales = codes[c]
-            sums[c, m] = sum_psum.tile([P, CHUNK], F32, name="acc")
+        def multiply(v, m):
+            sums[v, m] = sum_psum.tile([P, UNIT], F32, name="acc")
             for g in range(G):
+                key_codes, key_scales = codes[v, g // 2]
+                cols = slice(UNIT * (g % 2), UNIT * (g % 2 + 1))
                 nc.tensor.matmul_mx(
-                    out=sums[c, m][:],
-                    lhsT=q_codes[:, m, g, :].bitcast(FP8X4),
-                    lhsT_scale=q_scales[:, m, g, :],
-                    rhs=key_codes[:, g, :].bitcast(FP8X4),
-                    rhs_scale=key_scales[:, g, :],
+                    out=sums[v, m][:],
+                    lhsT=q_codes[m][:, P * g : P * (g + 1)].bitcast(FP8X4),
+                    lhsT_scale=q_scales[m][:, P * g : P * (g + 1)],
+                    rhs=key_codes[:, cols].bitcast(FP8X4),
+                    rhs_scale=key_scales[:, cols],
                     start=(g == 0),
                     stop=(g == G - 1),
                 )
 
-        def finish(c, m):
-            cols = slice(CHUNK * c, CHUNK * (c + 1))
-            result = result_pool.tile([P, CHUNK], F32, name="scores")
+        def finish(v, m):
+            c, half = divmod(v, 2)
+            if half == 0:
+                results[c, m] = result_pool.tile([P, 2 * UNIT], F32, name="scores")
+            cols = slice(UNIT * half, UNIT * (half + 1))
             nc.vector.scalar_tensor_tensor(
-                out=result[:].rearrange("p (r i) -> p r i", i=NT),
-                in0=stale[:, cols].rearrange("p (r i) -> p r i", i=NT),
+                out=results[c, m][:, cols].rearrange("p (r j) -> p r j", j=NT),
+                in0=stale[c][:, cols].rearrange("p (r j) -> p r j", j=NT),
                 scalar=neg_rate[:, m : m + 1],
-                in1=sums[c, m][:].rearrange("p (i r) -> p r i", i=NT),
+                in1=sums[v, m][:].rearrange("p (j r) -> p r j", j=NT),
                 op0=MULT,
                 op1=ADD,
             )
-            nc.sync.dma_start(out=out_view[:, m, cols], in_=result[:])
+            if c == NU // 2 - 1:
+                nc.sync.dma_start(out=out_view[:, m, UNIT * v : UNIT * (v + 1)], in_=results[c, m][:, cols])
+            elif half == 1:
+                nc.sync.dma_start(out=out_view[:, m, 2 * UNIT * c : 2 * UNIT * (c + 1)], in_=results[c, m][:])
 
-        def warm_up(n):
-            for i in range(n):
-                nc.tensor.matmul(idle_bank[:], lhsT=zeros[:, :P], rhs=zeros[:], start=True, stop=True)
 
         with tc.manual_schedule():
-            nc.scalar.dma_start(out=scale_first[:], in_=scale_view[:, 0, :])
             nc.scalar.dma_start(out=age_sb[:], in_=age.rearrange("(p i) -> p i", p=P))
-            nc.scalar.dma_start(out=scale_rest[:], in_=scale_view[:, 1:, :])
-            nc.scalar.dma_start(out=rate_sb[:], in_=rate.rearrange("(p m) -> p m", m=M))
-            load_keys(0, parts=NT)
-            load_keys(1, parts=2)
-            for m in range(M):
-                nc.sync.dma_start(out=query_sb[:, m, :], in_=query_view[:, m, :])
-
-            nc.vector.memset(zeros[:], 0.0)
+            nc.scalar.dma_start(out=scale_first[:], in_=scale_view[:, 0, :])
+            load_keys(0, 0, 1)
+            load_keys(0, 1, 1)
+            load_query(0)
+            nc.sync.dma_start(out=scale_rest[:], in_=scale_view[:, 1:, :])
+            load_keys(1)
+            load_query(1)
+            load_keys(2)
+            load_query(2)
+            load_query(3)
+            load_keys(3)
             make_identity(nc, ident[:])
             nc.scalar.activation(out=stale_sb[:], in_=age_sb[:], func=LN, bias=1.0)
-            nc.gpsimd.tensor_scalar(out=neg_rate[:], in0=rate_sb[:], scalar1=-1.0, scalar2=None, op0=MULT)
             nc.sync.dma_start(out=park.rearrange("o (p i) -> p (o i)", p=P), in_=stale_sb[:])
-            load_keys(2, parts=2)
-            for c in range(3, RAW_BUFS):
-                load_stale(c - 3)
-                load_keys(c, parts=2)
-            load_stale(RAW_BUFS - 3)
-
-            for c in range(2):
-                widen_scalar(c)
-                for i in range(1, NT):
-                    widen_vector(c, i)
-            idle_bank = sum_psum.tile([P, CHUNK], F32, name="acc")
-            warm_up(WARM_UP_HEAD)
-            for b in range(2 * G):
-                turn_keys(0, b)
-                warm_up(1)
-                empty_keys(0, b)
-            for m in range(M):
-                for h in range(2):
-                    turn_query(m, h)
-                    warm_up(1)
-                    empty_query(m, h)
-            widen_scalar(2)
-            for g in range(G):
-                quantize_keys(0, g)
-            widen_vector(2, 1)
+            nc.sync.dma_start(out=rate_sb[:], in_=rate.rearrange("(p m) -> p m", m=M))
+            load_keys(4)
+            load_stale(0)
+            load_keys(5)
+            load_stale(1)
+            load_keys(6)
+            load_stale(2)
+            widen(0, 0, 0, 2)
+            widen(0, 1, 0, 2)
+            widen(0, 0, 2, 4)
+            widen(0, 1, 2, 4)
+            turn_keys(0, 0)
+            empty_keys(0, 0)
+            turn_keys(0, 1)
+            empty_keys(0, 1)
+            turn_keys(0, 2)
+            empty_keys(0, 2)
+            turn_keys(0, 3)
+            empty_keys(0, 3)
+            turn_query(0, 0)
+            empty_query(0, 0)
+            turn_query(0, 1)
+            empty_query(0, 1)
+            widen(1, 0)
+            widen(1, 1)
+            turn_query(1, 0)
+            empty_query(1, 0)
+            turn_query(1, 1)
+            empty_query(1, 1)
+            quantize_keys(0, 0)
+            quantize_keys(0, 1)
             quantize_query(0)
+            turn_keys(1, 0)
+            empty_keys(1, 0)
+            turn_keys(1, 1)
+            empty_keys(1, 1)
+            turn_keys(1, 2)
+            empty_keys(1, 2)
+            turn_keys(1, 3)
+            empty_keys(1, 3)
             quantize_query(1)
-            widen_vector(2, 2)
+            multiply(0, 0)
+            multiply(0, 1)
+            widen(2, 0)
+            widen(2, 1)
+            turn_query(2, 0)
+            empty_query(2, 0)
+            turn_query(2, 1)
+            empty_query(2, 1)
+            turn_query(3, 0)
+            empty_query(3, 0)
+            turn_query(3, 1)
+            empty_query(3, 1)
+            quantize_keys(1, 0)
+            quantize_keys(1, 1)
+            nc.scalar.activation(out=neg_rate[:], in_=rate_sb[:], func=COPY, scale=-1.0)
+            cast_tile(3, 0)
+            cast_tile(3, 1)
+            multiply(1, 0)
+            multiply(1, 1)
+            finish(0, 0)
+            finish(0, 1)
             quantize_query(2)
             quantize_query(3)
-            widen_vector(2, 3)
+            turn_keys(2, 0)
+            empty_keys(2, 0)
+            turn_keys(2, 1)
+            empty_keys(2, 1)
+            turn_keys(2, 2)
+            empty_keys(2, 2)
+            turn_keys(2, 3)
+            empty_keys(2, 3)
+            finish(1, 0)
+            finish(1, 1)
+            multiply(0, 2)
+            multiply(0, 3)
+            cast_tile(4, 0)
+            cast_tile(4, 1)
+            widen(3, 0)
+            widen(3, 1)
+            quantize_keys(2, 0)
+            finish(0, 2)
+            finish(0, 3)
+            multiply(1, 2)
+            multiply(1, 3)
+            quantize_keys(2, 1)
+            finish(1, 2)
 
-            for c in range(NC):
-                turning, widening, loading = c + 1 < NC, c + 3 < NC, c + RAW_BUFS < NC
-                if c + 3 < NC:
-                    load_stale(c + 3)
-                if loading:
-                    load_keys(c + RAW_BUFS, parts=2)
-                for half in range(2):
-                    if turning:
-                        for b in range(4 * half, 4 * half + 4):
-                            turn_keys(c + 1, b)
-                            empty_keys(c + 1, b)
-                    if turning and half == 1:
-                        quantize_keys(c + 1, 2)
-                    multiply(c, 2 * half)
-                    multiply(c, 2 * half + 1)
-                    finish(c, 2 * half)
-                    if turning and half == 1:
-                        quantize_keys(c + 1, 3)
-                    finish(c, 2 * half + 1)
-                    if turning and half == 0:
-                        quantize_keys(c + 1, 0)
-                        quantize_keys(c + 1, 1)
-                if widening:
-                    widen_scalar(c + 3)
-                    for i in range(1, NT):
-                        widen_vector(c + 3, i)
+            for v in range(2, NU):
+                if v + 5 < NU:
+                    load_keys(v + 5)
+                if v % 2 == 0 and v // 2 + 2 < NU // 2:
+                    load_stale(v // 2 + 2)
+                if v + 1 < NU:
+                    for g in range(G):
+                        turn_keys(v + 1, g)
+                        empty_keys(v + 1, g)
+                if v + 3 < NU:
+                    cast_tile(v + 3, 0)
+                    cast_tile(v + 3, 1)
+                finish(v - 1, 3)
+                multiply(v, 0)
+                multiply(v, 1)
+                multiply(v, 2)
+                if v + 2 < NU:
+                    widen(v + 2, 0)
+                    widen(v + 2, 1)
+                if v + 1 < NU:
+                    quantize_keys(v + 1, 0)
+                finish(v, 0)
+                multiply(v, 3)
+                finish(v, 1)
+                if v + 1 < NU:
+                    quantize_keys(v + 1, 1)
+                finish(v, 2)
+            finish(NU - 1, 3)

@@ -23,6 +23,8 @@ G = K // PASS
 PAIRS = PASS // 2
 M = Q // P
 
+BLOCK = 32
+HALF = BLOCK // 2
 NT = 2
 UNIT = NT * P
 NU = T // UNIT
@@ -81,8 +83,8 @@ def tile_aged_key_retrieval_d3_kernel(tc, query, keys_bytes, keys_scale, age, ra
 
         def halves(v, j, g0, g1):
             if (v, j) not in split:
-                split[v, j] = split_pool.tile([P, 2, K // 4, 2], BF16, name="split_rows")
-            return split[v, j][:, :, P * g0 : P * g1, :]
+                split[v, j] = split_pool.tile([P, 2, K // BLOCK, HALF], BF16, name="split_rows")
+            return split[v, j][:, :, PASS // BLOCK * g0 : PASS // BLOCK * g1, :]
 
         def cast_tile(v, j):
             g = CAST[v][j]
@@ -96,7 +98,7 @@ def tile_aged_key_retrieval_d3_kernel(tc, query, keys_bytes, keys_scale, age, ra
                 hi = min(g, g1)
                 nc.vector.tensor_scalar(
                     out=halves(v, j, g0, hi),
-                    in0=cast[v, j][:, PASS * g0 : PASS * hi].rearrange("p (w u e) -> p u w e", u=2, e=2),
+                    in0=cast[v, j][:, PASS * g0 : PASS * hi].rearrange("p (w u e) -> p u w e", u=2, e=HALF),
                     scalar1=scale_col(v, j),
                     scalar2=None,
                     op0=MULT,
@@ -105,11 +107,17 @@ def tile_aged_key_retrieval_d3_kernel(tc, query, keys_bytes, keys_scale, age, ra
                 lo = max(g, g0)
                 nc.vector.tensor_scalar(
                     out=halves(v, j, lo, g1).rearrange("p u w e -> p w u e"),
-                    in0=raw[v, j][:, PASS * lo : PASS * g1].bitcast(FP8).rearrange("p (w u e) -> p w u e", u=2, e=2),
+                    in0=raw[v, j][:, PASS * lo : PASS * g1].bitcast(FP8).rearrange("p (w u e) -> p w u e", u=2, e=HALF),
                     scalar1=scale_col(v, j),
                     scalar2=None,
                     op0=MULT,
                 )
+
+        def part_query(m):
+            nc.vector.tensor_copy(
+                out=halves("query", m, 0, G),
+                in_=query_sb[m][:].rearrange("p (w u e) -> p u w e", u=2, e=HALF),
+            )
 
         def turn_keys(v, g):
             bank = turn_psum.tile([P, 2, NT, P], F32, name="bank")
@@ -122,11 +130,11 @@ def tile_aged_key_retrieval_d3_kernel(tc, query, keys_bytes, keys_scale, age, ra
         def turn_query(m, h):
             bank = turn_psum.tile([P, 2, 2, P], F32, name="bank")
             banks["query", m, h] = bank
-            words = query_sb[m][:].bitcast(F32)
             for j in range(2):
                 g = 2 * h + j
                 for u in range(2):
-                    nc.tensor.transpose(bank[:, u, j, :], words[:, PAIRS * g + u : PAIRS * (g + 1) : 2], ident[:])
+                    half = split["query", m][:, u].rearrange("p w e -> p (w e)").bitcast(F32)
+                    nc.tensor.transpose(bank[:, u, j, :], half[:, P * g : P * (g + 1)], ident[:])
 
         def empty(bank, key, half, engine):
             if half == 0:
@@ -222,6 +230,7 @@ def tile_aged_key_retrieval_d3_kernel(tc, query, keys_bytes, keys_scale, age, ra
             widen(0, 1, 0, 2)
             widen(0, 0, 2, 4)
             widen(0, 1, 2, 4)
+            part_query(0)
             turn_keys(0, 0)
             empty_keys(0, 0)
             turn_keys(0, 1)
@@ -235,6 +244,7 @@ def tile_aged_key_retrieval_d3_kernel(tc, query, keys_bytes, keys_scale, age, ra
             turn_query(0, 1)
             empty_query(0, 1)
             widen(1, 0)
+            part_query(1)
             widen(1, 1)
             turn_query(1, 0)
             empty_query(1, 0)
@@ -251,7 +261,9 @@ def tile_aged_key_retrieval_d3_kernel(tc, query, keys_bytes, keys_scale, age, ra
             empty_keys(1, 2)
             turn_keys(1, 3)
             empty_keys(1, 3)
+            part_query(2)
             quantize_query(1)
+            part_query(3)
             multiply(0, 0)
             multiply(0, 1)
             widen(2, 0)

@@ -28,7 +28,7 @@ HALF = BLOCK // 2
 NT = 2
 UNIT = NT * P
 NU = T // UNIT
-CAST = ((0, 0), (0, 0), (0, 0), (4, 2), (4, 2), (4, 2), (4, 2), (4, 2), (4, 2), (4, 2), (4, 2), (4, 2), (4, 2), (4, 2), (4, 2), (4, 2))
+CAST = ((0, 0), (0, 0), (4, 0), (4, 0), (4, 4), (4, 0), (4, 4), (4, 0), (4, 4), (4, 0), (4, 4), (4, 0), (4, 4), (4, 0), (4, 4), (4, 0))
 TURN_BANKS = 4
 SUM_BANKS = 8 - TURN_BANKS
 
@@ -40,15 +40,15 @@ def tile_aged_key_retrieval_d3_kernel(tc, query, keys_bytes, keys_scale, age, ra
         raw_pool = ctx.enter_context(tc.tile_pool(name="raw", bufs=8))
         cast_pool = ctx.enter_context(tc.tile_pool(name="cast", bufs=6))
         split_pool = ctx.enter_context(tc.tile_pool(name="split", bufs=8))
-        turned_pool = ctx.enter_context(tc.tile_pool(name="turned", bufs=6))
-        code_pool = ctx.enter_context(tc.tile_pool(name="code", bufs=6))
+        turned_pool = ctx.enter_context(tc.tile_pool(name="turned", bufs=4))
+        code_pool = ctx.enter_context(tc.tile_pool(name="code", bufs=4))
         result_pool = ctx.enter_context(tc.tile_pool(name="result", bufs=10))
         turn_psum = ctx.enter_context(tc.psum_pool(name="turn", bufs=TURN_BANKS))
         sum_psum = ctx.enter_context(tc.psum_pool(name="sum", bufs=SUM_BANKS))
 
         ident = const.tile([P, P], F32, name="ident")
-        scale_first = const.tile([P, NT], F32, name="scale_first")
-        scale_rest = const.tile([P, NU - 1, NT], F32, name="scale_rest")
+        scale_rows = const.tile([P, P], F32, name="scale_rows")
+        scale_sb = const.tile([P, T // P], F32, name="scale_sb")
         age_sb = const.tile([P, T // P], BF16, name="age_sb")
         stale_sb = const.tile([P, T // P], F32, name="stale_sb")
         rate_sb = const.tile([P, M], BF16, name="rate_sb")
@@ -58,8 +58,7 @@ def tile_aged_key_retrieval_d3_kernel(tc, query, keys_bytes, keys_scale, age, ra
         q_scales = [const.tile([P, G * P], U8, name="q_scales_%d" % m, align_bytes=64) for m in range(M)]
         stale = [const.tile([P, 2 * UNIT], F32, name="stale_%d" % c) for c in range(NU // 2)]
 
-        key_view = keys_bytes.rearrange("(v p j) k -> v p j k", p=P, j=NT)
-        scale_view = keys_scale.rearrange("(v p j) o -> p v (j o)", p=P, j=NT)
+        key_view = keys_bytes.rearrange("(v j p) k -> v p j k", p=P, j=NT)
         query_view = query.rearrange("(p m) k -> p m k", m=M)
         out_view = out.rearrange("(p m) n -> p m n", m=M)
         park = out[Q - 1 : Q, :]
@@ -79,7 +78,17 @@ def tile_aged_key_retrieval_d3_kernel(tc, query, keys_bytes, keys_scale, age, ra
             nc.sync.dma_start(out=stale[c][:], in_=park[0, 2 * UNIT * c : 2 * UNIT * (c + 1)].partition_broadcast(P))
 
         def scale_col(v, j):
-            return scale_first[:, j : j + 1] if v == 0 else scale_rest[:, v - 1, j : j + 1]
+            return scale_sb[:, NT * v + j : NT * v + j + 1]
+
+        def load_scales():
+            nc.scalar.dma_start(out=scale_rows[: T // P, :], in_=keys_scale.rearrange("(i p) o -> i (p o)", p=P))
+            nc.vector.memset(scale_rows[32:64, :], 0.0)
+            nc.vector.memset(scale_rows[64:, :], 0.0)
+
+        def turn_scales():
+            bank = turn_psum.tile([P, 2, NT, P], F32, name="bank")
+            nc.tensor.transpose(bank[:, 0, 0, :], scale_rows[:], ident[:])
+            nc.vector.tensor_copy(out=scale_sb[:], in_=bank[:, 0, 0, : T // P])
 
         def halves(v, j, g0, g1):
             if (v, j) not in split:
@@ -136,9 +145,9 @@ def tile_aged_key_retrieval_d3_kernel(tc, query, keys_bytes, keys_scale, age, ra
                     half = split["query", m][:, u].rearrange("p w e -> p (w e)").bitcast(F32)
                     nc.tensor.transpose(bank[:, u, j, :], half[:, P * g : P * (g + 1)], ident[:])
 
-        def empty(bank, key, half, engine):
+        def empty(bank, key, half, engine, width):
             if half == 0:
-                turned[key] = turned_pool.tile([P, PASS, 4], BF16, name="turned_rows", align_bytes=64)
+                turned[key] = turned_pool.tile([P, width, 4], BF16, name="turned_rows", align_bytes=64)
             dst = turned[key][:, 2 * P * half : 2 * P * (half + 1), :].bitcast(F32)
             src = bank[:].rearrange("p u j r -> p (j r) u")
             if engine == "scalar":
@@ -147,19 +156,22 @@ def tile_aged_key_retrieval_d3_kernel(tc, query, keys_bytes, keys_scale, age, ra
                 nc.vector.tensor_copy(out=dst, in_=src)
 
         def empty_keys(v, g, engine="scalar"):
-            empty(banks[v, g], (v, g // 2), g % 2, engine)
+            empty(banks[v, g], v, g, engine, G * UNIT)
 
         def empty_query(m, h, engine="scalar"):
-            empty(banks["query", m, h], ("query", m), h, engine)
+            empty(banks["query", m, h], ("query", m), h, engine, G * P)
 
-        def quantize_keys(v, h):
-            key_codes = code_pool.tile([P, PASS], U32, name="key_codes", align_bytes=64)
-            key_scales = code_pool.tile([P, PASS], U8, name="key_scales", align_bytes=64)
-            codes[v, h] = (key_codes, key_scales)
+        def quantize_keys(v, g0=0, g1=G):
+            if g0 == 0:
+                key_codes = code_pool.tile([P, G * UNIT], U32, name="key_codes", align_bytes=64)
+                key_scales = code_pool.tile([P, G * UNIT], U8, name="key_scales", align_bytes=64)
+                codes[v] = (key_codes, key_scales)
+            key_codes, key_scales = codes[v]
+            cols = slice(UNIT * g0, UNIT * g1)
             nc.vector.quantize_mx(
-                out=key_codes[:].bitcast(FP8X4),
-                scales=key_scales[:],
-                in_=turned[v, h][:].rearrange("p n t -> p (n t)"),
+                out=key_codes[:, cols].bitcast(FP8X4),
+                scales=key_scales[:, cols],
+                in_=turned[v][:, cols, :].rearrange("p n t -> p (n t)"),
             )
 
         def quantize_query(m):
@@ -170,12 +182,14 @@ def tile_aged_key_retrieval_d3_kernel(tc, query, keys_bytes, keys_scale, age, ra
             )
 
         def multiply(v, m):
-            sums[v, m] = sum_psum.tile([P, UNIT], F32, name="acc")
+            c, half = divmod(v, 2)
+            if half == 0:
+                sums[c, m] = sum_psum.tile([P, 2 * UNIT], F32, name="acc")
             for g in range(G):
-                key_codes, key_scales = codes[v, g // 2]
-                cols = slice(UNIT * (g % 2), UNIT * (g % 2 + 1))
+                key_codes, key_scales = codes[v]
+                cols = slice(UNIT * g, UNIT * (g + 1))
                 nc.tensor.matmul_mx(
-                    out=sums[v, m][:],
+                    out=sums[c, m][:, UNIT * half : UNIT * (half + 1)],
                     lhsT=q_codes[m][:, P * g : P * (g + 1)].bitcast(FP8X4),
                     lhsT_scale=q_scales[m][:, P * g : P * (g + 1)],
                     rhs=key_codes[:, cols].bitcast(FP8X4),
@@ -184,32 +198,25 @@ def tile_aged_key_retrieval_d3_kernel(tc, query, keys_bytes, keys_scale, age, ra
                     stop=(g == G - 1),
                 )
 
-        def finish(v, m):
-            c, half = divmod(v, 2)
-            if half == 0:
-                results[c, m] = result_pool.tile([P, 2 * UNIT], F32, name="scores")
-            cols = slice(UNIT * half, UNIT * (half + 1))
+        def finish(c, m, lo=0, hi=2 * UNIT):
+            result = result_pool.tile([P, hi - lo], F32, name="scores")
             nc.vector.scalar_tensor_tensor(
-                out=results[c, m][:, cols].rearrange("p (r j) -> p r j", j=NT),
-                in0=stale[c][:, cols].rearrange("p (r j) -> p r j", j=NT),
+                out=result[:],
+                in0=stale[c][:, lo:hi],
                 scalar=neg_rate[:, m : m + 1],
-                in1=sums[v, m][:].rearrange("p (j r) -> p r j", j=NT),
+                in1=sums[c, m][:, lo:hi],
                 op0=MULT,
                 op1=ADD,
             )
-            if c == NU // 2 - 1:
-                nc.sync.dma_start(out=out_view[:, m, UNIT * v : UNIT * (v + 1)], in_=results[c, m][:, cols])
-            elif half == 1:
-                nc.sync.dma_start(out=out_view[:, m, 2 * UNIT * c : 2 * UNIT * (c + 1)], in_=results[c, m][:])
+            nc.sync.dma_start(out=out_view[:, m, 2 * UNIT * c + lo : 2 * UNIT * c + hi], in_=result[:])
 
 
         with tc.manual_schedule():
+            load_scales()
             nc.scalar.dma_start(out=age_sb[:], in_=age.rearrange("(p i) -> p i", p=P))
-            nc.scalar.dma_start(out=scale_first[:], in_=scale_view[:, 0, :])
             load_keys(0, 0, 1)
             load_keys(0, 1, 1)
             load_query(0)
-            nc.sync.dma_start(out=scale_rest[:], in_=scale_view[:, 1:, :])
             load_keys(1)
             load_query(1)
             load_keys(2)
@@ -217,6 +224,7 @@ def tile_aged_key_retrieval_d3_kernel(tc, query, keys_bytes, keys_scale, age, ra
             load_query(3)
             load_keys(3)
             make_identity(nc, ident[:])
+            turn_scales()
             nc.scalar.activation(out=stale_sb[:], in_=age_sb[:], func=LN, bias=1.0)
             nc.sync.dma_start(out=park.rearrange("o (p i) -> p (o i)", p=P), in_=stale_sb[:])
             nc.sync.dma_start(out=rate_sb[:], in_=rate.rearrange("(p m) -> p m", m=M))
@@ -250,8 +258,7 @@ def tile_aged_key_retrieval_d3_kernel(tc, query, keys_bytes, keys_scale, age, ra
             empty_query(1, 0)
             turn_query(1, 1)
             empty_query(1, 1)
-            quantize_keys(0, 0)
-            quantize_keys(0, 1)
+            quantize_keys(0)
             quantize_query(0)
             turn_keys(1, 0)
             empty_keys(1, 0)
@@ -266,8 +273,8 @@ def tile_aged_key_retrieval_d3_kernel(tc, query, keys_bytes, keys_scale, age, ra
             part_query(3)
             multiply(0, 0)
             multiply(0, 1)
-            widen(2, 0)
-            widen(2, 1)
+            cast_tile(2, 0)
+            cast_tile(2, 1)
             turn_query(2, 0)
             empty_query(2, 0)
             turn_query(2, 1)
@@ -276,15 +283,14 @@ def tile_aged_key_retrieval_d3_kernel(tc, query, keys_bytes, keys_scale, age, ra
             empty_query(3, 0)
             turn_query(3, 1)
             empty_query(3, 1)
-            quantize_keys(1, 0)
-            quantize_keys(1, 1)
+            quantize_keys(1)
+            widen(2, 0)
+            widen(2, 1)
             nc.scalar.activation(out=neg_rate[:], in_=rate_sb[:], func=COPY, scale=-1.0)
             cast_tile(3, 0)
             cast_tile(3, 1)
             multiply(1, 0)
             multiply(1, 1)
-            finish(0, 0)
-            finish(0, 1)
             quantize_query(2)
             quantize_query(3)
             turn_keys(2, 0)
@@ -295,27 +301,24 @@ def tile_aged_key_retrieval_d3_kernel(tc, query, keys_bytes, keys_scale, age, ra
             empty_keys(2, 2)
             turn_keys(2, 3)
             empty_keys(2, 3)
-            finish(1, 0)
-            finish(1, 1)
+            finish(0, 0)
+            finish(0, 1)
             multiply(0, 2)
             multiply(0, 3)
             cast_tile(4, 0)
             cast_tile(4, 1)
             widen(3, 0)
             widen(3, 1)
-            quantize_keys(2, 0)
-            finish(0, 2)
-            finish(0, 3)
             multiply(1, 2)
             multiply(1, 3)
-            quantize_keys(2, 1)
-            finish(1, 2)
+            quantize_keys(2)
 
             for v in range(2, NU):
+                c, half = divmod(v, 2)
                 if v + 5 < NU:
                     load_keys(v + 5)
-                if v % 2 == 0 and v // 2 + 2 < NU // 2:
-                    load_stale(v // 2 + 2)
+                if half == 0 and c + 2 < NU // 2:
+                    load_stale(c + 2)
                 if v + 1 < NU:
                     for g in range(G):
                         turn_keys(v + 1, g)
@@ -323,19 +326,21 @@ def tile_aged_key_retrieval_d3_kernel(tc, query, keys_bytes, keys_scale, age, ra
                 if v + 3 < NU:
                     cast_tile(v + 3, 0)
                     cast_tile(v + 3, 1)
-                finish(v - 1, 3)
-                multiply(v, 0)
-                multiply(v, 1)
-                multiply(v, 2)
+                if half == 0:
+                    finish(c - 1, 2)
+                    finish(c - 1, 3)
+                for m in range(M):
+                    multiply(v, m)
                 if v + 2 < NU:
                     widen(v + 2, 0)
                     widen(v + 2, 1)
                 if v + 1 < NU:
-                    quantize_keys(v + 1, 0)
-                finish(v, 0)
-                multiply(v, 3)
-                finish(v, 1)
+                    quantize_keys(v + 1, 0, 2)
+                if half == 1:
+                    finish(c, 0)
                 if v + 1 < NU:
-                    quantize_keys(v + 1, 1)
-                finish(v, 2)
-            finish(NU - 1, 3)
+                    quantize_keys(v + 1, 2, 4)
+                if half == 1:
+                    finish(c, 1)
+            finish(NU // 2 - 1, 2)
+            finish(NU // 2 - 1, 3)

@@ -28,7 +28,7 @@ HALF = BLOCK // 2
 NT = 2
 UNIT = NT * P
 NU = T // UNIT
-CAST = ((0, 0), (0, 0), (4, 0), (4, 0), (4, 4), (4, 0), (4, 4), (4, 0), (4, 4), (4, 0), (4, 4), (4, 0), (4, 4), (4, 0), (4, 4), (4, 0))
+CAST = ((0, 4), (0, 4), (4, 0), (4, 0), (4, 4), (4, 0), (4, 4), (4, 0), (4, 4), (4, 0), (4, 4), (4, 0), (4, 4), (4, 0), (4, 4), (4, 2))
 TURN_BANKS = 4
 SUM_BANKS = 8 - TURN_BANKS
 
@@ -63,7 +63,7 @@ def tile_aged_key_retrieval_d3_kernel(tc, query, keys_bytes, keys_scale, age, ra
         out_view = out.rearrange("(p m) n -> p m n", m=M)
         park = out[Q - 1 : Q, :]
 
-        raw, cast, split, turned, codes, banks, sums, results = {}, {}, {}, {}, {}, {}, {}, {}
+        raw, cast, split, turned, codes, banks, sums, pair = {}, {}, {}, {}, {}, {}, {}, {}
 
         def load_keys(v, j=0, n=NT):
             rows = raw_pool.tile([P, n, K], U8, name="raw_keys")
@@ -95,11 +95,13 @@ def tile_aged_key_retrieval_d3_kernel(tc, query, keys_bytes, keys_scale, age, ra
                 split[v, j] = split_pool.tile([P, 2, K // BLOCK, HALF], BF16, name="split_rows")
             return split[v, j][:, :, PASS // BLOCK * g0 : PASS // BLOCK * g1, :]
 
-        def cast_tile(v, j):
-            g = CAST[v][j]
-            if g > 0:
-                cast[v, j] = cast_pool.tile([P, K], BF16, name="cast_rows")
-                nc.scalar.copy(out=cast[v, j][:, : PASS * g], in_=raw[v, j][:, : PASS * g].bitcast(FP8))
+        def cast_tile(v, j, g0=0, g1=G):
+            g1 = min(g1, CAST[v][j])
+            if g1 > g0:
+                if g0 == 0:
+                    cast[v, j] = cast_pool.tile([P, K], BF16, name="cast_rows")
+                cols = slice(PASS * g0, PASS * g1)
+                nc.scalar.copy(out=cast[v, j][:, cols], in_=raw[v, j][:, cols].bitcast(FP8))
 
         def widen(v, j, g0=0, g1=G):
             g = CAST[v][j]
@@ -181,15 +183,20 @@ def tile_aged_key_retrieval_d3_kernel(tc, query, keys_bytes, keys_scale, age, ra
                 in_=turned["query", m][:].rearrange("p n t -> p (n t)"),
             )
 
-        def multiply(v, m):
+        def multiply(v, m, g0=0, g1=G):
             c, half = divmod(v, 2)
-            if half == 0:
-                sums[c, m] = sum_psum.tile([P, 2 * UNIT], F32, name="acc")
-            for g in range(G):
-                key_codes, key_scales = codes[v]
+            if g0 == 0 and v == NU - 1:
+                bank = turn_psum.tile([P, 2, NT, P], F32, name="bank")
+                sums[v, m] = bank[:, 0].rearrange("p j r -> p (j r)")
+            elif g0 == 0:
+                if half == 0:
+                    pair[c, m] = sum_psum.tile([P, 2 * UNIT], F32, name="acc")
+                sums[v, m] = pair[c, m][:, UNIT * half : UNIT * (half + 1)]
+            key_codes, key_scales = codes[v]
+            for g in range(g0, g1):
                 cols = slice(UNIT * g, UNIT * (g + 1))
                 nc.tensor.matmul_mx(
-                    out=sums[c, m][:, UNIT * half : UNIT * (half + 1)],
+                    out=sums[v, m],
                     lhsT=q_codes[m][:, P * g : P * (g + 1)].bitcast(FP8X4),
                     lhsT_scale=q_scales[m][:, P * g : P * (g + 1)],
                     rhs=key_codes[:, cols].bitcast(FP8X4),
@@ -198,17 +205,24 @@ def tile_aged_key_retrieval_d3_kernel(tc, query, keys_bytes, keys_scale, age, ra
                     stop=(g == G - 1),
                 )
 
-        def finish(c, m, lo=0, hi=2 * UNIT):
-            result = result_pool.tile([P, hi - lo], F32, name="scores")
+        def finish(acc, first, width, m):
+            c, lo = divmod(first, 2 * UNIT)
+            result = result_pool.tile([P, width], F32, name="scores")
             nc.vector.scalar_tensor_tensor(
                 out=result[:],
-                in0=stale[c][:, lo:hi],
+                in0=stale[c][:, lo : lo + width],
                 scalar=neg_rate[:, m : m + 1],
-                in1=sums[c, m][:, lo:hi],
+                in1=acc,
                 op0=MULT,
                 op1=ADD,
             )
-            nc.sync.dma_start(out=out_view[:, m, 2 * UNIT * c + lo : 2 * UNIT * c + hi], in_=result[:])
+            nc.sync.dma_start(out=out_view[:, m, first : first + width], in_=result[:])
+
+        def finish_pair(c, m):
+            finish(pair[c, m][:], 2 * UNIT * c, 2 * UNIT, m)
+
+        def finish_unit(v, m):
+            finish(sums[v, m], UNIT * v, UNIT, m)
 
 
         with tc.manual_schedule():
@@ -216,8 +230,8 @@ def tile_aged_key_retrieval_d3_kernel(tc, query, keys_bytes, keys_scale, age, ra
             nc.scalar.dma_start(out=age_sb[:], in_=age.rearrange("(p i) -> p i", p=P))
             load_keys(0, 0, 1)
             load_keys(0, 1, 1)
-            load_query(0)
             load_keys(1)
+            load_query(0)
             load_query(1)
             load_keys(2)
             load_query(2)
@@ -234,11 +248,12 @@ def tile_aged_key_retrieval_d3_kernel(tc, query, keys_bytes, keys_scale, age, ra
             load_stale(1)
             load_keys(6)
             load_stale(2)
-            widen(0, 0, 0, 2)
+            cast_tile(0, 1, 0, 2)
+            cast_tile(0, 1, 2, 4)
+            widen(0, 0)
             widen(0, 1, 0, 2)
-            widen(0, 0, 2, 4)
             widen(0, 1, 2, 4)
-            part_query(0)
+            cast_tile(1, 1)
             turn_keys(0, 0)
             empty_keys(0, 0)
             turn_keys(0, 1)
@@ -247,19 +262,14 @@ def tile_aged_key_retrieval_d3_kernel(tc, query, keys_bytes, keys_scale, age, ra
             empty_keys(0, 2)
             turn_keys(0, 3)
             empty_keys(0, 3)
+            widen(1, 0)
+            part_query(0)
+            widen(1, 1)
             turn_query(0, 0)
             empty_query(0, 0)
             turn_query(0, 1)
             empty_query(0, 1)
-            widen(1, 0)
             part_query(1)
-            widen(1, 1)
-            turn_query(1, 0)
-            empty_query(1, 0)
-            turn_query(1, 1)
-            empty_query(1, 1)
-            quantize_keys(0)
-            quantize_query(0)
             turn_keys(1, 0)
             empty_keys(1, 0)
             turn_keys(1, 1)
@@ -268,11 +278,17 @@ def tile_aged_key_retrieval_d3_kernel(tc, query, keys_bytes, keys_scale, age, ra
             empty_keys(1, 2)
             turn_keys(1, 3)
             empty_keys(1, 3)
+            quantize_keys(0)
+            quantize_query(0)
+            turn_query(1, 0)
+            empty_query(1, 0)
+            turn_query(1, 1)
+            empty_query(1, 1)
             part_query(2)
-            quantize_query(1)
-            part_query(3)
             multiply(0, 0)
-            multiply(0, 1)
+            part_query(3)
+            quantize_keys(1)
+            quantize_query(1)
             cast_tile(2, 0)
             cast_tile(2, 1)
             turn_query(2, 0)
@@ -283,14 +299,14 @@ def tile_aged_key_retrieval_d3_kernel(tc, query, keys_bytes, keys_scale, age, ra
             empty_query(3, 0)
             turn_query(3, 1)
             empty_query(3, 1)
-            quantize_keys(1)
+            multiply(1, 0)
+            multiply(0, 1)
+            multiply(1, 1)
             widen(2, 0)
             widen(2, 1)
             nc.scalar.activation(out=neg_rate[:], in_=rate_sb[:], func=COPY, scale=-1.0)
             cast_tile(3, 0)
             cast_tile(3, 1)
-            multiply(1, 0)
-            multiply(1, 1)
             quantize_query(2)
             quantize_query(3)
             turn_keys(2, 0)
@@ -301,8 +317,8 @@ def tile_aged_key_retrieval_d3_kernel(tc, query, keys_bytes, keys_scale, age, ra
             empty_keys(2, 2)
             turn_keys(2, 3)
             empty_keys(2, 3)
-            finish(0, 0)
-            finish(0, 1)
+            finish_pair(0, 0)
+            finish_pair(0, 1)
             multiply(0, 2)
             multiply(0, 3)
             cast_tile(4, 0)
@@ -313,7 +329,7 @@ def tile_aged_key_retrieval_d3_kernel(tc, query, keys_bytes, keys_scale, age, ra
             multiply(1, 3)
             quantize_keys(2)
 
-            for v in range(2, NU):
+            for v in range(2, NU - 2):
                 c, half = divmod(v, 2)
                 if v + 5 < NU:
                     load_keys(v + 5)
@@ -327,8 +343,8 @@ def tile_aged_key_retrieval_d3_kernel(tc, query, keys_bytes, keys_scale, age, ra
                     cast_tile(v + 3, 0)
                     cast_tile(v + 3, 1)
                 if half == 0:
-                    finish(c - 1, 2)
-                    finish(c - 1, 3)
+                    finish_pair(c - 1, 2)
+                    finish_pair(c - 1, 3)
                 for m in range(M):
                     multiply(v, m)
                 if v + 2 < NU:
@@ -337,10 +353,40 @@ def tile_aged_key_retrieval_d3_kernel(tc, query, keys_bytes, keys_scale, age, ra
                 if v + 1 < NU:
                     quantize_keys(v + 1, 0, 2)
                 if half == 1:
-                    finish(c, 0)
+                    finish_pair(c, 0)
                 if v + 1 < NU:
                     quantize_keys(v + 1, 2, 4)
                 if half == 1:
-                    finish(c, 1)
-            finish(NU // 2 - 1, 2)
-            finish(NU // 2 - 1, 3)
+                    finish_pair(c, 1)
+            turn_keys(15, 0)
+            empty_keys(15, 0)
+            turn_keys(15, 1)
+            empty_keys(15, 1)
+            turn_keys(15, 2)
+            empty_keys(15, 2)
+            turn_keys(15, 3)
+            empty_keys(15, 3)
+            finish_pair(6, 2)
+            finish_pair(6, 3)
+            multiply(14, 0)
+            multiply(14, 1)
+            multiply(14, 2)
+            multiply(14, 3)
+            quantize_keys(15, 0, 2)
+            finish_unit(14, 0)
+            finish_unit(14, 1)
+            multiply(15, 0, 0, 2)
+            multiply(15, 1, 0, 2)
+            multiply(15, 2, 0, 2)
+            multiply(15, 3, 0, 2)
+            quantize_keys(15, 2, 4)
+            finish_unit(14, 2)
+            finish_unit(14, 3)
+            multiply(15, 0, 2, 4)
+            finish_unit(15, 0)
+            multiply(15, 1, 2, 4)
+            finish_unit(15, 1)
+            multiply(15, 2, 2, 4)
+            finish_unit(15, 2)
+            multiply(15, 3, 2, 4)
+            finish_unit(15, 3)

@@ -28,7 +28,8 @@ HALF = BLOCK // 2
 NT = 2
 UNIT = NT * P
 NU = T // UNIT
-CAST = ((0, 4), (0, 4), (4, 0), (4, 0), (4, 4), (4, 0), (4, 4), (4, 0), (4, 4), (4, 0), (4, 4), (4, 0), (4, 4), (4, 0), (4, 4), (4, 2))
+CAST = ((0, 4), (0, 4), (4, 0), (4, 0), (4, 4), (4, 0), (3, 4), (4, 0), (3, 4), (4, 0), (3, 4), (4, 0), (3, 4), (4, 0), (3, 4), (4, 2))
+POOLED = ((6, 0), (8, 0), (10, 0), (12, 0), (14, 0))
 TURN_BANKS = 4
 SUM_BANKS = 8 - TURN_BANKS
 
@@ -40,7 +41,8 @@ def tile_aged_key_retrieval_d3_kernel(tc, query, keys_bytes, keys_scale, age, ra
         raw_pool = ctx.enter_context(tc.tile_pool(name="raw", bufs=8))
         cast_pool = ctx.enter_context(tc.tile_pool(name="cast", bufs=6))
         split_pool = ctx.enter_context(tc.tile_pool(name="split", bufs=8))
-        turned_pool = ctx.enter_context(tc.tile_pool(name="turned", bufs=4))
+        hand_pool = ctx.enter_context(tc.tile_pool(name="hand", bufs=1))
+        turned_pool = ctx.enter_context(tc.tile_pool(name="turned", bufs=6))
         code_pool = ctx.enter_context(tc.tile_pool(name="code", bufs=4))
         result_pool = ctx.enter_context(tc.tile_pool(name="result", bufs=10))
         turn_psum = ctx.enter_context(tc.psum_pool(name="turn", bufs=TURN_BANKS))
@@ -91,6 +93,8 @@ def tile_aged_key_retrieval_d3_kernel(tc, query, keys_bytes, keys_scale, age, ra
             nc.vector.tensor_copy(out=scale_sb[:], in_=bank[:, 0, 0, : T // P])
 
         def halves(v, j, g0, g1):
+            if (v, j) not in split and (v, j) in POOLED:
+                split[v, j] = hand_pool.tile([P, 2, K // BLOCK, HALF], BF16, name="hand", align_bytes=64)
             if (v, j) not in split:
                 split[v, j] = split_pool.tile([P, 2, K // BLOCK, HALF], BF16, name="split_rows")
             return split[v, j][:, :, PASS // BLOCK * g0 : PASS // BLOCK * g1, :]
@@ -124,6 +128,17 @@ def tile_aged_key_retrieval_d3_kernel(tc, query, keys_bytes, keys_scale, age, ra
                     op0=MULT,
                 )
 
+        def scale_on_gpsimd(v, j):
+            g = CAST[v][j]
+            nc.gpsimd.tensor_scalar(
+                out=halves(v, j, 0, g),
+                in0=cast[v, j][:, : PASS * g].rearrange("p (w u e) -> p u w e", u=2, e=HALF),
+                scalar1=scale_col(v, j),
+                scalar2=0.0,
+                op0=MULT,
+                op1=ADD,
+            )
+
         def part_query(m):
             nc.vector.tensor_copy(
                 out=halves("query", m, 0, G),
@@ -147,9 +162,11 @@ def tile_aged_key_retrieval_d3_kernel(tc, query, keys_bytes, keys_scale, age, ra
                     half = split["query", m][:, u].rearrange("p w e -> p (w e)").bitcast(F32)
                     nc.tensor.transpose(bank[:, u, j, :], half[:, P * g : P * (g + 1)], ident[:])
 
-        def empty(bank, key, half, engine, width):
-            if half == 0:
-                turned[key] = turned_pool.tile([P, width, 4], BF16, name="turned_rows", align_bytes=64)
+        def empty(bank, key, half, engine):
+            if half == 0 and key[1] == 1 and (key[0] + 2, 0) in POOLED:
+                turned[key] = hand_pool.tile([P, PASS, 4], BF16, name="hand", align_bytes=64)
+            elif half == 0:
+                turned[key] = turned_pool.tile([P, PASS, 4], BF16, name="turned_rows", align_bytes=64)
             dst = turned[key][:, 2 * P * half : 2 * P * (half + 1), :].bitcast(F32)
             src = bank[:].rearrange("p u j r -> p (j r) u")
             if engine == "scalar":
@@ -158,10 +175,10 @@ def tile_aged_key_retrieval_d3_kernel(tc, query, keys_bytes, keys_scale, age, ra
                 nc.vector.tensor_copy(out=dst, in_=src)
 
         def empty_keys(v, g, engine="scalar"):
-            empty(banks[v, g], v, g, engine, G * UNIT)
+            empty(banks[v, g], (v, g // 2), g % 2, engine)
 
         def empty_query(m, h, engine="scalar"):
-            empty(banks["query", m, h], ("query", m), h, engine, G * P)
+            empty(banks["query", m, h], (-1 - m, 0), h, engine)
 
         def quantize_keys(v, g0=0, g1=G):
             if g0 == 0:
@@ -173,14 +190,14 @@ def tile_aged_key_retrieval_d3_kernel(tc, query, keys_bytes, keys_scale, age, ra
             nc.vector.quantize_mx(
                 out=key_codes[:, cols].bitcast(FP8X4),
                 scales=key_scales[:, cols],
-                in_=turned[v][:, cols, :].rearrange("p n t -> p (n t)"),
+                in_=turned[v, g0 // 2][:].rearrange("p n t -> p (n t)"),
             )
 
         def quantize_query(m):
             nc.vector.quantize_mx(
                 out=q_codes[m][:].bitcast(FP8X4),
                 scales=q_scales[m][:],
-                in_=turned["query", m][:].rearrange("p n t -> p (n t)"),
+                in_=turned[-1 - m, 0][:].rearrange("p n t -> p (n t)"),
             )
 
         def multiply(v, m, g0=0, g1=G):
@@ -278,7 +295,8 @@ def tile_aged_key_retrieval_d3_kernel(tc, query, keys_bytes, keys_scale, age, ra
             empty_keys(1, 2)
             turn_keys(1, 3)
             empty_keys(1, 3)
-            quantize_keys(0)
+            quantize_keys(0, 0, 2)
+            quantize_keys(0, 2, 4)
             quantize_query(0)
             turn_query(1, 0)
             empty_query(1, 0)
@@ -287,7 +305,8 @@ def tile_aged_key_retrieval_d3_kernel(tc, query, keys_bytes, keys_scale, age, ra
             part_query(2)
             multiply(0, 0)
             part_query(3)
-            quantize_keys(1)
+            quantize_keys(1, 0, 2)
+            quantize_keys(1, 2, 4)
             quantize_query(1)
             cast_tile(2, 0)
             cast_tile(2, 1)
@@ -327,7 +346,8 @@ def tile_aged_key_retrieval_d3_kernel(tc, query, keys_bytes, keys_scale, age, ra
             widen(3, 1)
             multiply(1, 2)
             multiply(1, 3)
-            quantize_keys(2)
+            quantize_keys(2, 0, 2)
+            quantize_keys(2, 2, 4)
 
             for v in range(2, NU - 2):
                 c, half = divmod(v, 2)
@@ -335,29 +355,23 @@ def tile_aged_key_retrieval_d3_kernel(tc, query, keys_bytes, keys_scale, age, ra
                     load_keys(v + 5)
                 if half == 0 and c + 2 < NU // 2:
                     load_stale(c + 2)
-                if v + 1 < NU:
-                    for g in range(G):
-                        turn_keys(v + 1, g)
-                        empty_keys(v + 1, g)
+                for g in range(G):
+                    turn_keys(v + 1, g)
+                    empty_keys(v + 1, g)
                 if v + 3 < NU:
                     cast_tile(v + 3, 0)
                     cast_tile(v + 3, 1)
                 if half == 0:
-                    finish_pair(c - 1, 2)
-                    finish_pair(c - 1, 3)
+                    if (v + 2, 0) in POOLED:
+                        scale_on_gpsimd(v + 2, 0)
+                    for m in range(2 if v == 2 else 0, M):
+                        finish_pair(c - 1, m)
                 for m in range(M):
                     multiply(v, m)
-                if v + 2 < NU:
-                    widen(v + 2, 0)
-                    widen(v + 2, 1)
-                if v + 1 < NU:
-                    quantize_keys(v + 1, 0, 2)
-                if half == 1:
-                    finish_pair(c, 0)
-                if v + 1 < NU:
-                    quantize_keys(v + 1, 2, 4)
-                if half == 1:
-                    finish_pair(c, 1)
+                widen(v + 2, 1)
+                widen(v + 2, 0, CAST[v + 2][0] if (v + 2, 0) in POOLED else 0)
+                quantize_keys(v + 1, 0, 2)
+                quantize_keys(v + 1, 2, 4)
             turn_keys(15, 0)
             empty_keys(15, 0)
             turn_keys(15, 1)
@@ -366,6 +380,8 @@ def tile_aged_key_retrieval_d3_kernel(tc, query, keys_bytes, keys_scale, age, ra
             empty_keys(15, 2)
             turn_keys(15, 3)
             empty_keys(15, 3)
+            finish_pair(6, 0)
+            finish_pair(6, 1)
             finish_pair(6, 2)
             finish_pair(6, 3)
             multiply(14, 0)

@@ -30,6 +30,7 @@ UNIT = NT * P
 NU = T // UNIT
 CAST = ((0, 4), (0, 4), (4, 0), (4, 0), (4, 4), (4, 0), (3, 4), (4, 0), (3, 4), (4, 0), (3, 4), (4, 0), (3, 4), (4, 0), (3, 4), (4, 2))
 POOLED = ((6, 0), (8, 0), (10, 0), (12, 0), (14, 0))
+POOL_PASSES = 2
 TURN_BANKS = 4
 SUM_BANKS = 8 - TURN_BANKS
 
@@ -73,6 +74,18 @@ def tile_aged_key_retrieval_d3_kernel(tc, query, keys_bytes, keys_scale, age, ra
             for i in range(n):
                 raw[v, j + i] = rows[:, i, :]
 
+        def load_key_half(v, h):
+            rows = raw_pool.tile([P, NT, K // 2], U8, name="raw_keys")
+            nc.sync.dma_start(out=rows[:], in_=key_view[v][:, :, K // 2 * h : K // 2 * (h + 1)])
+            for j in range(NT):
+                raw[v, j, h] = rows[:, j, :]
+
+        def key_bytes(v, j, g0, g1):
+            if (v, j) in raw:
+                return raw[v, j][:, PASS * g0 : PASS * g1].bitcast(FP8)
+            h = g0 // 2
+            return raw[v, j, h][:, PASS * (g0 - 2 * h) : PASS * (g1 - 2 * h)].bitcast(FP8)
+
         def load_query(m):
             nc.sync.dma_start(out=query_sb[m][:], in_=query_view[:, m, :])
 
@@ -105,15 +118,15 @@ def tile_aged_key_retrieval_d3_kernel(tc, query, keys_bytes, keys_scale, age, ra
                 if g0 == 0:
                     cast[v, j] = cast_pool.tile([P, K], BF16, name="cast_rows")
                 cols = slice(PASS * g0, PASS * g1)
-                nc.scalar.copy(out=cast[v, j][:, cols], in_=raw[v, j][:, cols].bitcast(FP8))
+                nc.scalar.copy(out=cast[v, j][:, cols], in_=key_bytes(v, j, g0, g1))
 
         def widen(v, j, g0=0, g1=G):
             g = CAST[v][j]
             if g > g0:
                 hi = min(g, g1)
                 nc.vector.tensor_scalar(
-                    out=halves(v, j, g0, hi),
-                    in0=cast[v, j][:, PASS * g0 : PASS * hi].rearrange("p (w u e) -> p u w e", u=2, e=HALF),
+                    out=halves(v, j, g0, hi).rearrange("p u w e -> p w u e"),
+                    in0=cast[v, j][:, PASS * g0 : PASS * hi].rearrange("p (w u e) -> p w u e", u=2, e=HALF),
                     scalar1=scale_col(v, j),
                     scalar2=None,
                     op0=MULT,
@@ -122,14 +135,14 @@ def tile_aged_key_retrieval_d3_kernel(tc, query, keys_bytes, keys_scale, age, ra
                 lo = max(g, g0)
                 nc.vector.tensor_scalar(
                     out=halves(v, j, lo, g1).rearrange("p u w e -> p w u e"),
-                    in0=raw[v, j][:, PASS * lo : PASS * g1].bitcast(FP8).rearrange("p (w u e) -> p w u e", u=2, e=HALF),
+                    in0=key_bytes(v, j, lo, g1).rearrange("p (w u e) -> p w u e", u=2, e=HALF),
                     scalar1=scale_col(v, j),
                     scalar2=None,
                     op0=MULT,
                 )
 
         def scale_on_gpsimd(v, j):
-            g = CAST[v][j]
+            g = POOL_PASSES
             nc.gpsimd.tensor_scalar(
                 out=halves(v, j, 0, g),
                 in0=cast[v, j][:, : PASS * g].rearrange("p (w u e) -> p u w e", u=2, e=HALF),
@@ -141,8 +154,8 @@ def tile_aged_key_retrieval_d3_kernel(tc, query, keys_bytes, keys_scale, age, ra
 
         def part_query(m):
             nc.vector.tensor_copy(
-                out=halves("query", m, 0, G),
-                in_=query_sb[m][:].rearrange("p (w u e) -> p u w e", u=2, e=HALF),
+                out=halves("query", m, 0, G).rearrange("p u w e -> p w u e"),
+                in_=query_sb[m][:].rearrange("p (w u e) -> p w u e", u=2, e=HALF),
             )
 
         def turn_keys(v, g):
@@ -245,9 +258,10 @@ def tile_aged_key_retrieval_d3_kernel(tc, query, keys_bytes, keys_scale, age, ra
         with tc.manual_schedule():
             load_scales()
             nc.scalar.dma_start(out=age_sb[:], in_=age.rearrange("(p i) -> p i", p=P))
-            load_keys(0, 0, 1)
-            load_keys(0, 1, 1)
-            load_keys(1)
+            load_key_half(0, 0)
+            load_key_half(0, 1)
+            load_keys(1, 1, 1)
+            load_keys(1, 0, 1)
             load_query(0)
             load_query(1)
             load_keys(2)
@@ -267,8 +281,9 @@ def tile_aged_key_retrieval_d3_kernel(tc, query, keys_bytes, keys_scale, age, ra
             load_stale(2)
             cast_tile(0, 1, 0, 2)
             cast_tile(0, 1, 2, 4)
-            widen(0, 0)
+            widen(0, 0, 0, 2)
             widen(0, 1, 0, 2)
+            widen(0, 0, 2, 4)
             widen(0, 1, 2, 4)
             cast_tile(1, 1)
             turn_keys(0, 0)
@@ -369,7 +384,7 @@ def tile_aged_key_retrieval_d3_kernel(tc, query, keys_bytes, keys_scale, age, ra
                 for m in range(M):
                     multiply(v, m)
                 widen(v + 2, 1)
-                widen(v + 2, 0, CAST[v + 2][0] if (v + 2, 0) in POOLED else 0)
+                widen(v + 2, 0, POOL_PASSES if (v + 2, 0) in POOLED else 0)
                 quantize_keys(v + 1, 0, 2)
                 quantize_keys(v + 1, 2, 4)
             turn_keys(15, 0)

@@ -45,7 +45,7 @@ def tile_aged_key_retrieval_d3_kernel(tc, query, keys_bytes, keys_scale, age, ra
         hand_pool = ctx.enter_context(tc.tile_pool(name="hand", bufs=1))
         turned_pool = ctx.enter_context(tc.tile_pool(name="turned", bufs=6))
         code_pool = ctx.enter_context(tc.tile_pool(name="code", bufs=4))
-        result_pool = ctx.enter_context(tc.tile_pool(name="result", bufs=10))
+        result_pool = ctx.enter_context(tc.tile_pool(name="result", bufs=14))
         turn_psum = ctx.enter_context(tc.psum_pool(name="turn", bufs=TURN_BANKS))
         sum_psum = ctx.enter_context(tc.psum_pool(name="sum", bufs=SUM_BANKS))
 
@@ -105,12 +105,19 @@ def tile_aged_key_retrieval_d3_kernel(tc, query, keys_bytes, keys_scale, age, ra
             nc.tensor.transpose(bank[:, 0, 0, :], scale_rows[:], ident[:])
             nc.vector.tensor_copy(out=scale_sb[:], in_=bank[:, 0, 0, : T // P])
 
-        def halves(v, j, g0, g1):
-            if (v, j) not in split and (v, j) in POOLED:
-                split[v, j] = hand_pool.tile([P, 2, K // BLOCK, HALF], BF16, name="hand", align_bytes=64)
-            if (v, j) not in split:
-                split[v, j] = split_pool.tile([P, 2, K // BLOCK, HALF], BF16, name="split_rows")
-            return split[v, j][:, :, PASS // BLOCK * g0 : PASS // BLOCK * g1, :]
+        def halves(v, j, g0, g1, pool=None):
+            n = g1 - g0
+            if pool is None:
+                piece = split_pool.tile([P, 2, n * PASS // BLOCK, HALF], BF16, name="split_%d" % n, bufs=8 if n == G else 4)
+            else:
+                piece = pool.tile([P, 2, n * PASS // BLOCK, HALF], BF16, name="hand", align_bytes=64)
+            for g in range(g0, g1):
+                split[v, j, g] = (piece, g - g0)
+            return piece[:]
+
+        def words(v, j, g, u):
+            piece, i = split[v, j, g]
+            return piece[:, u].rearrange("p w e -> p (w e)").bitcast(F32)[:, P * i : P * (i + 1)]
 
         def cast_tile(v, j, g0=0, g1=G):
             g1 = min(g1, CAST[v][j])
@@ -144,7 +151,7 @@ def tile_aged_key_retrieval_d3_kernel(tc, query, keys_bytes, keys_scale, age, ra
         def scale_on_gpsimd(v, j):
             g = POOL_PASSES
             nc.gpsimd.tensor_scalar(
-                out=halves(v, j, 0, g),
+                out=halves(v, j, 0, g, hand_pool),
                 in0=cast[v, j][:, : PASS * g].rearrange("p (w u e) -> p u w e", u=2, e=HALF),
                 scalar1=scale_col(v, j),
                 scalar2=0.0,
@@ -163,8 +170,7 @@ def tile_aged_key_retrieval_d3_kernel(tc, query, keys_bytes, keys_scale, age, ra
             banks[v, g] = bank
             for j in range(NT):
                 for u in range(2):
-                    half = split[v, j][:, u].rearrange("p w e -> p (w e)").bitcast(F32)
-                    nc.tensor.transpose(bank[:, u, j, :], half[:, P * g : P * (g + 1)], ident[:])
+                    nc.tensor.transpose(bank[:, u, j, :], words(v, j, g, u), ident[:])
 
         def turn_query(m, h):
             bank = turn_psum.tile([P, 2, 2, P], F32, name="bank")
@@ -172,8 +178,7 @@ def tile_aged_key_retrieval_d3_kernel(tc, query, keys_bytes, keys_scale, age, ra
             for j in range(2):
                 g = 2 * h + j
                 for u in range(2):
-                    half = split["query", m][:, u].rearrange("p w e -> p (w e)").bitcast(F32)
-                    nc.tensor.transpose(bank[:, u, j, :], half[:, P * g : P * (g + 1)], ident[:])
+                    nc.tensor.transpose(bank[:, u, j, :], words("query", m, g, u), ident[:])
 
         def empty(bank, key, half, engine):
             if half == 0 and key[1] == 1 and (key[0] + 2, 0) in POOLED:

@@ -56,6 +56,7 @@ def tile_aged_key_retrieval_d3_kernel(tc, query, keys_bytes, keys_scale, age, ra
         stale_sb = const.tile([P, T // P], F32, name="stale_sb")
         rate_sb = const.tile([P, M], BF16, name="rate_sb")
         neg_rate = const.tile([P, M], F32, name="neg_rate")
+        zeros = const.tile([P, 512], BF16, name="zeros")
         query_sb = [const.tile([P, K], BF16, name="query_%d" % m) for m in range(M)]
         q_codes = [const.tile([P, G * P], U32, name="q_codes_%d" % m, align_bytes=64) for m in range(M)]
         q_scales = [const.tile([P, G * P], U8, name="q_scales_%d" % m, align_bytes=64) for m in range(M)]
@@ -259,6 +260,10 @@ def tile_aged_key_retrieval_d3_kernel(tc, query, keys_bytes, keys_scale, age, ra
         def finish_unit(v, m):
             finish(sums[v, m], UNIT * v, UNIT, m)
 
+        def warm_up(n):
+            idle_bank = sum_psum.tile([P, 512], F32, name="acc")
+            for i in range(n):
+                nc.tensor.matmul(idle_bank[:], lhsT=zeros[:, :P], rhs=zeros[:], start=True, stop=True)
 
         with tc.manual_schedule():
             load_scales()
@@ -274,7 +279,9 @@ def tile_aged_key_retrieval_d3_kernel(tc, query, keys_bytes, keys_scale, age, ra
             load_query(3)
             load_keys(3)
             make_identity(nc, ident[:])
+            nc.vector.memset(zeros[:], 0.0)
             turn_scales()
+            warm_up(3)
             nc.scalar.activation(out=stale_sb[:], in_=age_sb[:], func=LN, bias=1.0)
             nc.sync.dma_start(out=park.rearrange("o (p i) -> p (o i)", p=P), in_=stale_sb[:])
             nc.sync.dma_start(out=rate_sb[:], in_=rate.rearrange("(p m) -> p m", m=M))
@@ -299,6 +306,7 @@ def tile_aged_key_retrieval_d3_kernel(tc, query, keys_bytes, keys_scale, age, ra
             empty_keys(0, 2)
             turn_keys(0, 3)
             empty_keys(0, 3)
+            warm_up(2)
             widen(1, 0)
             part_query(0)
             widen(1, 1)

@@ -25,14 +25,14 @@ M = Q // P
 
 BLOCK = 32
 HALF = BLOCK // 2
-NT = 2
-UNIT = NT * P
-NU = T // UNIT
-CAST = ((0, 4), (0, 4), (4, 0), (4, 0), (4, 4), (4, 0), (3, 4), (4, 0), (3, 4), (4, 0), (3, 4), (4, 0), (3, 4), (4, 0), (3, 4), (4, 2))
-POOLED = ((6, 0), (8, 0), (10, 0), (12, 0), (14, 0))
-POOL_PASSES = 2
+NT = T // P
+UNIT = 2 * P
+NS = NT // 2
+NARROW = (0, 1, 2, 3, NS - 2, NS - 1)
 TURN_BANKS = 4
-SUM_BANKS = 8 - TURN_BANKS
+SUM_BANKS = 4
+PLAN = ("d", "d", "d", "d", "ddcc", "ddcc", "cccg", "ddcc", "dccg", "ddcc", "cccg", "ddcc", "dccg", "ddcc", "cccg", "dc")
+POOLED = (6, 8, 10, 12, 14)
 
 
 def tile_aged_key_retrieval_d3_kernel(tc, query, keys_bytes, keys_scale, age, rate, out):
@@ -40,52 +40,52 @@ def tile_aged_key_retrieval_d3_kernel(tc, query, keys_bytes, keys_scale, age, ra
     with ExitStack() as ctx:
         const = ctx.enter_context(tc.tile_pool(name="const", bufs=1))
         raw_pool = ctx.enter_context(tc.tile_pool(name="raw", bufs=8))
-        cast_pool = ctx.enter_context(tc.tile_pool(name="cast", bufs=6))
-        split_pool = ctx.enter_context(tc.tile_pool(name="split", bufs=8))
+        cast_pool = ctx.enter_context(tc.tile_pool(name="cast", bufs=8))
+        split_pool = ctx.enter_context(tc.tile_pool(name="split", bufs=6))
         hand_pool = ctx.enter_context(tc.tile_pool(name="hand", bufs=1))
-        turned_pool = ctx.enter_context(tc.tile_pool(name="turned", bufs=6))
-        code_pool = ctx.enter_context(tc.tile_pool(name="code", bufs=4))
-        result_pool = ctx.enter_context(tc.tile_pool(name="result", bufs=14))
+        turned_pool = ctx.enter_context(tc.tile_pool(name="turned", bufs=5))
+        code_pool = ctx.enter_context(tc.tile_pool(name="code", bufs=7))
+        result_pool = ctx.enter_context(tc.tile_pool(name="result", bufs=12))
         turn_psum = ctx.enter_context(tc.psum_pool(name="turn", bufs=TURN_BANKS))
         sum_psum = ctx.enter_context(tc.psum_pool(name="sum", bufs=SUM_BANKS))
 
         ident = const.tile([P, P], F32, name="ident")
+        zeros = const.tile([P, 512], BF16, name="zeros")
         scale_rows = const.tile([P, P], F32, name="scale_rows")
-        scale_sb = const.tile([P, T // P], F32, name="scale_sb")
+        scale_sb = const.tile([P, NT], F32, name="scale_sb")
         age_sb = const.tile([P, T // P], BF16, name="age_sb")
         stale_sb = const.tile([P, T // P], F32, name="stale_sb")
         rate_sb = const.tile([P, M], BF16, name="rate_sb")
         neg_rate = const.tile([P, M], F32, name="neg_rate")
-        zeros = const.tile([P, 512], BF16, name="zeros")
         query_sb = [const.tile([P, K], BF16, name="query_%d" % m) for m in range(M)]
         q_codes = [const.tile([P, G * P], U32, name="q_codes_%d" % m, align_bytes=64) for m in range(M)]
         q_scales = [const.tile([P, G * P], U8, name="q_scales_%d" % m, align_bytes=64) for m in range(M)]
-        stale = [const.tile([P, 2 * UNIT], F32, name="stale_%d" % c) for c in range(NU // 2)]
+        stale = [const.tile([P, 2 * UNIT], F32, name="stale_%d" % c) for c in range(NS // 2)]
 
-        key_view = keys_bytes.rearrange("(v j p) k -> v p j k", p=P, j=NT)
+        key_view = keys_bytes.rearrange("(v j p) k -> v p j k", p=P, j=2)
         query_view = query.rearrange("(p m) k -> p m k", m=M)
         out_view = out.rearrange("(p m) n -> p m n", m=M)
         park = out[Q - 1 : Q, :]
 
-        raw, cast, split, turned, codes, banks, sums, pair = {}, {}, {}, {}, {}, {}, {}, {}
+        raw, cast, split, turned, codes, banks, sums = {}, {}, {}, {}, {}, {}, {}
 
-        def load_keys(v, j=0, n=NT):
+        def load_keys(v, j=0, n=2):
             rows = raw_pool.tile([P, n, K], U8, name="raw_keys")
             nc.sync.dma_start(out=rows[:], in_=key_view[v][:, j : j + n, :])
             for i in range(n):
-                raw[v, j + i] = rows[:, i, :]
+                for g in range(G):
+                    raw[2 * v + j + i, g] = (rows[:, i, :], g)
 
         def load_key_half(v, h):
-            rows = raw_pool.tile([P, NT, K // 2], U8, name="raw_keys")
+            rows = raw_pool.tile([P, 2, K // 2], U8, name="raw_keys")
             nc.sync.dma_start(out=rows[:], in_=key_view[v][:, :, K // 2 * h : K // 2 * (h + 1)])
-            for j in range(NT):
-                raw[v, j, h] = rows[:, j, :]
+            for j in range(2):
+                for g in range(2):
+                    raw[2 * v + j, 2 * h + g] = (rows[:, j, :], g)
 
-        def key_bytes(v, j, g0, g1):
-            if (v, j) in raw:
-                return raw[v, j][:, PASS * g0 : PASS * g1].bitcast(FP8)
-            h = g0 // 2
-            return raw[v, j, h][:, PASS * (g0 - 2 * h) : PASS * (g1 - 2 * h)].bitcast(FP8)
+        def key_bytes(t, g0, g1):
+            row, i = raw[t, g0]
+            return row[:, PASS * i : PASS * (i + g1 - g0)].bitcast(FP8)
 
         def load_query(m):
             nc.sync.dma_start(out=query_sb[m][:], in_=query_view[:, m, :])
@@ -93,68 +93,55 @@ def tile_aged_key_retrieval_d3_kernel(tc, query, keys_bytes, keys_scale, age, ra
         def load_stale(c):
             nc.sync.dma_start(out=stale[c][:], in_=park[0, 2 * UNIT * c : 2 * UNIT * (c + 1)].partition_broadcast(P))
 
-        def scale_col(v, j):
-            return scale_sb[:, NT * v + j : NT * v + j + 1]
-
         def load_scales():
-            nc.scalar.dma_start(out=scale_rows[: T // P, :], in_=keys_scale.rearrange("(i p) o -> i (p o)", p=P))
+            nc.scalar.dma_start(out=scale_rows[:NT, :], in_=keys_scale.rearrange("(i p) o -> i (p o)", p=P))
             nc.vector.memset(scale_rows[32:64, :], 0.0)
             nc.vector.memset(scale_rows[64:, :], 0.0)
 
         def turn_scales():
-            bank = turn_psum.tile([P, 2, NT, P], F32, name="bank")
+            bank = turn_psum.tile([P, 2, 2, P], F32, name="bank")
             nc.tensor.transpose(bank[:, 0, 0, :], scale_rows[:], ident[:])
-            nc.vector.tensor_copy(out=scale_sb[:], in_=bank[:, 0, 0, : T // P])
+            nc.vector.tensor_copy(out=scale_sb[:], in_=bank[:, 0, 0, :NT])
 
-        def halves(v, j, g0, g1, pool=None):
+        def halves(t, g0, g1, pool=None):
             n = g1 - g0
             if pool is None:
-                piece = split_pool.tile([P, 2, n * PASS // BLOCK, HALF], BF16, name="split_%d" % n, bufs=8 if n == G else 4)
+                piece = split_pool.tile([P, 2, n * PASS // BLOCK, HALF], BF16, name="split_%d" % n, bufs=8 if n == G else 10)
             else:
                 piece = pool.tile([P, 2, n * PASS // BLOCK, HALF], BF16, name="hand", align_bytes=64)
             for g in range(g0, g1):
-                split[v, j, g] = (piece, g - g0)
+                split[t, g] = (piece, g - g0)
             return piece[:]
 
-        def words(v, j, g, u):
-            piece, i = split[v, j, g]
+        def words(t, g, u):
+            piece, i = split[t, g]
             return piece[:, u].rearrange("p w e -> p (w e)").bitcast(F32)[:, P * i : P * (i + 1)]
 
-        def cast_tile(v, j, g0=0, g1=G):
-            g1 = min(g1, CAST[v][j])
-            if g1 > g0:
-                if g0 == 0:
-                    cast[v, j] = cast_pool.tile([P, K], BF16, name="cast_rows")
-                cols = slice(PASS * g0, PASS * g1)
-                nc.scalar.copy(out=cast[v, j][:, cols], in_=key_bytes(v, j, g0, g1))
+        def cast_tile(t, g0, g1):
+            rows = cast_pool.tile([P, PASS * (g1 - g0)], BF16, name="cast_rows")
+            for g in range(g0, g1):
+                cast[t, g] = (rows, g - g0)
+            nc.scalar.copy(out=rows[:], in_=key_bytes(t, g0, g1))
 
-        def widen(v, j, g0=0, g1=G):
-            g = CAST[v][j]
-            if g > g0:
-                hi = min(g, g1)
-                nc.vector.tensor_scalar(
-                    out=halves(v, j, g0, hi).rearrange("p u w e -> p w u e"),
-                    in0=cast[v, j][:, PASS * g0 : PASS * hi].rearrange("p (w u e) -> p w u e", u=2, e=HALF),
-                    scalar1=scale_col(v, j),
-                    scalar2=None,
-                    op0=MULT,
-                )
-            if g < g1:
-                lo = max(g, g0)
-                nc.vector.tensor_scalar(
-                    out=halves(v, j, lo, g1).rearrange("p u w e -> p w u e"),
-                    in0=key_bytes(v, j, lo, g1).rearrange("p (w u e) -> p w u e", u=2, e=HALF),
-                    scalar1=scale_col(v, j),
-                    scalar2=None,
-                    op0=MULT,
-                )
+        def cast_values(t, g0, g1):
+            rows, i = cast[t, g0]
+            return rows[:, PASS * i : PASS * (i + g1 - g0)]
 
-        def scale_on_gpsimd(v, j):
-            g = POOL_PASSES
+        def widen(t, g0, g1):
+            src = cast_values(t, g0, g1) if (t, g0) in cast else key_bytes(t, g0, g1)
+            nc.vector.tensor_scalar(
+                out=halves(t, g0, g1).rearrange("p u w e -> p w u e"),
+                in0=src.rearrange("p (w u e) -> p w u e", u=2, e=HALF),
+                scalar1=scale_sb[:, t : t + 1],
+                scalar2=None,
+                op0=MULT,
+            )
+
+        def scale_on_gpsimd(t, g0, g1):
             nc.gpsimd.tensor_scalar(
-                out=halves(v, j, 0, g, hand_pool),
-                in0=cast[v, j][:, : PASS * g].rearrange("p (w u e) -> p u w e", u=2, e=HALF),
-                scalar1=scale_col(v, j),
+                out=halves(t, g0, g1, hand_pool),
+                in0=cast_values(t, g0, g1).rearrange("p (w u e) -> p u w e", u=2, e=HALF),
+                scalar1=scale_sb[:, t : t + 1],
                 scalar2=0.0,
                 op0=MULT,
                 op1=ADD,
@@ -162,84 +149,89 @@ def tile_aged_key_retrieval_d3_kernel(tc, query, keys_bytes, keys_scale, age, ra
 
         def part_query(m):
             nc.vector.tensor_copy(
-                out=halves("query", m, 0, G).rearrange("p u w e -> p w u e"),
+                out=halves(NT + m, 0, G).rearrange("p u w e -> p w u e"),
                 in_=query_sb[m][:].rearrange("p (w u e) -> p w u e", u=2, e=HALF),
             )
 
-        def turn_keys(v, g):
-            bank = turn_psum.tile([P, 2, NT, P], F32, name="bank")
-            banks[v, g] = bank
-            for j in range(NT):
+        def quarter(s, q):
+            if s in NARROW:
+                return 2 * s, q
+            return 4 * (s // 2) + 2 * (q % 2), 2 * (s % 2) + q // 2
+
+        def turn_keys(s, q):
+            t, g = quarter(s, q)
+            bank = turn_psum.tile([P, 2, 2, P], F32, name="bank")
+            banks[s, q] = bank
+            for j in range(2):
                 for u in range(2):
-                    nc.tensor.transpose(bank[:, u, j, :], words(v, j, g, u), ident[:])
+                    nc.tensor.transpose(bank[:, u, j, :], words(t + j, g, u), ident[:])
 
         def turn_query(m, h):
             bank = turn_psum.tile([P, 2, 2, P], F32, name="bank")
             banks["query", m, h] = bank
             for j in range(2):
-                g = 2 * h + j
                 for u in range(2):
-                    nc.tensor.transpose(bank[:, u, j, :], words("query", m, g, u), ident[:])
+                    nc.tensor.transpose(bank[:, u, j, :], words(NT + m, 2 * h + j, u), ident[:])
 
-        def empty(bank, key, half, engine):
-            if half == 0 and key[1] == 1 and (key[0] + 2, 0) in POOLED:
+        def empty(bank, key, half):
+            if half == 0 and key[1] == 1 and key[0] + 2 in POOLED:
                 turned[key] = hand_pool.tile([P, PASS, 4], BF16, name="hand", align_bytes=64)
             elif half == 0:
                 turned[key] = turned_pool.tile([P, PASS, 4], BF16, name="turned_rows", align_bytes=64)
             dst = turned[key][:, 2 * P * half : 2 * P * (half + 1), :].bitcast(F32)
-            src = bank[:].rearrange("p u j r -> p (j r) u")
-            if engine == "scalar":
-                nc.scalar.copy(out=dst, in_=src)
-            else:
-                nc.vector.tensor_copy(out=dst, in_=src)
+            nc.scalar.copy(out=dst, in_=bank[:].rearrange("p u j r -> p (j r) u"))
 
-        def empty_keys(v, g, engine="scalar"):
-            empty(banks[v, g], (v, g // 2), g % 2, engine)
+        def empty_keys(s, q):
+            empty(banks[s, q], (s, q // 2), q % 2)
 
-        def empty_query(m, h, engine="scalar"):
-            empty(banks["query", m, h], (-1 - m, 0), h, engine)
+        def empty_query(m, h):
+            empty(banks["query", m, h], (NS + m, 0), h)
 
-        def quantize_keys(v, g0=0, g1=G):
-            if g0 == 0:
-                key_codes = code_pool.tile([P, G * UNIT], U32, name="key_codes", align_bytes=64)
-                key_scales = code_pool.tile([P, G * UNIT], U8, name="key_scales", align_bytes=64)
-                codes[v] = (key_codes, key_scales)
-            key_codes, key_scales = codes[v]
-            cols = slice(UNIT * g0, UNIT * g1)
+        def quantize_keys(s, z):
+            key_codes = code_pool.tile([P, PASS], U32, name="key_codes", align_bytes=64)
+            key_scales = code_pool.tile([P, PASS], U8, name="key_scales", align_bytes=64)
+            codes[s, z] = (key_codes, key_scales)
             nc.vector.quantize_mx(
-                out=key_codes[:, cols].bitcast(FP8X4),
-                scales=key_scales[:, cols],
-                in_=turned[v, g0 // 2][:].rearrange("p n t -> p (n t)"),
+                out=key_codes[:].bitcast(FP8X4),
+                scales=key_scales[:],
+                in_=turned[s, z][:].rearrange("p n t -> p (n t)"),
             )
 
         def quantize_query(m):
             nc.vector.quantize_mx(
                 out=q_codes[m][:].bitcast(FP8X4),
                 scales=q_scales[m][:],
-                in_=turned[-1 - m, 0][:].rearrange("p n t -> p (n t)"),
+                in_=turned[NS + m, 0][:].rearrange("p n t -> p (n t)"),
             )
 
-        def multiply(v, m, g0=0, g1=G):
-            c, half = divmod(v, 2)
-            if g0 == 0 and v == NU - 1:
-                bank = turn_psum.tile([P, 2, NT, P], F32, name="bank")
-                sums[v, m] = bank[:, 0].rearrange("p j r -> p (j r)")
-            elif g0 == 0:
-                if half == 0:
-                    pair[c, m] = sum_psum.tile([P, 2 * UNIT], F32, name="acc")
-                sums[v, m] = pair[c, m][:, UNIT * half : UNIT * (half + 1)]
-            key_codes, key_scales = codes[v]
-            for g in range(g0, g1):
-                cols = slice(UNIT * g, UNIT * (g + 1))
-                nc.tensor.matmul_mx(
-                    out=sums[v, m],
-                    lhsT=q_codes[m][:, P * g : P * (g + 1)].bitcast(FP8X4),
-                    lhsT_scale=q_scales[m][:, P * g : P * (g + 1)],
-                    rhs=key_codes[:, cols].bitcast(FP8X4),
-                    rhs_scale=key_scales[:, cols],
-                    start=(g == 0),
-                    stop=(g == G - 1),
-                )
+        def product(acc, m, g, key_codes, key_scales):
+            nc.tensor.matmul_mx(
+                out=acc,
+                lhsT=q_codes[m][:, P * g : P * (g + 1)].bitcast(FP8X4),
+                lhsT_scale=q_scales[m][:, P * g : P * (g + 1)],
+                rhs=key_codes.bitcast(FP8X4),
+                rhs_scale=key_scales,
+                start=(g == 0),
+                stop=(g == G - 1),
+            )
+
+        def multiply(s, m, z0=0, z1=2):
+            c, h = divmod(s, 2)
+            if s == NS - 1 and z0 == 0:
+                bank = turn_psum.tile([P, 2, 2, P], F32, name="bank")
+                sums["last", m] = bank[:].rearrange("p u j r -> p (u j r)")
+            elif h == 0 and z0 == 0:
+                acc = sum_psum.tile([P, 2 * UNIT], F32, name="acc")
+                sums[c, m] = acc[:]
+            for z in range(z0, z1):
+                key_codes, key_scales = codes[s, z]
+                if s not in NARROW:
+                    product(sums[c, m], m, 2 * h + z, key_codes[:], key_scales[:])
+                    continue
+                acc = sums["last", m][:, :UNIT] if s == NS - 1 else sums[c, m][:, UNIT * h : UNIT * (h + 1)]
+                for i in range(2):
+                    cols = slice(UNIT * i, UNIT * (i + 1))
+                    product(acc, m, 2 * z + i, key_codes[:, cols], key_scales[:, cols])
 
         def finish(acc, first, width, m):
             c, lo = divmod(first, 2 * UNIT)
@@ -255,15 +247,32 @@ def tile_aged_key_retrieval_d3_kernel(tc, query, keys_bytes, keys_scale, age, ra
             nc.sync.dma_start(out=out_view[:, m, first : first + width], in_=result[:])
 
         def finish_pair(c, m):
-            finish(pair[c, m][:], 2 * UNIT * c, 2 * UNIT, m)
+            finish(sums[c, m], 2 * UNIT * c, 2 * UNIT, m)
 
-        def finish_unit(v, m):
-            finish(sums[v, m], UNIT * v, UNIT, m)
+        def finish_unit(s, m):
+            finish(sums["last" if s == NS - 1 else s // 2, m][:, :UNIT], UNIT * s, UNIT, m)
 
         def warm_up(n):
             idle_bank = sum_psum.tile([P, 512], F32, name="acc")
             for i in range(n):
                 nc.tensor.matmul(idle_bank[:], lhsT=zeros[:, :P], rhs=zeros[:], start=True, stop=True)
+
+        def pieces(s, kinds):
+            if len(PLAN[s]) == 2:
+                every = [(2 * s + j, 0, G) for j in range(2)]
+            elif s in NARROW:
+                every = [(2 * s + j, g, g + 2) for g in (0, 2) for j in range(2)]
+            else:
+                every = [(4 * (s // 2) + j, 2 * (s % 2), 2 * (s % 2) + 2) for j in range(4)]
+            return [x for x, kind in zip(every, PLAN[s]) if kind in kinds]
+
+        def cast_step(s):
+            for x in pieces(s, "g") + pieces(s, "c"):
+                cast_tile(*x)
+
+        def widen_step(s):
+            for x in pieces(s, "cd"):
+                widen(*x)
 
         with tc.manual_schedule():
             load_scales()
@@ -273,17 +282,17 @@ def tile_aged_key_retrieval_d3_kernel(tc, query, keys_bytes, keys_scale, age, ra
             load_keys(1, 1, 1)
             load_keys(1, 0, 1)
             load_query(0)
-            load_query(1)
-            load_keys(2)
-            load_query(2)
-            load_query(3)
-            load_keys(3)
             make_identity(nc, ident[:])
             nc.vector.memset(zeros[:], 0.0)
             turn_scales()
             warm_up(3)
             nc.scalar.activation(out=stale_sb[:], in_=age_sb[:], func=LN, bias=1.0)
             nc.sync.dma_start(out=park.rearrange("o (p i) -> p (o i)", p=P), in_=stale_sb[:])
+            load_query(1)
+            load_keys(2)
+            load_query(2)
+            load_query(3)
+            load_keys(3)
             nc.sync.dma_start(out=rate_sb[:], in_=rate.rearrange("(p m) -> p m", m=M))
             load_keys(4)
             load_stale(0)
@@ -291,13 +300,14 @@ def tile_aged_key_retrieval_d3_kernel(tc, query, keys_bytes, keys_scale, age, ra
             load_stale(1)
             load_keys(6)
             load_stale(2)
-            cast_tile(0, 1, 0, 2)
-            cast_tile(0, 1, 2, 4)
-            widen(0, 0, 0, 2)
-            widen(0, 1, 0, 2)
-            widen(0, 0, 2, 4)
-            widen(0, 1, 2, 4)
-            cast_tile(1, 1)
+            load_keys(7)
+            cast_tile(1, 0, 2)
+            cast_tile(1, 2, 4)
+            widen(0, 0, 2)
+            widen(1, 0, 2)
+            widen(0, 2, 4)
+            widen(1, 2, 4)
+            cast_tile(3, 0, 4)
             turn_keys(0, 0)
             empty_keys(0, 0)
             turn_keys(0, 1)
@@ -307,9 +317,9 @@ def tile_aged_key_retrieval_d3_kernel(tc, query, keys_bytes, keys_scale, age, ra
             turn_keys(0, 3)
             empty_keys(0, 3)
             warm_up(2)
-            widen(1, 0)
+            widen(2, 0, 4)
             part_query(0)
-            widen(1, 1)
+            widen(3, 0, 4)
             turn_query(0, 0)
             empty_query(0, 0)
             turn_query(0, 1)
@@ -323,8 +333,8 @@ def tile_aged_key_retrieval_d3_kernel(tc, query, keys_bytes, keys_scale, age, ra
             empty_keys(1, 2)
             turn_keys(1, 3)
             empty_keys(1, 3)
-            quantize_keys(0, 0, 2)
-            quantize_keys(0, 2, 4)
+            quantize_keys(0, 0)
+            quantize_keys(0, 1)
             quantize_query(0)
             turn_query(1, 0)
             empty_query(1, 0)
@@ -333,11 +343,10 @@ def tile_aged_key_retrieval_d3_kernel(tc, query, keys_bytes, keys_scale, age, ra
             part_query(2)
             multiply(0, 0)
             part_query(3)
-            quantize_keys(1, 0, 2)
-            quantize_keys(1, 2, 4)
+            quantize_keys(1, 0)
+            quantize_keys(1, 1)
             quantize_query(1)
-            cast_tile(2, 0)
-            cast_tile(2, 1)
+            cast_tile(5, 0, 4)
             turn_query(2, 0)
             empty_query(2, 0)
             turn_query(2, 1)
@@ -349,11 +358,10 @@ def tile_aged_key_retrieval_d3_kernel(tc, query, keys_bytes, keys_scale, age, ra
             multiply(1, 0)
             multiply(0, 1)
             multiply(1, 1)
-            widen(2, 0)
-            widen(2, 1)
+            widen(4, 0, 4)
+            widen(5, 0, 4)
             nc.scalar.activation(out=neg_rate[:], in_=rate_sb[:], func=COPY, scale=-1.0)
-            cast_tile(3, 0)
-            cast_tile(3, 1)
+            cast_tile(7, 0, 4)
             quantize_query(2)
             quantize_query(3)
             turn_keys(2, 0)
@@ -368,38 +376,35 @@ def tile_aged_key_retrieval_d3_kernel(tc, query, keys_bytes, keys_scale, age, ra
             finish_pair(0, 1)
             multiply(0, 2)
             multiply(0, 3)
-            cast_tile(4, 0)
-            cast_tile(4, 1)
-            widen(3, 0)
-            widen(3, 1)
+            cast_step(4)
+            widen(6, 0, 4)
+            widen(7, 0, 4)
             multiply(1, 2)
             multiply(1, 3)
-            quantize_keys(2, 0, 2)
-            quantize_keys(2, 2, 4)
+            quantize_keys(2, 0)
+            quantize_keys(2, 1)
 
-            for v in range(2, NU - 2):
-                c, half = divmod(v, 2)
-                if v + 5 < NU:
-                    load_keys(v + 5)
-                if half == 0 and c + 2 < NU // 2:
+            for s in range(2, NS - 2):
+                c, h = divmod(s, 2)
+                if s + 6 < NS:
+                    load_keys(s + 6)
+                if h == 0 and c + 2 < NS // 2:
                     load_stale(c + 2)
-                for g in range(G):
-                    turn_keys(v + 1, g)
-                    empty_keys(v + 1, g)
-                if v + 3 < NU:
-                    cast_tile(v + 3, 0)
-                    cast_tile(v + 3, 1)
-                if half == 0:
-                    if (v + 2, 0) in POOLED:
-                        scale_on_gpsimd(v + 2, 0)
-                    for m in range(2 if v == 2 else 0, M):
+                for q in range(4):
+                    turn_keys(s + 1, q)
+                    empty_keys(s + 1, q)
+                if s + 3 < NS:
+                    cast_step(s + 3)
+                if h == 0:
+                    for x in pieces(s + 2, "g"):
+                        scale_on_gpsimd(*x)
+                    for m in range(2 if s == 2 else 0, M):
                         finish_pair(c - 1, m)
                 for m in range(M):
-                    multiply(v, m)
-                widen(v + 2, 1)
-                widen(v + 2, 0, POOL_PASSES if (v + 2, 0) in POOLED else 0)
-                quantize_keys(v + 1, 0, 2)
-                quantize_keys(v + 1, 2, 4)
+                    multiply(s, m)
+                widen_step(s + 2)
+                quantize_keys(s + 1, 0)
+                quantize_keys(s + 1, 1)
             turn_keys(15, 0)
             empty_keys(15, 0)
             turn_keys(15, 1)
@@ -416,21 +421,21 @@ def tile_aged_key_retrieval_d3_kernel(tc, query, keys_bytes, keys_scale, age, ra
             multiply(14, 1)
             multiply(14, 2)
             multiply(14, 3)
-            quantize_keys(15, 0, 2)
+            quantize_keys(15, 0)
             finish_unit(14, 0)
             finish_unit(14, 1)
-            multiply(15, 0, 0, 2)
-            multiply(15, 1, 0, 2)
-            multiply(15, 2, 0, 2)
-            multiply(15, 3, 0, 2)
-            quantize_keys(15, 2, 4)
+            multiply(15, 0, 0, 1)
+            multiply(15, 1, 0, 1)
+            multiply(15, 2, 0, 1)
+            multiply(15, 3, 0, 1)
+            quantize_keys(15, 1)
             finish_unit(14, 2)
             finish_unit(14, 3)
-            multiply(15, 0, 2, 4)
+            multiply(15, 0, 1, 2)
             finish_unit(15, 0)
-            multiply(15, 1, 2, 4)
+            multiply(15, 1, 1, 2)
             finish_unit(15, 1)
-            multiply(15, 2, 2, 4)
+            multiply(15, 2, 1, 2)
             finish_unit(15, 2)
-            multiply(15, 3, 2, 4)
+            multiply(15, 3, 1, 2)
             finish_unit(15, 3)

@@ -20,19 +20,20 @@ LN = mybir.ActivationFunctionType.Ln
 P = 128
 PASS = 512
 G = K // PASS
-PAIRS = PASS // 2
 M = Q // P
-
 BLOCK = 32
 HALF = BLOCK // 2
 NT = T // P
-UNIT = 2 * P
+GROUP = 4 * P
+TWO = 2 * P
+NG = T // GROUP
 NS = NT // 2
-NARROW = (0, 1, 2, 3, NS - 2, NS - 1)
-TURN_BANKS = 4
-SUM_BANKS = 4
-PLAN = ("d", "d", "d", "d", "ddcc", "ddcc", "cccg", "ddcc", "dccg", "ddcc", "cccg", "ddcc", "dccg", "ddcc", "cccg", "dc")
-POOLED = (6, 8, 10, 12, 14)
+BANKS = 4
+
+HEAD = 4
+NARROW = tuple(range(HEAD)) + (NS - 2, NS - 1)
+ON_GPSIMD = tuple(range(HEAD + 2, NS, 2))
+LOAD_AHEAD = 6
 
 
 def tile_aged_key_retrieval_d3_kernel(tc, query, keys_bytes, keys_scale, age, rate, out):
@@ -41,33 +42,34 @@ def tile_aged_key_retrieval_d3_kernel(tc, query, keys_bytes, keys_scale, age, ra
         const = ctx.enter_context(tc.tile_pool(name="const", bufs=1))
         raw_pool = ctx.enter_context(tc.tile_pool(name="raw", bufs=8))
         cast_pool = ctx.enter_context(tc.tile_pool(name="cast", bufs=8))
-        split_pool = ctx.enter_context(tc.tile_pool(name="split", bufs=6))
+        parted_pool = ctx.enter_context(tc.tile_pool(name="parted", bufs=1))
         hand_pool = ctx.enter_context(tc.tile_pool(name="hand", bufs=1))
         turned_pool = ctx.enter_context(tc.tile_pool(name="turned", bufs=5))
         code_pool = ctx.enter_context(tc.tile_pool(name="code", bufs=7))
         result_pool = ctx.enter_context(tc.tile_pool(name="result", bufs=12))
-        turn_psum = ctx.enter_context(tc.psum_pool(name="turn", bufs=TURN_BANKS))
-        sum_psum = ctx.enter_context(tc.psum_pool(name="sum", bufs=SUM_BANKS))
+        turn_psum = ctx.enter_context(tc.psum_pool(name="turn", bufs=BANKS))
+        sum_psum = ctx.enter_context(tc.psum_pool(name="sum", bufs=M))
 
         ident = const.tile([P, P], F32, name="ident")
-        zeros = const.tile([P, 512], BF16, name="zeros")
+        zeros = const.tile([P, GROUP], BF16, name="zeros")
         scale_rows = const.tile([P, P], F32, name="scale_rows")
         scale_sb = const.tile([P, NT], F32, name="scale_sb")
         age_sb = const.tile([P, T // P], BF16, name="age_sb")
-        stale_sb = const.tile([P, T // P], F32, name="stale_sb")
+        log_sb = const.tile([P, T // P], F32, name="log_sb")
         rate_sb = const.tile([P, M], BF16, name="rate_sb")
         neg_rate = const.tile([P, M], F32, name="neg_rate")
         query_sb = [const.tile([P, K], BF16, name="query_%d" % m) for m in range(M)]
         q_codes = [const.tile([P, G * P], U32, name="q_codes_%d" % m, align_bytes=64) for m in range(M)]
         q_scales = [const.tile([P, G * P], U8, name="q_scales_%d" % m, align_bytes=64) for m in range(M)]
-        stale = [const.tile([P, 2 * UNIT], F32, name="stale_%d" % c) for c in range(NS // 2)]
+        stale = [const.tile([P, GROUP], F32, name="stale_%d" % c) for c in range(NG)]
 
         key_view = keys_bytes.rearrange("(v j p) k -> v p j k", p=P, j=2)
         query_view = query.rearrange("(p m) k -> p m k", m=M)
         out_view = out.rearrange("(p m) n -> p m n", m=M)
         park = out[Q - 1 : Q, :]
 
-        raw, cast, split, turned, codes, banks, sums = {}, {}, {}, {}, {}, {}, {}
+        raw, cast, parted, turned, codes, sums = {}, {}, {}, {}, {}, {}
+
 
         def load_keys(v, j=0, n=2):
             rows = raw_pool.tile([P, n, K], U8, name="raw_keys")
@@ -76,62 +78,51 @@ def tile_aged_key_retrieval_d3_kernel(tc, query, keys_bytes, keys_scale, age, ra
                 for g in range(G):
                     raw[2 * v + j + i, g] = (rows[:, i, :], g)
 
-        def load_key_half(v, h):
+        def load_first_keys(h):
             rows = raw_pool.tile([P, 2, K // 2], U8, name="raw_keys")
-            nc.sync.dma_start(out=rows[:], in_=key_view[v][:, :, K // 2 * h : K // 2 * (h + 1)])
+            nc.sync.dma_start(out=rows[:], in_=key_view[0][:, :, K // 2 * h : K // 2 * (h + 1)])
             for j in range(2):
-                for g in range(2):
-                    raw[2 * v + j, 2 * h + g] = (rows[:, j, :], g)
-
-        def key_bytes(t, g0, g1):
-            row, i = raw[t, g0]
-            return row[:, PASS * i : PASS * (i + g1 - g0)].bitcast(FP8)
+                for i in range(2):
+                    raw[j, 2 * h + i] = (rows[:, j, :], i)
 
         def load_query(m):
             nc.sync.dma_start(out=query_sb[m][:], in_=query_view[:, m, :])
 
         def load_stale(c):
-            nc.sync.dma_start(out=stale[c][:], in_=park[0, 2 * UNIT * c : 2 * UNIT * (c + 1)].partition_broadcast(P))
+            nc.sync.dma_start(out=stale[c][:], in_=park[0, GROUP * c : GROUP * (c + 1)].partition_broadcast(P))
 
-        def load_scales():
-            nc.scalar.dma_start(out=scale_rows[:NT, :], in_=keys_scale.rearrange("(i p) o -> i (p o)", p=P))
-            nc.vector.memset(scale_rows[32:64, :], 0.0)
-            nc.vector.memset(scale_rows[64:, :], 0.0)
 
-        def turn_scales():
-            bank = turn_psum.tile([P, 2, 2, P], F32, name="bank")
-            nc.tensor.transpose(bank[:, 0, 0, :], scale_rows[:], ident[:])
-            nc.vector.tensor_copy(out=scale_sb[:], in_=bank[:, 0, 0, :NT])
-
-        def halves(t, g0, g1, pool=None):
-            n = g1 - g0
-            if pool is None:
-                piece = split_pool.tile([P, 2, n * PASS // BLOCK, HALF], BF16, name="split_%d" % n, bufs=8 if n == G else 10)
-            else:
-                piece = pool.tile([P, 2, n * PASS // BLOCK, HALF], BF16, name="hand", align_bytes=64)
-            for g in range(g0, g1):
-                split[t, g] = (piece, g - g0)
-            return piece[:]
-
-        def words(t, g, u):
-            piece, i = split[t, g]
-            return piece[:, u].rearrange("p w e -> p (w e)").bitcast(F32)[:, P * i : P * (i + 1)]
-
-        def cast_tile(t, g0, g1):
-            rows = cast_pool.tile([P, PASS * (g1 - g0)], BF16, name="cast_rows")
-            for g in range(g0, g1):
-                cast[t, g] = (rows, g - g0)
-            nc.scalar.copy(out=rows[:], in_=key_bytes(t, g0, g1))
+        def key_bytes(t, g0, g1):
+            row, i = raw[t, g0]
+            return row[:, PASS * i : PASS * (i + g1 - g0)].bitcast(FP8)
 
         def cast_values(t, g0, g1):
-            rows, i = cast[t, g0]
-            return rows[:, PASS * i : PASS * (i + g1 - g0)]
+            row, i = cast[t, g0]
+            return row[:, PASS * i : PASS * (i + g1 - g0)]
 
-        def widen(t, g0, g1):
-            src = cast_values(t, g0, g1) if (t, g0) in cast else key_bytes(t, g0, g1)
+        def new_piece(t, g0, g1, on_gpsimd=False):
+            shape = [P, 2, (g1 - g0) * PASS // BLOCK, HALF]
+            if on_gpsimd:
+                piece = hand_pool.tile(shape, BF16, name="hand", align_bytes=64)
+            elif g1 - g0 == G:
+                piece = parted_pool.tile(shape, BF16, name="parted_4", bufs=8)
+            else:
+                piece = parted_pool.tile(shape, BF16, name="parted_2", bufs=10)
+            for g in range(g0, g1):
+                parted[t, g] = (piece, g - g0)
+            return piece[:]
+
+        def cast_piece(t, g0, g1):
+            row = cast_pool.tile([P, PASS * (g1 - g0)], BF16, name="cast_row")
+            for g in range(g0, g1):
+                cast[t, g] = (row, g - g0)
+            nc.scalar.copy(out=row[:], in_=key_bytes(t, g0, g1))
+
+        def scale_piece(t, g0, g1):
+            values = cast_values(t, g0, g1) if (t, g0) in cast else key_bytes(t, g0, g1)
             nc.vector.tensor_scalar(
-                out=halves(t, g0, g1).rearrange("p u w e -> p w u e"),
-                in0=src.rearrange("p (w u e) -> p w u e", u=2, e=HALF),
+                out=new_piece(t, g0, g1).rearrange("p u a x -> p a u x"),
+                in0=values.rearrange("p (a u x) -> p a u x", u=2, x=HALF),
                 scalar1=scale_sb[:, t : t + 1],
                 scalar2=None,
                 op0=MULT,
@@ -139,8 +130,8 @@ def tile_aged_key_retrieval_d3_kernel(tc, query, keys_bytes, keys_scale, age, ra
 
         def scale_on_gpsimd(t, g0, g1):
             nc.gpsimd.tensor_scalar(
-                out=halves(t, g0, g1, hand_pool),
-                in0=cast_values(t, g0, g1).rearrange("p (w u e) -> p u w e", u=2, e=HALF),
+                out=new_piece(t, g0, g1, on_gpsimd=True),
+                in0=cast_values(t, g0, g1).rearrange("p (a u x) -> p u a x", u=2, x=HALF),
                 scalar1=scale_sb[:, t : t + 1],
                 scalar2=0.0,
                 op0=MULT,
@@ -149,60 +140,76 @@ def tile_aged_key_retrieval_d3_kernel(tc, query, keys_bytes, keys_scale, age, ra
 
         def part_query(m):
             nc.vector.tensor_copy(
-                out=halves(NT + m, 0, G).rearrange("p u w e -> p w u e"),
-                in_=query_sb[m][:].rearrange("p (w u e) -> p w u e", u=2, e=HALF),
+                out=new_piece(NT + m, 0, G).rearrange("p u a x -> p a u x"),
+                in_=query_sb[m][:].rearrange("p (a u x) -> p a u x", u=2, x=HALF),
             )
 
-        def quarter(s, q):
+        def pieces(s):
+            if s == NS - 1:
+                return [(2 * s + j, 0, G) for j in range(2)]
             if s in NARROW:
-                return 2 * s, q
-            return 4 * (s // 2) + 2 * (q % 2), 2 * (s % 2) + q // 2
+                return [(2 * s + j, g, g + 2) for g in (0, 2) for j in range(2)]
+            return [(4 * (s // 2) + j, 2 * (s % 2), 2 * (s % 2) + 2) for j in range(4)]
 
-        def turn_keys(s, q):
-            t, g = quarter(s, q)
+        def cast_step(s):
+            every = pieces(s)
+            if s in ON_GPSIMD:
+                chosen = every[3:] + every[0 if s % 4 == 0 else 1 : 3]
+            else:
+                chosen = every[len(every) // 2 :]
+            for piece in chosen:
+                cast_piece(*piece)
+
+        def scale_step(s):
+            for piece in pieces(s)[: 3 if s in ON_GPSIMD else 4]:
+                scale_piece(*piece)
+
+
+        def words(t, g, u):
+            piece, i = parted[t, g]
+            return piece[:, u].rearrange("p a x -> p (a x)").bitcast(F32)[:, P * i : P * (i + 1)]
+
+        def turn(key, half, pairs):
             bank = turn_psum.tile([P, 2, 2, P], F32, name="bank")
-            banks[s, q] = bank
-            for j in range(2):
+            for j, (t, g) in enumerate(pairs):
                 for u in range(2):
-                    nc.tensor.transpose(bank[:, u, j, :], words(t + j, g, u), ident[:])
-
-        def turn_query(m, h):
-            bank = turn_psum.tile([P, 2, 2, P], F32, name="bank")
-            banks["query", m, h] = bank
-            for j in range(2):
-                for u in range(2):
-                    nc.tensor.transpose(bank[:, u, j, :], words(NT + m, 2 * h + j, u), ident[:])
-
-        def empty(bank, key, half):
-            if half == 0 and key[1] == 1 and key[0] + 2 in POOLED:
+                    nc.tensor.transpose(bank[:, u, j, :], words(t, g, u), ident[:])
+            if half == 0 and key[1] == 1 and key[0] + 2 in ON_GPSIMD:
                 turned[key] = hand_pool.tile([P, PASS, 4], BF16, name="hand", align_bytes=64)
             elif half == 0:
                 turned[key] = turned_pool.tile([P, PASS, 4], BF16, name="turned_rows", align_bytes=64)
-            dst = turned[key][:, 2 * P * half : 2 * P * (half + 1), :].bitcast(F32)
-            nc.scalar.copy(out=dst, in_=bank[:].rearrange("p u j r -> p (j r) u"))
+            nc.scalar.copy(
+                out=turned[key][:, TWO * half : TWO * (half + 1), :].bitcast(F32),
+                in_=bank[:].rearrange("p u j r -> p (j r) u"),
+            )
 
-        def empty_keys(s, q):
-            empty(banks[s, q], (s, q // 2), q % 2)
+        def turn_step(s):
+            for q in range(BANKS):
+                z, half = divmod(q, 2)
+                t, g = (2 * s, q) if s in NARROW else (4 * (s // 2) + 2 * half, 2 * (s % 2) + z)
+                turn((s, z), half, [(t, g), (t + 1, g)])
 
-        def empty_query(m, h):
-            empty(banks["query", m, h], (NS + m, 0), h)
+        def turn_query(m):
+            for half in range(2):
+                turn((NS + m, 0), half, [(NT + m, 2 * half), (NT + m, 2 * half + 1)])
+
+
+        def quantize(key, out_codes, out_scales):
+            nc.vector.quantize_mx(
+                out=out_codes[:].bitcast(FP8X4),
+                scales=out_scales[:],
+                in_=turned[key][:].rearrange("p n t -> p (n t)"),
+            )
 
         def quantize_keys(s, z):
             key_codes = code_pool.tile([P, PASS], U32, name="key_codes", align_bytes=64)
             key_scales = code_pool.tile([P, PASS], U8, name="key_scales", align_bytes=64)
             codes[s, z] = (key_codes, key_scales)
-            nc.vector.quantize_mx(
-                out=key_codes[:].bitcast(FP8X4),
-                scales=key_scales[:],
-                in_=turned[s, z][:].rearrange("p n t -> p (n t)"),
-            )
+            quantize((s, z), key_codes, key_scales)
 
         def quantize_query(m):
-            nc.vector.quantize_mx(
-                out=q_codes[m][:].bitcast(FP8X4),
-                scales=q_scales[m][:],
-                in_=turned[NS + m, 0][:].rearrange("p n t -> p (n t)"),
-            )
+            quantize((NS + m, 0), q_codes[m], q_scales[m])
+
 
         def product(acc, m, g, key_codes, key_scales):
             nc.tensor.matmul_mx(
@@ -215,26 +222,26 @@ def tile_aged_key_retrieval_d3_kernel(tc, query, keys_bytes, keys_scale, age, ra
                 stop=(g == G - 1),
             )
 
-        def multiply(s, m, z0=0, z1=2):
+        def multiply(s, m, halves=(0, 1)):
             c, h = divmod(s, 2)
-            if s == NS - 1 and z0 == 0:
+            if s == NS - 1 and 0 in halves:
                 bank = turn_psum.tile([P, 2, 2, P], F32, name="bank")
-                sums["last", m] = bank[:].rearrange("p u j r -> p (u j r)")
-            elif h == 0 and z0 == 0:
-                acc = sum_psum.tile([P, 2 * UNIT], F32, name="acc")
+                sums[NG, m] = bank[:].rearrange("p u j r -> p (u j r)")
+            elif h == 0 and 0 in halves:
+                acc = sum_psum.tile([P, GROUP], F32, name="acc")
                 sums[c, m] = acc[:]
-            for z in range(z0, z1):
+            for z in halves:
                 key_codes, key_scales = codes[s, z]
-                if s not in NARROW:
+                if s in NARROW:
+                    cols = sums[NG, m][:, :TWO] if s == NS - 1 else sums[c, m][:, TWO * h : TWO * (h + 1)]
+                    for i in range(2):
+                        n = slice(TWO * i, TWO * (i + 1))
+                        product(cols, m, 2 * z + i, key_codes[:, n], key_scales[:, n])
+                else:
                     product(sums[c, m], m, 2 * h + z, key_codes[:], key_scales[:])
-                    continue
-                acc = sums["last", m][:, :UNIT] if s == NS - 1 else sums[c, m][:, UNIT * h : UNIT * (h + 1)]
-                for i in range(2):
-                    cols = slice(UNIT * i, UNIT * (i + 1))
-                    product(acc, m, 2 * z + i, key_codes[:, cols], key_scales[:, cols])
 
         def finish(acc, first, width, m):
-            c, lo = divmod(first, 2 * UNIT)
+            c, lo = divmod(first, GROUP)
             result = result_pool.tile([P, width], F32, name="scores")
             nc.vector.scalar_tensor_tensor(
                 out=result[:],
@@ -246,139 +253,90 @@ def tile_aged_key_retrieval_d3_kernel(tc, query, keys_bytes, keys_scale, age, ra
             )
             nc.sync.dma_start(out=out_view[:, m, first : first + width], in_=result[:])
 
-        def finish_pair(c, m):
-            finish(sums[c, m], 2 * UNIT * c, 2 * UNIT, m)
+        def finish_group(c, m):
+            finish(sums[c, m], GROUP * c, GROUP, m)
 
-        def finish_unit(s, m):
-            finish(sums["last" if s == NS - 1 else s // 2, m][:, :UNIT], UNIT * s, UNIT, m)
+        def finish_step(s, m):
+            finish(sums[NG - 1 + s % 2, m][:, :TWO], TWO * s, TWO, m)
 
         def warm_up(n):
-            idle_bank = sum_psum.tile([P, 512], F32, name="acc")
+            idle_bank = sum_psum.tile([P, GROUP], F32, name="acc")
             for i in range(n):
                 nc.tensor.matmul(idle_bank[:], lhsT=zeros[:, :P], rhs=zeros[:], start=True, stop=True)
 
-        def pieces(s, kinds):
-            if len(PLAN[s]) == 2:
-                every = [(2 * s + j, 0, G) for j in range(2)]
-            elif s in NARROW:
-                every = [(2 * s + j, g, g + 2) for g in (0, 2) for j in range(2)]
-            else:
-                every = [(4 * (s // 2) + j, 2 * (s % 2), 2 * (s % 2) + 2) for j in range(4)]
-            return [x for x, kind in zip(every, PLAN[s]) if kind in kinds]
-
-        def cast_step(s):
-            for x in pieces(s, "g") + pieces(s, "c"):
-                cast_tile(*x)
-
-        def widen_step(s):
-            for x in pieces(s, "cd"):
-                widen(*x)
-
         with tc.manual_schedule():
-            load_scales()
+            nc.scalar.dma_start(out=scale_rows[:NT, :], in_=keys_scale.rearrange("(t p) o -> t (p o)", p=P))
+            nc.vector.memset(scale_rows[32:64, :], 0.0)
+            nc.vector.memset(scale_rows[64:, :], 0.0)
             nc.scalar.dma_start(out=age_sb[:], in_=age.rearrange("(p i) -> p i", p=P))
-            load_key_half(0, 0)
-            load_key_half(0, 1)
+            load_first_keys(0)
+            load_first_keys(1)
             load_keys(1, 1, 1)
             load_keys(1, 0, 1)
             load_query(0)
             make_identity(nc, ident[:])
             nc.vector.memset(zeros[:], 0.0)
-            turn_scales()
+            scale_bank = turn_psum.tile([P, 2, 2, P], F32, name="bank")
+            nc.tensor.transpose(scale_bank[:, 0, 0, :], scale_rows[:], ident[:])
+            nc.vector.tensor_copy(out=scale_sb[:], in_=scale_bank[:, 0, 0, :NT])
             warm_up(3)
-            nc.scalar.activation(out=stale_sb[:], in_=age_sb[:], func=LN, bias=1.0)
-            nc.sync.dma_start(out=park.rearrange("o (p i) -> p (o i)", p=P), in_=stale_sb[:])
+            nc.scalar.activation(out=log_sb[:], in_=age_sb[:], func=LN, bias=1.0)
+            nc.sync.dma_start(out=park.rearrange("o (p i) -> p (o i)", p=P), in_=log_sb[:])
             load_query(1)
             load_keys(2)
             load_query(2)
             load_query(3)
             load_keys(3)
             nc.sync.dma_start(out=rate_sb[:], in_=rate.rearrange("(p m) -> p m", m=M))
-            load_keys(4)
-            load_stale(0)
-            load_keys(5)
-            load_stale(1)
-            load_keys(6)
-            load_stale(2)
-            load_keys(7)
-            cast_tile(1, 0, 2)
-            cast_tile(1, 2, 4)
-            widen(0, 0, 2)
-            widen(1, 0, 2)
-            widen(0, 2, 4)
-            widen(1, 2, 4)
-            cast_tile(3, 0, 4)
-            turn_keys(0, 0)
-            empty_keys(0, 0)
-            turn_keys(0, 1)
-            empty_keys(0, 1)
-            turn_keys(0, 2)
-            empty_keys(0, 2)
-            turn_keys(0, 3)
-            empty_keys(0, 3)
+            for c in range(3):
+                load_keys(HEAD + c)
+                load_stale(c)
+            load_keys(HEAD + 3)
+
+            for g in (0, 2):
+                cast_piece(1, g, g + 2)
+            for g in (0, 2):
+                scale_piece(0, g, g + 2)
+                scale_piece(1, g, g + 2)
+            cast_piece(3, 0, G)
+            turn_step(0)
             warm_up(2)
-            widen(2, 0, 4)
+            scale_piece(2, 0, G)
             part_query(0)
-            widen(3, 0, 4)
-            turn_query(0, 0)
-            empty_query(0, 0)
-            turn_query(0, 1)
-            empty_query(0, 1)
+            scale_piece(3, 0, G)
+            turn_query(0)
             part_query(1)
-            turn_keys(1, 0)
-            empty_keys(1, 0)
-            turn_keys(1, 1)
-            empty_keys(1, 1)
-            turn_keys(1, 2)
-            empty_keys(1, 2)
-            turn_keys(1, 3)
-            empty_keys(1, 3)
+            turn_step(1)
             quantize_keys(0, 0)
             quantize_keys(0, 1)
             quantize_query(0)
-            turn_query(1, 0)
-            empty_query(1, 0)
-            turn_query(1, 1)
-            empty_query(1, 1)
+            turn_query(1)
             part_query(2)
             multiply(0, 0)
             part_query(3)
             quantize_keys(1, 0)
             quantize_keys(1, 1)
+            scale_piece(4, 0, G)
             quantize_query(1)
-            cast_tile(5, 0, 4)
-            turn_query(2, 0)
-            empty_query(2, 0)
-            turn_query(2, 1)
-            empty_query(2, 1)
-            turn_query(3, 0)
-            empty_query(3, 0)
-            turn_query(3, 1)
-            empty_query(3, 1)
+            cast_piece(5, 0, G)
+            turn_query(2)
+            turn_query(3)
             multiply(1, 0)
             multiply(0, 1)
             multiply(1, 1)
-            widen(4, 0, 4)
-            widen(5, 0, 4)
+            scale_piece(5, 0, G)
             nc.scalar.activation(out=neg_rate[:], in_=rate_sb[:], func=COPY, scale=-1.0)
-            cast_tile(7, 0, 4)
+            cast_piece(7, 0, G)
             quantize_query(2)
+            scale_piece(6, 0, G)
             quantize_query(3)
-            turn_keys(2, 0)
-            empty_keys(2, 0)
-            turn_keys(2, 1)
-            empty_keys(2, 1)
-            turn_keys(2, 2)
-            empty_keys(2, 2)
-            turn_keys(2, 3)
-            empty_keys(2, 3)
-            finish_pair(0, 0)
-            finish_pair(0, 1)
+            turn_step(2)
+            finish_group(0, 0)
+            finish_group(0, 1)
             multiply(0, 2)
             multiply(0, 3)
-            cast_step(4)
-            widen(6, 0, 4)
-            widen(7, 0, 4)
+            cast_step(HEAD)
+            scale_piece(7, 0, G)
             multiply(1, 2)
             multiply(1, 3)
             quantize_keys(2, 0)
@@ -386,56 +344,38 @@ def tile_aged_key_retrieval_d3_kernel(tc, query, keys_bytes, keys_scale, age, ra
 
             for s in range(2, NS - 2):
                 c, h = divmod(s, 2)
-                if s + 6 < NS:
-                    load_keys(s + 6)
-                if h == 0 and c + 2 < NS // 2:
+                if s + LOAD_AHEAD < NS:
+                    load_keys(s + LOAD_AHEAD)
+                if h == 0 and c + 2 < NG:
                     load_stale(c + 2)
-                for q in range(4):
-                    turn_keys(s + 1, q)
-                    empty_keys(s + 1, q)
+                turn_step(s + 1)
                 if s + 3 < NS:
                     cast_step(s + 3)
                 if h == 0:
-                    for x in pieces(s + 2, "g"):
-                        scale_on_gpsimd(*x)
-                    for m in range(2 if s == 2 else 0, M):
-                        finish_pair(c - 1, m)
+                    if s + 2 in ON_GPSIMD:
+                        scale_on_gpsimd(*pieces(s + 2)[3])
+                    for m in range(2 if c == 1 else 0, M):
+                        finish_group(c - 1, m)
                 for m in range(M):
                     multiply(s, m)
-                widen_step(s + 2)
+                scale_step(s + 2)
                 quantize_keys(s + 1, 0)
                 quantize_keys(s + 1, 1)
-            turn_keys(15, 0)
-            empty_keys(15, 0)
-            turn_keys(15, 1)
-            empty_keys(15, 1)
-            turn_keys(15, 2)
-            empty_keys(15, 2)
-            turn_keys(15, 3)
-            empty_keys(15, 3)
-            finish_pair(6, 0)
-            finish_pair(6, 1)
-            finish_pair(6, 2)
-            finish_pair(6, 3)
-            multiply(14, 0)
-            multiply(14, 1)
-            multiply(14, 2)
-            multiply(14, 3)
-            quantize_keys(15, 0)
-            finish_unit(14, 0)
-            finish_unit(14, 1)
-            multiply(15, 0, 0, 1)
-            multiply(15, 1, 0, 1)
-            multiply(15, 2, 0, 1)
-            multiply(15, 3, 0, 1)
-            quantize_keys(15, 1)
-            finish_unit(14, 2)
-            finish_unit(14, 3)
-            multiply(15, 0, 1, 2)
-            finish_unit(15, 0)
-            multiply(15, 1, 1, 2)
-            finish_unit(15, 1)
-            multiply(15, 2, 1, 2)
-            finish_unit(15, 2)
-            multiply(15, 3, 1, 2)
-            finish_unit(15, 3)
+
+            last = NS - 1
+            turn_step(last)
+            for m in range(M):
+                finish_group(NG - 2, m)
+            for m in range(M):
+                multiply(last - 1, m)
+            quantize_keys(last, 0)
+            finish_step(last - 1, 0)
+            finish_step(last - 1, 1)
+            for m in range(M):
+                multiply(last, m, halves=(0,))
+            quantize_keys(last, 1)
+            finish_step(last - 1, 2)
+            finish_step(last - 1, 3)
+            for m in range(M):
+                multiply(last, m, halves=(1,))
+                finish_step(last, m)

@@ -154,7 +154,7 @@ def tile_aged_key_retrieval_d3_kernel(tc, query, keys_bytes, keys_scale, age, ra
         def cast_step(s):
             every = pieces(s)
             if s in ON_GPSIMD:
-                chosen = every[3:] + every[0 if s % 4 == 0 else 1 : 3]
+                chosen = every[3:] + every[0 if s % 4 == 2 else 1 : 3]
             else:
                 chosen = every[len(every) // 2 :]
             for piece in chosen:
@@ -179,8 +179,8 @@ def tile_aged_key_retrieval_d3_kernel(tc, query, keys_bytes, keys_scale, age, ra
             elif half == 0:
                 turned[key] = turned_pool.tile([P, PASS, 4], BF16, name="turned_rows", align_bytes=64)
             nc.scalar.copy(
-                out=turned[key][:, TWO * half : TWO * (half + 1), :].bitcast(F32),
-                in_=bank[:].rearrange("p u j r -> p (j r) u"),
+                out=turned[key][:, TWO * half : TWO * (half + 1), :].bitcast(F32).rearrange("p (n i) u -> p n u i", i=2),
+                in_=bank[:].rearrange("p u j (r i) -> p (j r) u i", i=2),
             )
 
         def turn_step(s):

@@ -33,6 +33,7 @@ BANKS = 4
 HEAD = 4
 NARROW = tuple(range(HEAD)) + (NS - 2, NS - 1)
 ON_GPSIMD = tuple(range(HEAD + 2, NS, 2))
+BEFORE_GPSIMD = tuple(s - 2 for s in ON_GPSIMD)
 LOAD_AHEAD = 6
 
 
@@ -41,14 +42,13 @@ def tile_aged_key_retrieval_d3_kernel(tc, query, keys_bytes, keys_scale, age, ra
     with ExitStack() as ctx:
         const = ctx.enter_context(tc.tile_pool(name="const", bufs=1))
         raw_pool = ctx.enter_context(tc.tile_pool(name="raw", bufs=8))
-        cast_pool = ctx.enter_context(tc.tile_pool(name="cast", bufs=8))
+        cast_pool = ctx.enter_context(tc.tile_pool(name="cast", bufs=4))
         parted_pool = ctx.enter_context(tc.tile_pool(name="parted", bufs=1))
         hand_pool = ctx.enter_context(tc.tile_pool(name="hand", bufs=1))
         turned_pool = ctx.enter_context(tc.tile_pool(name="turned", bufs=5))
         code_pool = ctx.enter_context(tc.tile_pool(name="code", bufs=7))
         result_pool = ctx.enter_context(tc.tile_pool(name="result", bufs=12))
-        turn_psum = ctx.enter_context(tc.psum_pool(name="turn", bufs=BANKS))
-        sum_psum = ctx.enter_context(tc.psum_pool(name="sum", bufs=M))
+        psum = ctx.enter_context(tc.psum_pool(name="psum", bufs=1))
 
         ident = const.tile([P, P], F32, name="ident")
         zeros = const.tile([P, GROUP], BF16, name="zeros")
@@ -64,11 +64,16 @@ def tile_aged_key_retrieval_d3_kernel(tc, query, keys_bytes, keys_scale, age, ra
         stale = [const.tile([P, GROUP], F32, name="stale_%d" % c) for c in range(NG)]
 
         key_view = keys_bytes.rearrange("(v j p) k -> v p j k", p=P, j=2)
+        group_view = keys_bytes.rearrange("(c j p) k -> c p j k", p=P, j=4)
+        step_rows = {}
         query_view = query.rearrange("(p m) k -> p m k", m=M)
         out_view = out.rearrange("(p m) n -> p m n", m=M)
         park = out[Q - 1 : Q, :]
 
         raw, cast, parted, turned, codes, sums = {}, {}, {}, {}, {}, {}
+
+        def new_bank(i):
+            return psum.tile([P, GROUP], F32, name="bank_%d" % i)
 
 
         def load_keys(v, j=0, n=2):
@@ -84,6 +89,21 @@ def tile_aged_key_retrieval_d3_kernel(tc, query, keys_bytes, keys_scale, age, ra
             for j in range(2):
                 for i in range(2):
                     raw[j, 2 * h + i] = (rows[:, j, :], i)
+
+        def load_step(s):
+            if s in NARROW:
+                load_keys(s)
+                return
+            rows = raw_pool.tile([P, 4 * K // 2], U8, name="raw_keys")
+            h = s % 2
+            nc.sync.dma_start(
+                out=rows[:].rearrange("p (j k) -> p j k", j=4),
+                in_=group_view[s // 2][:, :, K // 2 * h : K // 2 * (h + 1)],
+            )
+            step_rows[s] = rows
+            for j in range(4):
+                for i in range(2):
+                    raw[4 * (s // 2) + j, 2 * h + i] = (rows[:, K // 2 * j : K // 2 * (j + 1)], i)
 
         def load_query(m):
             nc.sync.dma_start(out=query_sb[m][:], in_=query_view[:, m, :])
@@ -105,7 +125,7 @@ def tile_aged_key_retrieval_d3_kernel(tc, query, keys_bytes, keys_scale, age, ra
             if on_gpsimd:
                 piece = hand_pool.tile(shape, BF16, name="hand", align_bytes=64)
             elif g1 - g0 == G:
-                piece = parted_pool.tile(shape, BF16, name="parted_4", bufs=8)
+                piece = parted_pool.tile(shape, BF16, name="parted_4", bufs=6)
             else:
                 piece = parted_pool.tile(shape, BF16, name="parted_2", bufs=10)
             for g in range(g0, g1):
@@ -153,6 +173,18 @@ def tile_aged_key_retrieval_d3_kernel(tc, query, keys_bytes, keys_scale, age, ra
 
         def cast_step(s):
             every = pieces(s)
+            if s not in NARROW:
+                first = 2 if s not in ON_GPSIMD else 0 if s % 4 == 2 else 1
+                end = 3 if s in ON_GPSIMD else 4
+                if s in ON_GPSIMD:
+                    cast_piece(*every[3])
+                row = cast_pool.tile([P, (end - first) * K // 2], BF16, name="cast_step", bufs=3)
+                for j in range(first, end):
+                    t, g0, g1 = every[j]
+                    for g in range(g0, g1):
+                        cast[t, g] = (row[:, K // 2 * (j - first) : K // 2 * (j - first + 1)], g - g0)
+                nc.scalar.copy(out=row[:], in_=step_rows[s][:, K // 2 * first : K // 2 * end].bitcast(FP8))
+                return
             if s in ON_GPSIMD:
                 chosen = every[3:] + every[0 if s % 4 == 2 else 1 : 3]
             else:
@@ -169,29 +201,62 @@ def tile_aged_key_retrieval_d3_kernel(tc, query, keys_bytes, keys_scale, age, ra
             piece, i = parted[t, g]
             return piece[:, u].rearrange("p a x -> p (a x)").bitcast(F32)[:, P * i : P * (i + 1)]
 
-        def turn(key, half, pairs):
-            bank = turn_psum.tile([P, 2, 2, P], F32, name="bank")
+        def turn(key, half, pairs, b):
+            bank = new_bank(b)[:].rearrange("p (u j r) -> p u j r", u=2, j=2)
             for j, (t, g) in enumerate(pairs):
                 for u in range(2):
                     nc.tensor.transpose(bank[:, u, j, :], words(t, g, u), ident[:])
-            if half == 0 and key[1] == 1 and key[0] + 2 in ON_GPSIMD:
+            if half == 0 and key[1] == 1 and key[0] in BEFORE_GPSIMD:
                 turned[key] = hand_pool.tile([P, PASS, 4], BF16, name="hand", align_bytes=64)
             elif half == 0:
                 turned[key] = turned_pool.tile([P, PASS, 4], BF16, name="turned_rows", align_bytes=64)
             nc.scalar.copy(
                 out=turned[key][:, TWO * half : TWO * (half + 1), :].bitcast(F32).rearrange("p (n i) u -> p n u i", i=2),
-                in_=bank[:].rearrange("p u j (r i) -> p (j r) u i", i=2),
+                in_=bank.rearrange("p u j (r i) -> p (j r) u i", i=2),
             )
 
-        def turn_step(s):
+        def turn_step(s, b0=0, rot=0):
             for q in range(BANKS):
                 z, half = divmod(q, 2)
                 t, g = (2 * s, q) if s in NARROW else (4 * (s // 2) + 2 * half, 2 * (s % 2) + z)
-                turn((s, z), half, [(t, g), (t + 1, g)])
+                turn((s, z), half, [(t, g), (t + 1, g)], b0 + (q + rot) % BANKS)
+
+        def turn_tile(t, b0):
+            for half in range(2):
+                turn((t, 2), half, [(t, 2 * half), (t, 2 * half + 1)], b0 + half)
+
+        def quantize_tile(t, half=None):
+            if half in (None, 0):
+                key_codes = code_pool.tile([P, PASS], U32, name="key_codes", align_bytes=64)
+                key_scales = code_pool.tile([P, PASS], U8, name="key_scales", align_bytes=64)
+                codes[t, 2] = (key_codes, key_scales)
+            key_codes, key_scales = codes[t, 2]
+            n = slice(0, PASS) if half is None else slice(TWO * half, TWO * (half + 1))
+            nc.vector.quantize_mx(
+                out=key_codes[:, n].bitcast(FP8X4),
+                scales=key_scales[:, n],
+                in_=turned[t, 2][:, n, :].rearrange("p n t -> p (n t)"),
+            )
+
+        def multiply_tile(t, m, b, g0=0, g1=G):
+            if b is None:
+                sums[t, m, 2] = sums[t - 1, m, 2][:, P:]
+            else:
+                sums[t, m, 2] = new_bank(b)[:]
+            key_codes, key_scales = codes[t, 2]
+            for g in range(g0, g1):
+                n = slice(P * g, P * (g + 1))
+                product(sums[t, m, 2][:, :P], m, g, key_codes[:, n], key_scales[:, n])
+
+        def finish_tile(t, m):
+            finish(sums[t, m, 2][:, :P], P * t, P, m)
+
+        def finish_pair(m):
+            finish(sums[NT - 2, m, 2][:, :TWO], T - TWO, TWO, m)
 
         def turn_query(m):
             for half in range(2):
-                turn((NS + m, 0), half, [(NT + m, 2 * half), (NT + m, 2 * half + 1)])
+                turn((NS + m, 0), half, [(NT + m, 2 * half), (NT + m, 2 * half + 1)], 2 * (m % 2) + half)
 
 
         def quantize(key, out_codes, out_scales):
@@ -222,14 +287,12 @@ def tile_aged_key_retrieval_d3_kernel(tc, query, keys_bytes, keys_scale, age, ra
                 stop=(g == G - 1),
             )
 
-        def multiply(s, m, halves=(0, 1)):
+        def multiply(s, m, halves=(0, 1), b0=BANKS):
             c, h = divmod(s, 2)
             if s == NS - 1 and 0 in halves:
-                bank = turn_psum.tile([P, 2, 2, P], F32, name="bank")
-                sums[NG, m] = bank[:].rearrange("p u j r -> p (u j r)")
+                sums[NG, m] = new_bank(BANKS - b0 + m)[:]
             elif h == 0 and 0 in halves:
-                acc = sum_psum.tile([P, GROUP], F32, name="acc")
-                sums[c, m] = acc[:]
+                sums[c, m] = new_bank(b0 + m)[:]
             for z in halves:
                 key_codes, key_scales = codes[s, z]
                 if s in NARROW:
@@ -260,7 +323,7 @@ def tile_aged_key_retrieval_d3_kernel(tc, query, keys_bytes, keys_scale, age, ra
             finish(sums[NG - 1 + s % 2, m][:, :TWO], TWO * s, TWO, m)
 
         def warm_up(n):
-            idle_bank = sum_psum.tile([P, GROUP], F32, name="acc")
+            idle_bank = new_bank(2 * BANKS - 1)
             for i in range(n):
                 nc.tensor.matmul(idle_bank[:], lhsT=zeros[:, :P], rhs=zeros[:], start=True, stop=True)
 
@@ -276,9 +339,9 @@ def tile_aged_key_retrieval_d3_kernel(tc, query, keys_bytes, keys_scale, age, ra
             load_query(0)
             make_identity(nc, ident[:])
             nc.vector.memset(zeros[:], 0.0)
-            scale_bank = turn_psum.tile([P, 2, 2, P], F32, name="bank")
-            nc.tensor.transpose(scale_bank[:, 0, 0, :], scale_rows[:], ident[:])
-            nc.vector.tensor_copy(out=scale_sb[:], in_=scale_bank[:, 0, 0, :NT])
+            scale_bank = new_bank(BANKS)
+            nc.tensor.transpose(scale_bank[:, :P], scale_rows[:], ident[:])
+            nc.vector.tensor_copy(out=scale_sb[:], in_=scale_bank[:, :NT])
             warm_up(3)
             nc.scalar.activation(out=log_sb[:], in_=age_sb[:], func=LN, bias=1.0)
             nc.sync.dma_start(out=park.rearrange("o (p i) -> p (o i)", p=P), in_=log_sb[:])
@@ -289,9 +352,9 @@ def tile_aged_key_retrieval_d3_kernel(tc, query, keys_bytes, keys_scale, age, ra
             load_keys(3)
             nc.sync.dma_start(out=rate_sb[:], in_=rate.rearrange("(p m) -> p m", m=M))
             for c in range(3):
-                load_keys(HEAD + c)
+                load_step(HEAD + c)
                 load_stale(c)
-            load_keys(HEAD + 3)
+            load_step(HEAD + 3)
 
             for g in (0, 2):
                 cast_piece(1, g, g + 2)
@@ -306,7 +369,7 @@ def tile_aged_key_retrieval_d3_kernel(tc, query, keys_bytes, keys_scale, age, ra
             scale_piece(3, 0, G)
             turn_query(0)
             part_query(1)
-            turn_step(1)
+            turn_step(1, rot=2)
             quantize_keys(0, 0)
             quantize_keys(0, 1)
             quantize_query(0)
@@ -316,8 +379,8 @@ def tile_aged_key_retrieval_d3_kernel(tc, query, keys_bytes, keys_scale, age, ra
             part_query(3)
             quantize_keys(1, 0)
             quantize_keys(1, 1)
-            scale_piece(4, 0, G)
             quantize_query(1)
+            scale_piece(4, 0, G)
             cast_piece(5, 0, G)
             turn_query(2)
             turn_query(3)
@@ -342,15 +405,17 @@ def tile_aged_key_retrieval_d3_kernel(tc, query, keys_bytes, keys_scale, age, ra
             quantize_keys(2, 0)
             quantize_keys(2, 1)
 
-            for s in range(2, NS - 2):
+            for s in range(2, NS - 3):
                 c, h = divmod(s, 2)
                 if s + LOAD_AHEAD < NS:
-                    load_keys(s + LOAD_AHEAD)
+                    load_step(s + LOAD_AHEAD)
                 if h == 0 and c + 2 < NG:
                     load_stale(c + 2)
                 turn_step(s + 1)
-                if s + 3 < NS:
+                if s + 3 < NS - 1:
                     cast_step(s + 3)
+                else:
+                    cast_piece(NT - 1, 0, G)
                 if h == 0:
                     if s + 2 in ON_GPSIMD:
                         scale_on_gpsimd(*pieces(s + 2)[3])
@@ -358,24 +423,46 @@ def tile_aged_key_retrieval_d3_kernel(tc, query, keys_bytes, keys_scale, age, ra
                         finish_group(c - 1, m)
                 for m in range(M):
                     multiply(s, m)
-                scale_step(s + 2)
+                if s + 2 < NS - 1:
+                    scale_step(s + 2)
+                else:
+                    scale_piece(NT - 2, 0, G)
                 quantize_keys(s + 1, 0)
                 quantize_keys(s + 1, 1)
 
-            last = NS - 1
-            turn_step(last)
-            for m in range(M):
-                finish_group(NG - 2, m)
-            for m in range(M):
-                multiply(last - 1, m)
-            quantize_keys(last, 0)
-            finish_step(last - 1, 0)
-            finish_step(last - 1, 1)
-            for m in range(M):
-                multiply(last, m, halves=(0,))
-            quantize_keys(last, 1)
-            finish_step(last - 1, 2)
-            finish_step(last - 1, 3)
-            for m in range(M):
-                multiply(last, m, halves=(1,))
-                finish_step(last, m)
+            turn_step(14)
+            multiply(13,0)
+            multiply(13,1)
+            multiply(13,2)
+            multiply(13,3)
+            scale_piece(NT - 2,0,G)
+            scale_piece(NT - 1,0,G)
+            quantize_keys(14,0)
+            finish_group(6,0)
+            quantize_keys(14,1)
+            finish_group(6,1)
+            turn_step(15)
+            finish_group(6,2)
+            finish_group(6,3)
+            multiply(14,0)
+            multiply(14,1)
+            multiply(14,2)
+            multiply(14,3)
+            quantize_keys(15,0)
+            finish_step(14,0)
+            multiply(15,0,halves=(0,))
+            multiply(15,1,halves=(0,))
+            multiply(15,2,halves=(0,))
+            multiply(15,3,halves=(0,))
+            quantize_keys(15,1)
+            finish_step(14,1)
+            finish_step(14,2)
+            finish_step(14,3)
+            multiply(15,0,halves=(1,))
+            finish_step(15,0)
+            multiply(15,1,halves=(1,))
+            finish_step(15,1)
+            multiply(15,2,halves=(1,))
+            finish_step(15,2)
+            multiply(15,3,halves=(1,))
+            finish_step(15,3)

@@ -123,7 +123,7 @@ def tile_aged_key_retrieval_d3_kernel(tc, query, keys_bytes, keys_scale, age, ra
         def new_piece(t, g0, g1, on_gpsimd=False):
             shape = [P, 2, (g1 - g0) * PASS // BLOCK, HALF]
             if on_gpsimd:
-                piece = hand_pool.tile(shape, BF16, name="hand", align_bytes=64)
+                piece = hand_pool.tile(shape, BF16, name="hand_%d" % ((t // 4 + 1) % 2))
             elif g1 - g0 == G:
                 piece = parted_pool.tile(shape, BF16, name="parted_4", bufs=6)
             else:
@@ -178,7 +178,10 @@ def tile_aged_key_retrieval_d3_kernel(tc, query, keys_bytes, keys_scale, age, ra
                 end = 3 if s in ON_GPSIMD else 4
                 if s in ON_GPSIMD:
                     cast_piece(*every[3])
-                row = cast_pool.tile([P, (end - first) * K // 2], BF16, name="cast_step", bufs=3)
+                if s + 1 in ON_GPSIMD:
+                    row = hand_pool.tile([P, (end - first) * K // 2], BF16, name="hand_%d" % (s // 2 % 2))
+                else:
+                    row = cast_pool.tile([P, (end - first) * K // 2], BF16, name="cast_step", bufs=2)
                 for j in range(first, end):
                     t, g0, g1 = every[j]
                     for g in range(g0, g1):
@@ -192,8 +195,8 @@ def tile_aged_key_retrieval_d3_kernel(tc, query, keys_bytes, keys_scale, age, ra
             for piece in chosen:
                 cast_piece(*piece)
 
-        def scale_step(s):
-            for piece in pieces(s)[: 3 if s in ON_GPSIMD else 4]:
+        def scale_step(s, lo=0, hi=4):
+            for piece in pieces(s)[: 3 if s in ON_GPSIMD else 4][lo:hi]:
                 scale_piece(*piece)
 
 
@@ -206,7 +209,7 @@ def tile_aged_key_retrieval_d3_kernel(tc, query, keys_bytes, keys_scale, age, ra
             for j, (t, g) in enumerate(pairs):
                 for u in range(2):
                     nc.tensor.transpose(bank[:, u, j, :], words(t, g, u), ident[:])
-            if half == 0 and key[1] == 1 and key[0] in BEFORE_GPSIMD:
+            if False:
                 turned[key] = hand_pool.tile([P, PASS, 4], BF16, name="hand", align_bytes=64)
             elif half == 0:
                 turned[key] = turned_pool.tile([P, PASS, 4], BF16, name="turned_rows", align_bytes=64)
@@ -423,11 +426,10 @@ def tile_aged_key_retrieval_d3_kernel(tc, query, keys_bytes, keys_scale, age, ra
                         finish_group(c - 1, m)
                 for m in range(M):
                     multiply(s, m)
-                if s + 2 < NS - 1:
-                    scale_step(s + 2)
-                else:
-                    scale_piece(NT - 2, 0, G)
+                held = 3 if s + 3 in ON_GPSIMD else 4
+                scale_step(s + 2, 0, held)
                 quantize_keys(s + 1, 0)
+                scale_step(s + 2, held, 4)
                 quantize_keys(s + 1, 1)
 
             turn_step(14)

@@ -174,7 +174,7 @@ def tile_aged_key_retrieval_d3_kernel(tc, query, keys_bytes, keys_scale, age, ra
         def cast_step(s):
             every = pieces(s)
             if s not in NARROW:
-                first = 2 if s not in ON_GPSIMD else 0 if s % 4 == 2 else 1
+                first = 2 if s not in ON_GPSIMD else 1
                 end = 3 if s in ON_GPSIMD else 4
                 if s in ON_GPSIMD:
                     cast_piece(*every[3])

@@ -257,9 +257,9 @@ def tile_aged_key_retrieval_d3_kernel(tc, query, keys_bytes, keys_scale, age, ra
         def finish_pair(m):
             finish(sums[NT - 2, m, 2][:, :TWO], T - TWO, TWO, m)
 
-        def turn_query(m):
+        def turn_query(m, b0, b1):
             for half in range(2):
-                turn((NS + m, 0), half, [(NT + m, 2 * half), (NT + m, 2 * half + 1)], 2 * (m % 2) + half)
+                turn((NS + m, 0), half, [(NT + m, 2 * half), (NT + m, 2 * half + 1)], (b0, b1)[half])
 
 
         def quantize(key, out_codes, out_scales):
@@ -306,6 +306,14 @@ def tile_aged_key_retrieval_d3_kernel(tc, query, keys_bytes, keys_scale, age, ra
                 else:
                     product(sums[c, m], m, 2 * h + z, key_codes[:], key_scales[:])
 
+        def multiply_end(z, j):
+            if z == 0:
+                sums[NG, M - 1 + j] = new_bank(M - 1 + j)[:]
+            key_codes, key_scales = codes[NS - 1, z]
+            for i in range(2):
+                n = slice(TWO * i + P * j, TWO * i + P * (j + 1))
+                product(sums[NG, M - 1 + j][:, :P], M - 1, 2 * z + i, key_codes[:, n], key_scales[:, n])
+
         def finish(acc, first, width, m):
             c, lo = divmod(first, GROUP)
             result = result_pool.tile([P, width], F32, name="scores")
@@ -321,6 +329,9 @@ def tile_aged_key_retrieval_d3_kernel(tc, query, keys_bytes, keys_scale, age, ra
 
         def finish_group(c, m):
             finish(sums[c, m], GROUP * c, GROUP, m)
+
+        def finish_end(j):
+            finish(sums[NG, M - 1 + j][:, :P], T - TWO + P * j, P, M - 1)
 
         def finish_step(s, m):
             finish(sums[NG - 1 + s % 2, m][:, :TWO], TWO * s, TWO, m)
@@ -359,54 +370,57 @@ def tile_aged_key_retrieval_d3_kernel(tc, query, keys_bytes, keys_scale, age, ra
                 load_stale(c)
             load_step(HEAD + 3)
 
-            for g in (0, 2):
-                cast_piece(1, g, g + 2)
-            for g in (0, 2):
-                scale_piece(0, g, g + 2)
-                scale_piece(1, g, g + 2)
-            cast_piece(3, 0, G)
+            cast_piece(1,0,2)
+            cast_piece(1,2,4)
+            scale_piece(0,0,2)
+            scale_piece(1,0,2)
+            scale_piece(0,2,4)
+            scale_piece(1,2,4)
+            cast_piece(3,0,G)
             turn_step(0)
             warm_up(2)
-            scale_piece(2, 0, G)
+            scale_piece(2,0,G)
             part_query(0)
-            scale_piece(3, 0, G)
-            turn_query(0)
+            scale_piece(3,0,G)
+            turn_query(0,5,6)
             part_query(1)
-            turn_step(1, rot=2)
-            quantize_keys(0, 0)
-            quantize_keys(0, 1)
+            turn_step(1)
+            quantize_keys(0,0)
+            quantize_keys(0,1)
             quantize_query(0)
-            turn_query(1)
+            turn_query(1,7,5)
             part_query(2)
-            multiply(0, 0)
+            multiply(0,0)
             part_query(3)
-            quantize_keys(1, 0)
-            quantize_keys(1, 1)
+            quantize_keys(1,0)
+            quantize_keys(1,1)
+            scale_piece(4,0,2)
             quantize_query(1)
-            scale_piece(4, 0, G)
-            cast_piece(5, 0, G)
-            turn_query(2)
-            turn_query(3)
-            multiply(1, 0)
-            multiply(0, 1)
-            multiply(1, 1)
-            scale_piece(5, 0, G)
+            scale_piece(4,2,4)
+            cast_piece(5,0,G)
+            turn_query(2,0,1)
+            turn_query(3,2,3)
+            multiply(1,0)
+            multiply(0,1)
+            multiply(1,1)
+            scale_piece(5,0,G)
             nc.scalar.activation(out=neg_rate[:], in_=rate_sb[:], func=COPY, scale=-1.0)
-            cast_piece(7, 0, G)
+            cast_piece(7,0,G)
             quantize_query(2)
-            scale_piece(6, 0, G)
+            scale_piece(6,0,2)
             quantize_query(3)
+            scale_piece(6,2,4)
             turn_step(2)
-            finish_group(0, 0)
-            finish_group(0, 1)
-            multiply(0, 2)
-            multiply(0, 3)
+            scale_piece(7,0,G)
+            finish_group(0,0)
+            finish_group(0,1)
+            multiply(0,2)
+            multiply(1,2)
             cast_step(HEAD)
-            scale_piece(7, 0, G)
-            multiply(1, 2)
-            multiply(1, 3)
-            quantize_keys(2, 0)
-            quantize_keys(2, 1)
+            multiply(0,3)
+            multiply(1,3)
+            quantize_keys(2,0)
+            quantize_keys(2,1)
 
             for s in range(2, NS - 3):
                 c, h = divmod(s, 2)
@@ -454,8 +468,6 @@ def tile_aged_key_retrieval_d3_kernel(tc, query, keys_bytes, keys_scale, age, ra
             finish_step(14,0)
             multiply(15,0,halves=(0,))
             multiply(15,1,halves=(0,))
-            multiply(15,2,halves=(0,))
-            multiply(15,3,halves=(0,))
             quantize_keys(15,1)
             finish_step(14,1)
             finish_step(14,2)
@@ -464,7 +476,11 @@ def tile_aged_key_retrieval_d3_kernel(tc, query, keys_bytes, keys_scale, age, ra
             finish_step(15,0)
             multiply(15,1,halves=(1,))
             finish_step(15,1)
-            multiply(15,2,halves=(1,))
+            multiply(15,2)
             finish_step(15,2)
-            multiply(15,3,halves=(1,))
-            finish_step(15,3)
+            multiply_end(0,0)
+            multiply_end(1,0)
+            finish_end(0)
+            multiply_end(0,1)
+            multiply_end(1,1)
+            finish_end(1)

@@ -18,32 +18,31 @@ COPY = mybir.ActivationFunctionType.Copy
 LN = mybir.ActivationFunctionType.Ln
 
 P = 128
+QUAD = 32
 PASS = 512
 G = K // PASS
 M = Q // P
 BLOCK = 32
 HALF = BLOCK // 2
+NB = K // BLOCK
+PB = PASS // BLOCK
 NT = T // P
 GROUP = 4 * P
 TWO = 2 * P
 NG = T // GROUP
-NS = NT // 2
-BANKS = 4
-
-HEAD = 4
-NARROW = tuple(range(HEAD)) + (NS - 2, NS - 1)
-ON_GPSIMD = tuple(range(HEAD + 2, NS, 2))
-BEFORE_GPSIMD = tuple(s - 2 for s in ON_GPSIMD)
-LOAD_AHEAD = 6
+BANKS = 8
+RAW_BUFS = 3
+DIRECT = 20
+ON_GPSIMD = 40
 
 
 def tile_aged_key_retrieval_d3_kernel(tc, query, keys_bytes, keys_scale, age, rate, out):
     nc = tc.nc
     with ExitStack() as ctx:
         const = ctx.enter_context(tc.tile_pool(name="const", bufs=1))
-        raw_pool = ctx.enter_context(tc.tile_pool(name="raw", bufs=8))
-        cast_pool = ctx.enter_context(tc.tile_pool(name="cast", bufs=4))
-        parted_pool = ctx.enter_context(tc.tile_pool(name="parted", bufs=1))
+        raw_pool = ctx.enter_context(tc.tile_pool(name="raw", bufs=4))
+        cast_pool = ctx.enter_context(tc.tile_pool(name="cast", bufs=2))
+        parted_pool = ctx.enter_context(tc.tile_pool(name="parted", bufs=2))
         hand_pool = ctx.enter_context(tc.tile_pool(name="hand", bufs=1))
         turned_pool = ctx.enter_context(tc.tile_pool(name="turned", bufs=5))
         code_pool = ctx.enter_context(tc.tile_pool(name="code", bufs=7))
@@ -51,9 +50,8 @@ def tile_aged_key_retrieval_d3_kernel(tc, query, keys_bytes, keys_scale, age, ra
         psum = ctx.enter_context(tc.psum_pool(name="psum", bufs=1))
 
         ident = const.tile([P, P], F32, name="ident")
-        zeros = const.tile([P, GROUP], BF16, name="zeros")
-        scale_rows = const.tile([P, P], F32, name="scale_rows")
-        scale_sb = const.tile([P, NT], F32, name="scale_sb")
+        scale_rows = const.tile([P, QUAD], F32, name="scale_rows", align_bytes=64)
+        scale_sb = const.tile([P, NT], F32, name="scale_sb", align_bytes=64)
         age_sb = const.tile([P, T // P], BF16, name="age_sb")
         log_sb = const.tile([P, T // P], F32, name="log_sb")
         rate_sb = const.tile([P, M], BF16, name="rate_sb")
@@ -63,9 +61,8 @@ def tile_aged_key_retrieval_d3_kernel(tc, query, keys_bytes, keys_scale, age, ra
         q_scales = [const.tile([P, G * P], U8, name="q_scales_%d" % m, align_bytes=64) for m in range(M)]
         stale = [const.tile([P, GROUP], F32, name="stale_%d" % c) for c in range(NG)]
 
-        key_view = keys_bytes.rearrange("(v j p) k -> v p j k", p=P, j=2)
-        group_view = keys_bytes.rearrange("(c j p) k -> c p j k", p=P, j=4)
-        step_rows = {}
+        key_view = keys_bytes.rearrange("(t p) k -> p t k", p=P)
+        scale_view = keys_scale.rearrange("(t q i) o -> q t (i o)", q=P // QUAD, i=QUAD)
         query_view = query.rearrange("(p m) k -> p m k", m=M)
         out_view = out.rearrange("(p m) n -> p m n", m=M)
         park = out[Q - 1 : Q, :]
@@ -73,37 +70,17 @@ def tile_aged_key_retrieval_d3_kernel(tc, query, keys_bytes, keys_scale, age, ra
         raw, cast, parted, turned, codes, sums = {}, {}, {}, {}, {}, {}
 
         def new_bank(i):
-            return psum.tile([P, GROUP], F32, name="bank_%d" % i)
+            return psum.tile([P, GROUP], F32, name="bank_%d" % (i % BANKS))
 
 
-        def load_keys(v, j=0, n=2):
-            rows = raw_pool.tile([P, n, K], U8, name="raw_keys")
-            nc.sync.dma_start(out=rows[:], in_=key_view[v][:, j : j + n, :])
-            for i in range(n):
-                for g in range(G):
-                    raw[2 * v + j + i, g] = (rows[:, i, :], g)
-
-        def load_first_keys(h):
-            rows = raw_pool.tile([P, 2, K // 2], U8, name="raw_keys")
-            nc.sync.dma_start(out=rows[:], in_=key_view[0][:, :, K // 2 * h : K // 2 * (h + 1)])
-            for j in range(2):
-                for i in range(2):
-                    raw[j, 2 * h + i] = (rows[:, j, :], i)
-
-        def load_step(s):
-            if s in NARROW:
-                load_keys(s)
-                return
-            rows = raw_pool.tile([P, 4 * K // 2], U8, name="raw_keys")
-            h = s % 2
+        def load_keys(t, n, g0=0, g1=G, tag="raw_keys", bufs=None):
+            width = PASS * (g1 - g0)
+            rows = raw_pool.tile([P, n * width], U8, name=tag, bufs=bufs)
             nc.sync.dma_start(
-                out=rows[:].rearrange("p (j k) -> p j k", j=4),
-                in_=group_view[s // 2][:, :, K // 2 * h : K // 2 * (h + 1)],
+                out=rows[:].rearrange("p (j k) -> p j k", j=n), in_=key_view[:, t : t + n, PASS * g0 : PASS * g1]
             )
-            step_rows[s] = rows
-            for j in range(4):
-                for i in range(2):
-                    raw[4 * (s // 2) + j, 2 * h + i] = (rows[:, K // 2 * j : K // 2 * (j + 1)], i)
+            for j in range(n):
+                raw.setdefault(t + j, []).append((PB * g0, PB * g1, rows, width * j))
 
         def load_query(m):
             nc.sync.dma_start(out=query_sb[m][:], in_=query_view[:, m, :])
@@ -111,47 +88,57 @@ def tile_aged_key_retrieval_d3_kernel(tc, query, keys_bytes, keys_scale, age, ra
         def load_stale(c):
             nc.sync.dma_start(out=stale[c][:], in_=park[0, GROUP * c : GROUP * (c + 1)].partition_broadcast(P))
 
+        def find(table, t, a0):
+            for first, end, row, at in table.get(t, []):
+                if first <= a0 < end:
+                    return row, at + BLOCK * (a0 - first)
+            return None
 
-        def key_bytes(t, g0, g1):
-            row, i = raw[t, g0]
-            return row[:, PASS * i : PASS * (i + g1 - g0)].bitcast(FP8)
+        def cast_run(t, a0, n, tag, pool=cast_pool):
+            row, at = find(raw, t, a0)
+            values = pool.tile([P, BLOCK * n], BF16, name=tag)
+            nc.scalar.copy(out=values[:], in_=row[:, at : at + BLOCK * n].bitcast(FP8))
+            done = 0
+            while done < n:
+                end = min(NB, a0 + n - done)
+                cast.setdefault(t, []).append((a0, end, values, BLOCK * done))
+                done = done + end - a0
+                t, a0 = t + 1, 0
 
-        def cast_values(t, g0, g1):
-            row, i = cast[t, g0]
-            return row[:, PASS * i : PASS * (i + g1 - g0)]
-
-        def new_piece(t, g0, g1, on_gpsimd=False):
-            shape = [P, 2, (g1 - g0) * PASS // BLOCK, HALF]
-            if on_gpsimd:
-                piece = hand_pool.tile(shape, BF16, name="hand_%d" % ((t // 4 + 1) % 2))
-            elif g1 - g0 == G:
-                piece = parted_pool.tile(shape, BF16, name="parted_4", bufs=6)
-            else:
-                piece = parted_pool.tile(shape, BF16, name="parted_2", bufs=10)
+        def new_piece(t, g0, g1, tag, pool=parted_pool, bufs=None):
+            piece = pool.tile([P, 2, PB * (g1 - g0), HALF], BF16, name=tag, bufs=bufs)
             for g in range(g0, g1):
                 parted[t, g] = (piece, g - g0)
-            return piece[:]
 
-        def cast_piece(t, g0, g1):
-            row = cast_pool.tile([P, PASS * (g1 - g0)], BF16, name="cast_row")
-            for g in range(g0, g1):
-                cast[t, g] = (row, g - g0)
-            nc.scalar.copy(out=row[:], in_=key_bytes(t, g0, g1))
+        def piece_blocks(t, a0, a1):
+            piece, i = parted[t, a0 // PB]
+            lo = PB * i + a0 % PB
+            return piece[:, :, lo : lo + a1 - a0, :]
 
-        def scale_piece(t, g0, g1):
-            values = cast_values(t, g0, g1) if (t, g0) in cast else key_bytes(t, g0, g1)
+        def scale(t, a0, a1):
+            if find(cast, t, a0) is None:
+                row, at = find(raw, t, a0)
+                values = row[:, at : at + BLOCK * (a1 - a0)].bitcast(FP8)
+            else:
+                row, at = find(cast, t, a0)
+                values = row[:, at : at + BLOCK * (a1 - a0)]
             nc.vector.tensor_scalar(
-                out=new_piece(t, g0, g1).rearrange("p u a x -> p a u x"),
+                out=piece_blocks(t, a0, a1).rearrange("p u a x -> p a u x"),
                 in0=values.rearrange("p (a u x) -> p a u x", u=2, x=HALF),
                 scalar1=scale_sb[:, t : t + 1],
                 scalar2=None,
                 op0=MULT,
             )
 
-        def scale_on_gpsimd(t, g0, g1):
+        def scale_piece(t, g0, g1, tag, bufs=None):
+            new_piece(t, g0, g1, tag, bufs=bufs)
+            scale(t, PB * g0, PB * g1)
+
+        def scale_on_gpsimd(t, a1):
+            row, at = find(cast, t, 0)
             nc.gpsimd.tensor_scalar(
-                out=new_piece(t, g0, g1, on_gpsimd=True),
-                in0=cast_values(t, g0, g1).rearrange("p (a u x) -> p u a x", u=2, x=HALF),
+                out=piece_blocks(t, 0, a1),
+                in0=row[:, at : at + BLOCK * a1].rearrange("p (a u x) -> p u a x", u=2, x=HALF),
                 scalar1=scale_sb[:, t : t + 1],
                 scalar2=0.0,
                 op0=MULT,
@@ -159,108 +146,38 @@ def tile_aged_key_retrieval_d3_kernel(tc, query, keys_bytes, keys_scale, age, ra
             )
 
         def part_query(m):
+            new_piece(NT + m, 0, G, "parted_query")
             nc.vector.tensor_copy(
-                out=new_piece(NT + m, 0, G).rearrange("p u a x -> p a u x"),
+                out=piece_blocks(NT + m, 0, NB).rearrange("p u a x -> p a u x"),
                 in_=query_sb[m][:].rearrange("p (a u x) -> p a u x", u=2, x=HALF),
             )
-
-        def pieces(s):
-            if s == NS - 1:
-                return [(2 * s + j, 0, G) for j in range(2)]
-            if s in NARROW:
-                return [(2 * s + j, g, g + 2) for g in (0, 2) for j in range(2)]
-            return [(4 * (s // 2) + j, 2 * (s % 2), 2 * (s % 2) + 2) for j in range(4)]
-
-        def cast_step(s):
-            every = pieces(s)
-            if s not in NARROW:
-                first = 2 if s not in ON_GPSIMD else 1
-                end = 3 if s in ON_GPSIMD else 4
-                if s in ON_GPSIMD:
-                    cast_piece(*every[3])
-                if s + 1 in ON_GPSIMD:
-                    row = hand_pool.tile([P, (end - first) * K // 2], BF16, name="hand_%d" % (s // 2 % 2))
-                else:
-                    row = cast_pool.tile([P, (end - first) * K // 2], BF16, name="cast_step", bufs=2)
-                for j in range(first, end):
-                    t, g0, g1 = every[j]
-                    for g in range(g0, g1):
-                        cast[t, g] = (row[:, K // 2 * (j - first) : K // 2 * (j - first + 1)], g - g0)
-                nc.scalar.copy(out=row[:], in_=step_rows[s][:, K // 2 * first : K // 2 * end].bitcast(FP8))
-                return
-            if s in ON_GPSIMD:
-                chosen = every[3:] + every[0 if s % 4 == 2 else 1 : 3]
-            else:
-                chosen = every[len(every) // 2 :]
-            for piece in chosen:
-                cast_piece(*piece)
-
-        def scale_step(s, lo=0, hi=4):
-            for piece in pieces(s)[: 3 if s in ON_GPSIMD else 4][lo:hi]:
-                scale_piece(*piece)
-
 
         def words(t, g, u):
             piece, i = parted[t, g]
             return piece[:, u].rearrange("p a x -> p (a x)").bitcast(F32)[:, P * i : P * (i + 1)]
 
-        def turn(key, half, pairs, b):
+        def turn(key, half, pairs, b, copy=nc.scalar.copy):
             bank = new_bank(b)[:].rearrange("p (u j r) -> p u j r", u=2, j=2)
             for j, (t, g) in enumerate(pairs):
                 for u in range(2):
                     nc.tensor.transpose(bank[:, u, j, :], words(t, g, u), ident[:])
-            if False:
-                turned[key] = hand_pool.tile([P, PASS, 4], BF16, name="hand", align_bytes=64)
-            elif half == 0:
+            if key not in turned:
                 turned[key] = turned_pool.tile([P, PASS, 4], BF16, name="turned_rows", align_bytes=64)
-            nc.scalar.copy(
+            copy(
                 out=turned[key][:, TWO * half : TWO * (half + 1), :].bitcast(F32).rearrange("p (n i) u -> p n u i", i=2),
                 in_=bank.rearrange("p u j (r i) -> p (j r) u i", i=2),
             )
 
-        def turn_step(s, b0=0, rot=0):
-            for q in range(BANKS):
-                z, half = divmod(q, 2)
-                t, g = (2 * s, q) if s in NARROW else (4 * (s // 2) + 2 * half, 2 * (s % 2) + z)
-                turn((s, z), half, [(t, g), (t + 1, g)], b0 + (q + rot) % BANKS)
+        def turn_wide(c, g, half, b):
+            t = 4 * c + 2 * half
+            turn(("wide", c, g), half, [(t, g), (t + 1, g)], b)
 
-        def turn_tile(t, b0):
-            for half in range(2):
-                turn((t, 2), half, [(t, 2 * half), (t, 2 * half + 1)], b0 + half)
-
-        def quantize_tile(t, half=None):
-            if half in (None, 0):
-                key_codes = code_pool.tile([P, PASS], U32, name="key_codes", align_bytes=64)
-                key_scales = code_pool.tile([P, PASS], U8, name="key_scales", align_bytes=64)
-                codes[t, 2] = (key_codes, key_scales)
-            key_codes, key_scales = codes[t, 2]
-            n = slice(0, PASS) if half is None else slice(TWO * half, TWO * (half + 1))
-            nc.vector.quantize_mx(
-                out=key_codes[:, n].bitcast(FP8X4),
-                scales=key_scales[:, n],
-                in_=turned[t, 2][:, n, :].rearrange("p n t -> p (n t)"),
-            )
-
-        def multiply_tile(t, m, b, g0=0, g1=G):
-            if b is None:
-                sums[t, m, 2] = sums[t - 1, m, 2][:, P:]
-            else:
-                sums[t, m, 2] = new_bank(b)[:]
-            key_codes, key_scales = codes[t, 2]
-            for g in range(g0, g1):
-                n = slice(P * g, P * (g + 1))
-                product(sums[t, m, 2][:, :P], m, g, key_codes[:, n], key_scales[:, n])
-
-        def finish_tile(t, m):
-            finish(sums[t, m, 2][:, :P], P * t, P, m)
-
-        def finish_pair(m):
-            finish(sums[NT - 2, m, 2][:, :TWO], T - TWO, TWO, m)
+        def turn_pair(v, g, b, copy=nc.scalar.copy):
+            turn(("pair", v, g // 2), g % 2, [(2 * v, g), (2 * v + 1, g)], b, copy)
 
         def turn_query(m, b0, b1):
-            for half in range(2):
-                turn((NS + m, 0), half, [(NT + m, 2 * half), (NT + m, 2 * half + 1)], (b0, b1)[half])
-
+            for half, b in enumerate((b0, b1)):
+                turn(("query", m), half, [(NT + m, 2 * half), (NT + m, 2 * half + 1)], b)
 
         def quantize(key, out_codes, out_scales):
             nc.vector.quantize_mx(
@@ -269,15 +186,14 @@ def tile_aged_key_retrieval_d3_kernel(tc, query, keys_bytes, keys_scale, age, ra
                 in_=turned[key][:].rearrange("p n t -> p (n t)"),
             )
 
-        def quantize_keys(s, z):
+        def quantize_keys(*key):
             key_codes = code_pool.tile([P, PASS], U32, name="key_codes", align_bytes=64)
             key_scales = code_pool.tile([P, PASS], U8, name="key_scales", align_bytes=64)
-            codes[s, z] = (key_codes, key_scales)
-            quantize((s, z), key_codes, key_scales)
+            codes[key] = (key_codes, key_scales)
+            quantize(key, key_codes, key_scales)
 
         def quantize_query(m):
-            quantize((NS + m, 0), q_codes[m], q_scales[m])
-
+            quantize(("query", m), q_codes[m], q_scales[m])
 
         def product(acc, m, g, key_codes, key_scales):
             nc.tensor.matmul_mx(
@@ -290,29 +206,18 @@ def tile_aged_key_retrieval_d3_kernel(tc, query, keys_bytes, keys_scale, age, ra
                 stop=(g == G - 1),
             )
 
-        def multiply(s, m, halves=(0, 1), b0=BANKS):
-            c, h = divmod(s, 2)
-            if s == NS - 1 and 0 in halves:
-                sums[NG, m] = new_bank(BANKS - b0 + m)[:]
-            elif h == 0 and 0 in halves:
-                sums[c, m] = new_bank(b0 + m)[:]
-            for z in halves:
-                key_codes, key_scales = codes[s, z]
-                if s in NARROW:
-                    cols = sums[NG, m][:, :TWO] if s == NS - 1 else sums[c, m][:, TWO * h : TWO * (h + 1)]
-                    for i in range(2):
-                        n = slice(TWO * i, TWO * (i + 1))
-                        product(cols, m, 2 * z + i, key_codes[:, n], key_scales[:, n])
-                else:
-                    product(sums[c, m], m, 2 * h + z, key_codes[:], key_scales[:])
+        def multiply_wide(c, g, m, b=None):
+            if b is not None:
+                sums[c, m] = new_bank(b)[:]
+            key_codes, key_scales = codes["wide", c, g]
+            product(sums[c, m], m, g, key_codes[:], key_scales[:])
 
-        def multiply_end(z, j):
-            if z == 0:
-                sums[NG, M - 1 + j] = new_bank(M - 1 + j)[:]
-            key_codes, key_scales = codes[NS - 1, z]
-            for i in range(2):
-                n = slice(TWO * i + P * j, TWO * i + P * (j + 1))
-                product(sums[NG, M - 1 + j][:, :P], M - 1, 2 * z + i, key_codes[:, n], key_scales[:, n])
+        def multiply_pair(v, m, acc, halves=(0, 1), lo=0, hi=TWO):
+            for z in halves:
+                key_codes, key_scales = codes["pair", v, z]
+                for i in range(2):
+                    n = slice(TWO * i + lo, TWO * i + hi)
+                    product(acc, m, 2 * z + i, key_codes[:, n], key_scales[:, n])
 
         def finish(acc, first, width, m):
             c, lo = divmod(first, GROUP)
@@ -330,157 +235,166 @@ def tile_aged_key_retrieval_d3_kernel(tc, query, keys_bytes, keys_scale, age, ra
         def finish_group(c, m):
             finish(sums[c, m], GROUP * c, GROUP, m)
 
-        def finish_end(j):
-            finish(sums[NG, M - 1 + j][:, :P], T - TWO + P * j, P, M - 1)
-
-        def finish_step(s, m):
-            finish(sums[NG - 1 + s % 2, m][:, :TWO], TWO * s, TWO, m)
-
-        def warm_up(n):
-            idle_bank = new_bank(2 * BANKS - 1)
+        def warm_up(n, b):
+            idle_bank = new_bank(b)
             for i in range(n):
-                nc.tensor.matmul(idle_bank[:], lhsT=zeros[:, :P], rhs=zeros[:], start=True, stop=True)
+                nc.tensor.matmul(idle_bank[:, :P], lhsT=ident[:], rhs=ident[:], start=True, stop=True)
+
+        def load_group(c):
+            load_keys(4 * c, 4, tag="raw_group", bufs=RAW_BUFS)
+
+        def hand(c):
+            return "hand_%d" % (c % 3)
 
         with tc.manual_schedule():
-            nc.scalar.dma_start(out=scale_rows[:NT, :], in_=keys_scale.rearrange("(t p) o -> t (p o)", p=P))
-            nc.vector.memset(scale_rows[32:64, :], 0.0)
-            nc.vector.memset(scale_rows[64:, :], 0.0)
+            for q in range(P // QUAD):
+                nc.scalar.dma_start(out=scale_rows[QUAD * q : QUAD * (q + 1), :], in_=scale_view[q])
             nc.scalar.dma_start(out=age_sb[:], in_=age.rearrange("(p i) -> p i", p=P))
-            load_first_keys(0)
-            load_first_keys(1)
-            load_keys(1, 1, 1)
-            load_keys(1, 0, 1)
+            load_keys(0, 2, 0, 2)
+            load_keys(0, 2, 2, 4)
+            load_keys(3, 1)
+            load_keys(2, 1)
             load_query(0)
-            make_identity(nc, ident[:])
-            nc.vector.memset(zeros[:], 0.0)
-            scale_bank = new_bank(BANKS)
-            nc.tensor.transpose(scale_bank[:, :P], scale_rows[:], ident[:])
-            nc.vector.tensor_copy(out=scale_sb[:], in_=scale_bank[:, :NT])
-            warm_up(3)
-            nc.scalar.activation(out=log_sb[:], in_=age_sb[:], func=LN, bias=1.0)
-            nc.sync.dma_start(out=park.rearrange("o (p i) -> p (o i)", p=P), in_=log_sb[:])
             load_query(1)
-            load_keys(2)
+            make_identity(nc, ident[:])
+            warm_up(4, 7)
+            nc.vector.transpose(scale_sb[:], scale_rows[:])
+            nc.scalar.activation(out=log_sb[:], in_=age_sb[:], func=LN, bias=1.0)
             load_query(2)
             load_query(3)
-            load_keys(3)
+            nc.sync.dma_start(out=park.rearrange("o (p i) -> p (o i)", p=P), in_=log_sb[:])
+            load_group(1)
             nc.sync.dma_start(out=rate_sb[:], in_=rate.rearrange("(p m) -> p m", m=M))
-            for c in range(3):
-                load_step(HEAD + c)
-                load_stale(c)
-            load_step(HEAD + 3)
+            load_group(2)
+            load_stale(0)
+            load_stale(1)
+            load_group(3)
 
-            cast_piece(1,0,2)
-            cast_piece(1,2,4)
-            scale_piece(0,0,2)
-            scale_piece(1,0,2)
-            scale_piece(0,2,4)
-            scale_piece(1,2,4)
-            cast_piece(3,0,G)
-            turn_step(0)
-            warm_up(2)
-            scale_piece(2,0,G)
+            cast_run(1, 0, NB // 2, "cast_gpsimd")
+            cast_run(1, NB // 2, NB // 2, "cast_gpsimd")
+            scale_piece(0, 0, 2, "parted_2")
+            scale_piece(0, 2, 4, "parted_0b")
+            scale_piece(1, 0, 2, "parted_3")
+            scale_piece(1, 2, 4, "parted_0b")
+            cast_run(3, 0, NB, "cast_last")
+            for g in range(G):
+                turn_pair(0, g, g)
+            warm_up(2, 7)
+            scale_piece(2, 0, G, "parted_2")
             part_query(0)
-            scale_piece(3,0,G)
-            turn_query(0,5,6)
+            scale_piece(3, 0, G, "parted_3")
+            turn_query(0, 4, 5)
             part_query(1)
-            turn_step(1)
-            quantize_keys(0,0)
-            quantize_keys(0,1)
+            turn_pair(1, 0, 0)
+            turn_pair(1, 1, 1)
+            turn_query(1, 6, 7)
+            turn_pair(1, 2, 2)
+            turn_pair(1, 3, 3)
+            quantize_keys("pair", 0, 0)
+            quantize_keys("pair", 0, 1)
             quantize_query(0)
-            turn_query(1,7,5)
             part_query(2)
-            multiply(0,0)
+            quantize_keys("pair", 1, 0)
             part_query(3)
-            quantize_keys(1,0)
-            quantize_keys(1,1)
-            scale_piece(4,0,2)
             quantize_query(1)
-            scale_piece(4,2,4)
-            cast_piece(5,0,G)
-            turn_query(2,0,1)
-            turn_query(3,2,3)
-            multiply(1,0)
-            multiply(0,1)
-            multiply(1,1)
-            scale_piece(5,0,G)
-            nc.scalar.activation(out=neg_rate[:], in_=rate_sb[:], func=COPY, scale=-1.0)
-            cast_piece(7,0,G)
+            sums[0, 0] = new_bank(4)[:]
+            multiply_pair(0, 0, sums[0, 0][:, :TWO])
+            turn_query(2, 0, 1)
+            turn_query(3, 6, 7)
+            sums[0, 1] = new_bank(5)[:]
+            multiply_pair(0, 1, sums[0, 1][:, :TWO])
+            scale_piece(4, 0, 1, "parted_0a")
+            quantize_keys("pair", 1, 1)
+            new_piece(5, 0, G, hand(0), pool=hand_pool)
+            scale(5, 0, NB // 2)
             quantize_query(2)
-            scale_piece(6,0,2)
+            scale(5, NB // 2, NB)
             quantize_query(3)
-            scale_piece(6,2,4)
-            turn_step(2)
-            scale_piece(7,0,G)
-            finish_group(0,0)
-            finish_group(0,1)
-            multiply(0,2)
-            multiply(1,2)
-            cast_step(HEAD)
-            multiply(0,3)
-            multiply(1,3)
-            quantize_keys(2,0)
-            quantize_keys(2,1)
+            multiply_pair(1, 0, sums[0, 0][:, TWO:])
+            multiply_pair(1, 1, sums[0, 1][:, TWO:])
+            cast_run(6, 0, NB, "cast_last")
+            cast_run(7, 0, NB, hand(1), pool=hand_pool)
+            nc.scalar.activation(out=neg_rate[:], in_=rate_sb[:], func=COPY, scale=-1.0)
+            turn_wide(1, 0, 0, 2)
+            cast_run(9, 0, ON_GPSIMD, "cast_gpsimd")
+            cast_run(9, ON_GPSIMD, 2 * NB - ON_GPSIMD - DIRECT, hand(2), pool=hand_pool)
+            scale_piece(4, 1, G, "parted_0b")
+            for m in (2, 3):
+                sums[0, m] = new_bank(m - 2)[:]
+                multiply_pair(0, m, sums[0, m][:, :TWO])
+                multiply_pair(1, m, sums[0, m][:, TWO:])
+            scale_piece(8, 0, 1, "parted_0a")
+            scale_piece(6, 0, G, "parted_2")
+            scale_piece(7, 0, G, "parted_3")
+            ring = [3, 6, 7, 2, 4, 5, 0, 1]
 
-            for s in range(2, NS - 3):
-                c, h = divmod(s, 2)
-                if s + LOAD_AHEAD < NS:
-                    load_step(s + LOAD_AHEAD)
-                if h == 0 and c + 2 < NG:
-                    load_stale(c + 2)
-                turn_step(s + 1)
-                if s + 3 < NS - 1:
-                    cast_step(s + 3)
-                else:
-                    cast_piece(NT - 1, 0, G)
-                if h == 0:
-                    if s + 2 in ON_GPSIMD:
-                        scale_on_gpsimd(*pieces(s + 2)[3])
-                    for m in range(2 if c == 1 else 0, M):
-                        finish_group(c - 1, m)
+            for c in range(1, NG - 1):
+                t = 4 * (c + 1)
+                if c + 3 < NG:
+                    load_group(c + 3)
+                load_stale(c + 1)
+                new_piece(t + 1, 0, G, hand(c), pool=hand_pool)
+                scale_on_gpsimd(t + 1, ON_GPSIMD)
                 for m in range(M):
-                    multiply(s, m)
-                held = 3 if s + 3 in ON_GPSIMD else 4
-                scale_step(s + 2, 0, held)
-                quantize_keys(s + 1, 0)
-                scale_step(s + 2, held, 4)
-                quantize_keys(s + 1, 1)
+                    finish_group(c - 1, m)
+                turn_wide(c, 0, 1, ring[0])
+                for g in range(1, G):
+                    for half in range(2):
+                        turn_wide(c, g, half, ring[2 * g - 1 + half])
+                cast_run(t + 3, 0, NB, "cast_last")
+                if c + 2 < NG:
+                    cast_run(t + 5, 0, ON_GPSIMD, "cast_gpsimd")
+                if c + 1 < NG - 1:
+                    turn_wide(c + 1, 0, 0, ring[7])
+                else:
+                    turn_pair(NT // 2 - 2, 0, ring[7])
+                if c + 2 < NG:
+                    cast_run(t + 5, ON_GPSIMD, 2 * NB - ON_GPSIMD - DIRECT, hand(c + 2), pool=hand_pool)
+                quantize_keys("wide", c, 0)
+                for m in range(M):
+                    multiply_wide(c, 0, m, ring[m])
+                new_piece(t + 2, 0, G, "parted_2")
+                scale(t + 2, 0, NB - DIRECT)
+                if c + 2 < NG:
+                    scale_piece(t + 4, 0, 1, "parted_0a")
+                quantize_keys("wide", c, 1)
+                for m in range(M):
+                    multiply_wide(c, 1, m)
+                scale(t + 2, NB - DIRECT, NB)
+                quantize_keys("wide", c, 2)
+                for m in range(M):
+                    multiply_wide(c, 2, m)
+                scale_piece(t, 1, G, "parted_0b")
+                quantize_keys("wide", c, 3)
+                for m in range(M):
+                    multiply_wide(c, 3, m)
+                scale(t + 1, ON_GPSIMD, NB)
+                scale_piece(t + 3, 0, G, "parted_3")
+                ring = ring[4:] + ring[:4]
 
-            turn_step(14)
-            multiply(13,0)
-            multiply(13,1)
-            multiply(13,2)
-            multiply(13,3)
-            scale_piece(NT - 2,0,G)
-            scale_piece(NT - 1,0,G)
-            quantize_keys(14,0)
-            finish_group(6,0)
-            quantize_keys(14,1)
-            finish_group(6,1)
-            turn_step(15)
-            finish_group(6,2)
-            finish_group(6,3)
-            multiply(14,0)
-            multiply(14,1)
-            multiply(14,2)
-            multiply(14,3)
-            quantize_keys(15,0)
-            finish_step(14,0)
-            multiply(15,0,halves=(0,))
-            multiply(15,1,halves=(0,))
-            quantize_keys(15,1)
-            finish_step(14,1)
-            finish_step(14,2)
-            finish_step(14,3)
-            multiply(15,0,halves=(1,))
-            finish_step(15,0)
-            multiply(15,1,halves=(1,))
-            finish_step(15,1)
-            multiply(15,2)
-            finish_step(15,2)
-            multiply_end(0,0)
-            multiply_end(1,0)
-            finish_end(0)
-            multiply_end(0,1)
-            multiply_end(1,1)
-            finish_end(1)
+            v = NT // 2 - 2
+            for m in range(M):
+                finish_group(NG - 2, m)
+            for g in range(1, G):
+                turn_pair(v, g, ring[g - 1])
+            for g in range(G - 1):
+                turn_pair(v + 1, g, ring[3 + g])
+            quantize_keys("pair", v, 0)
+            quantize_keys("pair", v, 1)
+            turn_pair(v + 1, G - 1, ring[6], copy=nc.vector.tensor_copy)
+            first = [new_bank(ring[(7 + m) % BANKS])[:, :TWO] for m in range(M)]
+            for z in range(2):
+                for m in range(M):
+                    multiply_pair(v, m, first[m], halves=(z,))
+            quantize_keys("pair", v + 1, 0)
+            quantize_keys("pair", v + 1, 1)
+            for m in range(M):
+                finish(first[m], TWO * v, TWO, m)
+            for m in range(M - 1):
+                second = new_bank(ring[3 + m])[:, :TWO]
+                multiply_pair(v + 1, m, second)
+                finish(second, T - TWO, TWO, m)
+            for j in range(2):
+                end = new_bank(ring[6 + j])[:, :P]
+                multiply_pair(v + 1, M - 1, end, lo=P * j, hi=P * (j + 1))
+                finish(end, T - TWO + P * j, P, M - 1)

@@ -31,21 +31,21 @@ GROUP = 4 * P
 TWO = 2 * P
 NG = T // GROUP
 BANKS = 8
-RAW_BUFS = 3
-DIRECT = 20
-ON_GPSIMD = 40
+NS = NT // 2
+HB = NB // 2
+LOAD_AHEAD = 6
 
 
 def tile_aged_key_retrieval_d3_kernel(tc, query, keys_bytes, keys_scale, age, rate, out):
     nc = tc.nc
     with ExitStack() as ctx:
         const = ctx.enter_context(tc.tile_pool(name="const", bufs=1))
-        raw_pool = ctx.enter_context(tc.tile_pool(name="raw", bufs=4))
+        raw_pool = ctx.enter_context(tc.tile_pool(name="raw", bufs=8))
         cast_pool = ctx.enter_context(tc.tile_pool(name="cast", bufs=2))
         parted_pool = ctx.enter_context(tc.tile_pool(name="parted", bufs=2))
         hand_pool = ctx.enter_context(tc.tile_pool(name="hand", bufs=1))
-        turned_pool = ctx.enter_context(tc.tile_pool(name="turned", bufs=5))
-        code_pool = ctx.enter_context(tc.tile_pool(name="code", bufs=7))
+        turned_pool = ctx.enter_context(tc.tile_pool(name="turned", bufs=4))
+        code_pool = ctx.enter_context(tc.tile_pool(name="code", bufs=4))
         result_pool = ctx.enter_context(tc.tile_pool(name="result", bufs=12))
         psum = ctx.enter_context(tc.psum_pool(name="psum", bufs=1))
 
@@ -91,19 +91,19 @@ def tile_aged_key_retrieval_d3_kernel(tc, query, keys_bytes, keys_scale, age, ra
         def find(table, t, a0):
             for first, end, row, at in table.get(t, []):
                 if first <= a0 < end:
-                    return row, at + BLOCK * (a0 - first)
+                    return row, at + BLOCK * (a0 - first), first, end
             return None
 
         def cast_run(t, a0, n, tag, pool=cast_pool):
-            row, at = find(raw, t, a0)
+            row, at, first, last = find(raw, t, a0)
             values = pool.tile([P, BLOCK * n], BF16, name=tag)
             nc.scalar.copy(out=values[:], in_=row[:, at : at + BLOCK * n].bitcast(FP8))
             done = 0
             while done < n:
-                end = min(NB, a0 + n - done)
+                end = min(last, a0 + n - done)
                 cast.setdefault(t, []).append((a0, end, values, BLOCK * done))
                 done = done + end - a0
-                t, a0 = t + 1, 0
+                t, a0 = t + 1, first
 
         def new_piece(t, g0, g1, tag, pool=parted_pool, bufs=None):
             piece = pool.tile([P, 2, PB * (g1 - g0), HALF], BF16, name=tag, bufs=bufs)
@@ -117,10 +117,10 @@ def tile_aged_key_retrieval_d3_kernel(tc, query, keys_bytes, keys_scale, age, ra
 
         def scale(t, a0, a1):
             if find(cast, t, a0) is None:
-                row, at = find(raw, t, a0)
+                row, at = find(raw, t, a0)[:2]
                 values = row[:, at : at + BLOCK * (a1 - a0)].bitcast(FP8)
             else:
-                row, at = find(cast, t, a0)
+                row, at = find(cast, t, a0)[:2]
                 values = row[:, at : at + BLOCK * (a1 - a0)]
             nc.vector.tensor_scalar(
                 out=piece_blocks(t, a0, a1).rearrange("p u a x -> p a u x"),
@@ -134,11 +134,11 @@ def tile_aged_key_retrieval_d3_kernel(tc, query, keys_bytes, keys_scale, age, ra
             new_piece(t, g0, g1, tag, bufs=bufs)
             scale(t, PB * g0, PB * g1)
 
-        def scale_on_gpsimd(t, a1):
-            row, at = find(cast, t, 0)
+        def scale_on_gpsimd(t, a0, a1):
+            row, at = find(cast, t, a0)[:2]
             nc.gpsimd.tensor_scalar(
-                out=piece_blocks(t, 0, a1),
-                in0=row[:, at : at + BLOCK * a1].rearrange("p (a u x) -> p u a x", u=2, x=HALF),
+                out=piece_blocks(t, a0, a1),
+                in0=row[:, at : at + BLOCK * (a1 - a0)].rearrange("p (a u x) -> p u a x", u=2, x=HALF),
                 scalar1=scale_sb[:, t : t + 1],
                 scalar2=0.0,
                 op0=MULT,
@@ -162,7 +162,10 @@ def tile_aged_key_retrieval_d3_kernel(tc, query, keys_bytes, keys_scale, age, ra
                 for u in range(2):
                     nc.tensor.transpose(bank[:, u, j, :], words(t, g, u), ident[:])
             if key not in turned:
-                turned[key] = turned_pool.tile([P, PASS, 4], BF16, name="turned_rows", align_bytes=64)
+                if key[0] == "step":
+                    turned[key] = turned_pool.tile([P, 2 * PASS, 4], BF16, name="turned_step", align_bytes=64, bufs=2)
+                else:
+                    turned[key] = turned_pool.tile([P, PASS, 4], BF16, name="turned_rows", align_bytes=64)
             copy(
                 out=turned[key][:, TWO * half : TWO * (half + 1), :].bitcast(F32).rearrange("p (n i) u -> p n u i", i=2),
                 in_=bank.rearrange("p u j (r i) -> p (j r) u i", i=2),
@@ -236,15 +239,49 @@ def tile_aged_key_retrieval_d3_kernel(tc, query, keys_bytes, keys_scale, age, ra
             finish(sums[c, m], GROUP * c, GROUP, m)
 
         def warm_up(n, b):
-            idle_bank = new_bank(b)
-            for i in range(n):
-                nc.tensor.matmul(idle_bank[:, :P], lhsT=ident[:], rhs=ident[:], start=True, stop=True)
+            rows = ident[:].unsqueeze(1).to_broadcast([P, n, P])
+            nc.tensor.matmul(new_bank(b)[:, : P * n], lhsT=ident[:], rhs=rows, start=True, stop=True)
 
-        def load_group(c):
-            load_keys(4 * c, 4, tag="raw_group", bufs=RAW_BUFS)
+        def load_step(s):
+            if s < NS - 2:
+                load_keys(4 * (s // 2), 4, 2 * (s % 2), 2 * (s % 2) + 2)
+            else:
+                load_keys(2 * s, 2)
 
         def hand(c):
-            return "hand_%d" % (c % 3)
+            return "hand_%d" % (c % 2)
+
+        def turn_step(s):
+            c, h = divmod(s, 2)
+            for q in range(4):
+                z, half = divmod(q, 2)
+                t = 4 * c + 2 * half
+                turn(("step", s), q, [(t, 2 * h + z), (t + 1, 2 * h + z)], q)
+
+        def quantize_step(s, halves=None):
+            if ("step", s) not in codes:
+                step_codes = code_pool.tile([P, 2 * PASS], U32, name="step_codes", align_bytes=64, bufs=3)
+                step_scales = code_pool.tile([P, 2 * PASS], U8, name="step_scales", align_bytes=64, bufs=3)
+                codes["step", s] = (step_codes, step_scales)
+            step_codes, step_scales = codes["step", s]
+            n = slice(0, 2 * PASS) if halves is None else slice(PASS * halves, PASS * (halves + 1))
+            nc.vector.quantize_mx(
+                out=step_codes[:, n].bitcast(FP8X4),
+                scales=step_scales[:, n],
+                in_=turned["step", s][:, n, :].rearrange("p n t -> p (n t)"),
+            )
+
+        def multiply_step(s, m):
+            c, h = divmod(s, 2)
+            if h == 0:
+                sums[c, m] = new_bank(4 + m)[:]
+            step_codes, step_scales = codes["step", s]
+            for z in range(2):
+                n = slice(PASS * z, PASS * (z + 1))
+                product(sums[c, m], m, 2 * h + z, step_codes[:, n], step_scales[:, n])
+
+        def scale_half(t, h):
+            scale_piece(t, 2 * h, 2 * h + 2, "parted_half", bufs=9)
 
         with tc.manual_schedule():
             for q in range(P // QUAD):
@@ -263,26 +300,29 @@ def tile_aged_key_retrieval_d3_kernel(tc, query, keys_bytes, keys_scale, age, ra
             load_query(2)
             load_query(3)
             nc.sync.dma_start(out=park.rearrange("o (p i) -> p (o i)", p=P), in_=log_sb[:])
-            load_group(1)
+            load_step(2)
+            load_step(3)
             nc.sync.dma_start(out=rate_sb[:], in_=rate.rearrange("(p m) -> p m", m=M))
-            load_group(2)
+            load_step(4)
             load_stale(0)
+            load_step(5)
             load_stale(1)
-            load_group(3)
+            load_step(6)
+            load_step(7)
 
-            cast_run(1, 0, NB // 2, "cast_gpsimd")
-            cast_run(1, NB // 2, NB // 2, "cast_gpsimd")
-            scale_piece(0, 0, 2, "parted_2")
-            scale_piece(0, 2, 4, "parted_0b")
-            scale_piece(1, 0, 2, "parted_3")
-            scale_piece(1, 2, 4, "parted_0b")
-            cast_run(3, 0, NB, "cast_last")
+            cast_run(1, 0, HB, "cast_gpsimd")
+            cast_run(1, HB, HB, "cast_gpsimd")
+            scale_half(0, 0)
+            scale_half(0, 1)
+            scale_half(1, 0)
+            scale_half(1, 1)
+            cast_run(3, 0, NB, "cast_step")
             for g in range(G):
                 turn_pair(0, g, g)
             warm_up(2, 7)
-            scale_piece(2, 0, G, "parted_2")
+            scale_piece(2, 0, G, "parted_tile")
             part_query(0)
-            scale_piece(3, 0, G, "parted_3")
+            scale_piece(3, 0, G, "parted_tile")
             turn_query(0, 4, 5)
             part_query(1)
             turn_pair(1, 0, 0)
@@ -299,102 +339,109 @@ def tile_aged_key_retrieval_d3_kernel(tc, query, keys_bytes, keys_scale, age, ra
             quantize_query(1)
             sums[0, 0] = new_bank(4)[:]
             multiply_pair(0, 0, sums[0, 0][:, :TWO])
+            cast_run(7, 0, HB, "cast_gpsimd")
             turn_query(2, 0, 1)
             turn_query(3, 6, 7)
             sums[0, 1] = new_bank(5)[:]
             multiply_pair(0, 1, sums[0, 1][:, :TWO])
-            scale_piece(4, 0, 1, "parted_0a")
+            scale_half(4, 0)
             quantize_keys("pair", 1, 1)
-            new_piece(5, 0, G, hand(0), pool=hand_pool)
-            scale(5, 0, NB // 2)
+            scale_half(5, 0)
+            scale_half(6, 0)
+            scale_half(7, 0)
             quantize_query(2)
-            scale(5, NB // 2, NB)
-            quantize_query(3)
             multiply_pair(1, 0, sums[0, 0][:, TWO:])
             multiply_pair(1, 1, sums[0, 1][:, TWO:])
-            cast_run(6, 0, NB, "cast_last")
-            cast_run(7, 0, NB, hand(1), pool=hand_pool)
+            cast_run(7, HB, HB, hand(0), pool=hand_pool)
+            turn_step(2)
             nc.scalar.activation(out=neg_rate[:], in_=rate_sb[:], func=COPY, scale=-1.0)
-            turn_wide(1, 0, 0, 2)
-            cast_run(9, 0, ON_GPSIMD, "cast_gpsimd")
-            cast_run(9, ON_GPSIMD, 2 * NB - ON_GPSIMD - DIRECT, hand(2), pool=hand_pool)
-            scale_piece(4, 1, G, "parted_0b")
+            cast_run(11, 0, HB, "cast_gpsimd")
+            cast_run(9, 0, NB, "cast_step")
+            scale_half(4, 1)
+            quantize_query(3)
+            scale_half(5, 1)
             for m in (2, 3):
-                sums[0, m] = new_bank(m - 2)[:]
+                sums[0, m] = new_bank(4 + m)[:]
                 multiply_pair(0, m, sums[0, m][:, :TWO])
                 multiply_pair(1, m, sums[0, m][:, TWO:])
-            scale_piece(8, 0, 1, "parted_0a")
-            scale_piece(6, 0, G, "parted_2")
-            scale_piece(7, 0, G, "parted_3")
-            ring = [3, 6, 7, 2, 4, 5, 0, 1]
+            scale_half(6, 1)
+            quantize_step(2, 0)
+            scale_half(7, 1)
+            quantize_step(2, 1)
 
-            for c in range(1, NG - 1):
+            for s in range(2, NS - 3):
+                c, h = divmod(s, 2)
                 t = 4 * (c + 1)
-                if c + 3 < NG:
-                    load_group(c + 3)
-                load_stale(c + 1)
-                new_piece(t + 1, 0, G, hand(c), pool=hand_pool)
-                scale_on_gpsimd(t + 1, ON_GPSIMD)
-                for m in range(M):
-                    finish_group(c - 1, m)
-                turn_wide(c, 0, 1, ring[0])
-                for g in range(1, G):
-                    for half in range(2):
-                        turn_wide(c, g, half, ring[2 * g - 1 + half])
-                cast_run(t + 3, 0, NB, "cast_last")
-                if c + 2 < NG:
-                    cast_run(t + 5, 0, ON_GPSIMD, "cast_gpsimd")
-                if c + 1 < NG - 1:
-                    turn_wide(c + 1, 0, 0, ring[7])
+                if s + LOAD_AHEAD < NS:
+                    load_step(s + LOAD_AHEAD)
+                if h == 0 and c + 1 < NG:
+                    load_stale(c + 1)
+                if s + 1 < NS - 2:
+                    turn_step(s + 1)
+                if h == 0:
+                    if s + 3 < NS - 1:
+                        cast_run(t + 2, HB, NB, hand(c), pool=hand_pool)
+                    else:
+                        cast_run(NT - 1, 0, NB, "cast_step")
+                    gt, ga = (t + 3, 0) if s + 2 < NS - 2 else (t + 1, HB)
+                    new_piece(gt, ga // PB, ga // PB + 2, hand(c - 1), pool=hand_pool)
+                    scale_on_gpsimd(gt, ga, ga + HB)
+                    for m in range(M):
+                        finish_group(c - 1, m)
+                elif s + 3 < NS - 2:
+                    cast_run(t + 7, 0, HB, "cast_gpsimd")
+                    cast_run(t + 5, 0, NB, "cast_step")
                 else:
-                    turn_pair(NT // 2 - 2, 0, ring[7])
-                if c + 2 < NG:
-                    cast_run(t + 5, ON_GPSIMD, 2 * NB - ON_GPSIMD - DIRECT, hand(c + 2), pool=hand_pool)
-                quantize_keys("wide", c, 0)
+                    cast_run(t + 5, HB, HB, "cast_gpsimd")
+                    cast_run(t + 4, HB, NB, "cast_step")
                 for m in range(M):
-                    multiply_wide(c, 0, m, ring[m])
-                new_piece(t + 2, 0, G, "parted_2")
-                scale(t + 2, 0, NB - DIRECT)
-                if c + 2 < NG:
-                    scale_piece(t + 4, 0, 1, "parted_0a")
-                quantize_keys("wide", c, 1)
-                for m in range(M):
-                    multiply_wide(c, 1, m)
-                scale(t + 2, NB - DIRECT, NB)
-                quantize_keys("wide", c, 2)
-                for m in range(M):
-                    multiply_wide(c, 2, m)
-                scale_piece(t, 1, G, "parted_0b")
-                quantize_keys("wide", c, 3)
-                for m in range(M):
-                    multiply_wide(c, 3, m)
-                scale(t + 1, ON_GPSIMD, NB)
-                scale_piece(t + 3, 0, G, "parted_3")
-                ring = ring[4:] + ring[:4]
+                    multiply_step(s, m)
+                if s + 2 < NS - 2:
+                    for j in range(3):
+                        scale_half(t + j, h)
+                else:
+                    scale_half(t, 0)
+                    scale_half(t + 1, 0)
+                    scale_half(t, 1)
+                if h == 0:
+                    quantize_step(s + 1)
+                else:
+                    quantize_step(s + 1, 0)
+                    scale_half(t + 3, h)
+                    quantize_step(s + 1, 1)
 
-            v = NT // 2 - 2
+            v = NS - 2
+            for g in range(G):
+                turn_pair(v, g, g)
             for m in range(M):
-                finish_group(NG - 2, m)
-            for g in range(1, G):
-                turn_pair(v, g, ring[g - 1])
-            for g in range(G - 1):
-                turn_pair(v + 1, g, ring[3 + g])
+                multiply_step(v - 1, m)
+            scale_piece(NT - 2, 0, G, "parted_tile")
+            scale_piece(NT - 1, 0, G, "parted_tile")
             quantize_keys("pair", v, 0)
+            finish_group(NG - 2, 0)
             quantize_keys("pair", v, 1)
-            turn_pair(v + 1, G - 1, ring[6], copy=nc.vector.tensor_copy)
-            first = [new_bank(ring[(7 + m) % BANKS])[:, :TWO] for m in range(M)]
-            for z in range(2):
-                for m in range(M):
-                    multiply_pair(v, m, first[m], halves=(z,))
-            quantize_keys("pair", v + 1, 0)
-            quantize_keys("pair", v + 1, 1)
+            finish_group(NG - 2, 1)
+            for g in range(G):
+                turn_pair(v + 1, g, g)
+            finish_group(NG - 2, 2)
+            finish_group(NG - 2, 3)
+            first = [new_bank(4 + m)[:, :TWO] for m in range(M)]
             for m in range(M):
+                multiply_pair(v, m, first[m])
+            quantize_keys("pair", v + 1, 0)
+            finish(first[0], TWO * v, TWO, 0)
+            second = [new_bank(m)[:, :TWO] for m in range(M - 1)]
+            for m in range(2):
+                multiply_pair(v + 1, m, second[m], halves=(0,))
+            quantize_keys("pair", v + 1, 1)
+            for m in range(1, M):
                 finish(first[m], TWO * v, TWO, m)
-            for m in range(M - 1):
-                second = new_bank(ring[3 + m])[:, :TWO]
-                multiply_pair(v + 1, m, second)
-                finish(second, T - TWO, TWO, m)
+            for m in range(2):
+                multiply_pair(v + 1, m, second[m], halves=(1,))
+                finish(second[m], T - TWO, TWO, m)
+            multiply_pair(v + 1, 2, second[2])
+            finish(second[2], T - TWO, TWO, 2)
             for j in range(2):
-                end = new_bank(ring[6 + j])[:, :P]
+                end = new_bank(M - 1 + j)[:, :P]
                 multiply_pair(v + 1, M - 1, end, lo=P * j, hi=P * (j + 1))
                 finish(end, T - TWO + P * j, P, M - 1)

@@ -50,7 +50,7 @@ def tile_aged_key_retrieval_d3_kernel(tc, query, keys_bytes, keys_scale, age, ra
         psum = ctx.enter_context(tc.psum_pool(name="psum", bufs=1))
 
         ident = const.tile([P, P], F32, name="ident")
-        scale_rows = const.tile([P, QUAD], F32, name="scale_rows", align_bytes=64)
+        scale_rows = const.tile([P, P], F32, name="scale_rows")
         scale_sb = const.tile([P, NT], F32, name="scale_sb", align_bytes=64)
         age_sb = const.tile([P, T // P], BF16, name="age_sb")
         log_sb = const.tile([P, T // P], F32, name="log_sb")
@@ -62,7 +62,6 @@ def tile_aged_key_retrieval_d3_kernel(tc, query, keys_bytes, keys_scale, age, ra
         stale = [const.tile([P, GROUP], F32, name="stale_%d" % c) for c in range(NG)]
 
         key_view = keys_bytes.rearrange("(t p) k -> p t k", p=P)
-        scale_view = keys_scale.rearrange("(t q i) o -> q t (i o)", q=P // QUAD, i=QUAD)
         query_view = query.rearrange("(p m) k -> p m k", m=M)
         out_view = out.rearrange("(p m) n -> p m n", m=M)
         park = out[Q - 1 : Q, :]
@@ -284,8 +283,9 @@ def tile_aged_key_retrieval_d3_kernel(tc, query, keys_bytes, keys_scale, age, ra
             scale_piece(t, 2 * h, 2 * h + 2, "parted_half", bufs=9)
 
         with tc.manual_schedule():
-            for q in range(P // QUAD):
-                nc.scalar.dma_start(out=scale_rows[QUAD * q : QUAD * (q + 1), :], in_=scale_view[q])
+            nc.scalar.dma_start(out=scale_rows[:NT, :], in_=keys_scale.rearrange("(t p) o -> t (p o)", p=P))
+            nc.vector.memset(scale_rows[QUAD : 2 * QUAD, :], 0.0)
+            nc.vector.memset(scale_rows[2 * QUAD :, :], 0.0)
             nc.scalar.dma_start(out=age_sb[:], in_=age.rearrange("(p i) -> p i", p=P))
             load_keys(0, 2, 0, 2)
             load_keys(0, 2, 2, 4)
@@ -294,8 +294,10 @@ def tile_aged_key_retrieval_d3_kernel(tc, query, keys_bytes, keys_scale, age, ra
             load_query(0)
             load_query(1)
             make_identity(nc, ident[:])
-            warm_up(4, 7)
-            nc.vector.transpose(scale_sb[:], scale_rows[:])
+            scale_bank = new_bank(4)
+            nc.tensor.transpose(scale_bank[:, :P], scale_rows[:], ident[:])
+            nc.vector.tensor_copy(out=scale_sb[:], in_=scale_bank[:, :NT])
+            warm_up(3, 7)
             nc.scalar.activation(out=log_sb[:], in_=age_sb[:], func=LN, bias=1.0)
             load_query(2)
             load_query(3)

@@ -283,11 +283,12 @@ def tile_aged_key_retrieval_d3_kernel(tc, query, keys_bytes, keys_scale, age, ra
             scale_piece(t, 2 * h, 2 * h + 2, "parted_half", bufs=9)
 
         with tc.manual_schedule():
-            nc.scalar.dma_start(out=scale_rows[:NT, :], in_=keys_scale.rearrange("(t p) o -> t (p o)", p=P))
+            nc.sync.dma_start(out=scale_rows[:NT, :], in_=keys_scale.rearrange("(t p) o -> t (p o)", p=P))
             nc.vector.memset(scale_rows[QUAD : 2 * QUAD, :], 0.0)
             nc.vector.memset(scale_rows[2 * QUAD :, :], 0.0)
-            nc.scalar.dma_start(out=age_sb[:], in_=age.rearrange("(p i) -> p i", p=P))
-            load_keys(0, 2, 0, 2)
+            load_keys(1, 1, 0, 2)
+            nc.sync.dma_start(out=age_sb[:], in_=age.rearrange("(p i) -> p i", p=P))
+            load_keys(0, 1, 0, 2)
             load_keys(0, 2, 2, 4)
             load_keys(3, 1)
             load_keys(2, 1)
@@ -315,8 +316,8 @@ def tile_aged_key_retrieval_d3_kernel(tc, query, keys_bytes, keys_scale, age, ra
             cast_run(1, 0, HB, "cast_gpsimd")
             cast_run(1, HB, HB, "cast_gpsimd")
             scale_half(0, 0)
-            scale_half(0, 1)
             scale_half(1, 0)
+            scale_half(0, 1)
             scale_half(1, 1)
             cast_run(3, 0, NB, "cast_step")
             for g in range(G):
@@ -382,9 +383,13 @@ def tile_aged_key_retrieval_d3_kernel(tc, query, keys_bytes, keys_scale, age, ra
                     turn_step(s + 1)
                 if h == 0:
                     if s + 3 < NS - 1:
-                        cast_run(t + 2, HB, NB, hand(c), pool=hand_pool)
+                        if c % 2 == 1:
+                            cast_run(t + 1, HB, 3 * HB, hand(c), pool=hand_pool)
+                        else:
+                            cast_run(t + 2, HB, NB, hand(c), pool=hand_pool)
                     else:
-                        cast_run(NT - 1, 0, NB, "cast_step")
+                        cast_run(NT - 2, HB, NB, "cast_step")
+                        cast_run(NT - 1, HB, HB, "cast_gpsimd")
                     gt, ga = (t + 3, 0) if s + 2 < NS - 2 else (t + 1, HB)
                     new_piece(gt, ga // PB, ga // PB + 2, hand(c - 1), pool=hand_pool)
                     scale_on_gpsimd(gt, ga, ga + HB)
@@ -417,8 +422,9 @@ def tile_aged_key_retrieval_d3_kernel(tc, query, keys_bytes, keys_scale, age, ra
                 turn_pair(v, g, g)
             for m in range(M):
                 multiply_step(v - 1, m)
-            scale_piece(NT - 2, 0, G, "parted_tile")
-            scale_piece(NT - 1, 0, G, "parted_tile")
+            for h in range(2):
+                scale_half(NT - 2, h)
+                scale_half(NT - 1, h)
             quantize_keys("pair", v, 0)
             finish_group(NG - 2, 0)
             quantize_keys("pair", v, 1)

@@ -50,6 +50,8 @@ def tile_aged_key_retrieval_d3_kernel(tc, query, keys_bytes, keys_scale, age, ra
         psum = ctx.enter_context(tc.psum_pool(name="psum", bufs=1))
 
         ident = const.tile([P, P], F32, name="ident")
+        ident_bf = const.tile([P, P], BF16, name="ident_bf")
+        spread = const.tile([P, TWO], BF16, name="spread")
         scale_rows = const.tile([P, P], F32, name="scale_rows")
         scale_sb = const.tile([P, NT], F32, name="scale_sb", align_bytes=64)
         age_sb = const.tile([P, T // P], BF16, name="age_sb")
@@ -155,11 +157,22 @@ def tile_aged_key_retrieval_d3_kernel(tc, query, keys_bytes, keys_scale, age, ra
             piece, i = parted[t, g]
             return piece[:, u].rearrange("p a x -> p (a x)").bitcast(F32)[:, P * i : P * (i + 1)]
 
-        def turn(key, half, pairs, b, copy=nc.scalar.copy):
-            bank = new_bank(b)[:].rearrange("p (u j r) -> p u j r", u=2, j=2)
+        def elements(t, g, u, e):
+            piece, i = parted[t, g]
+            return piece[:, u].rearrange("p a x -> p (a x)")[:, TWO * i + e : TWO * (i + 1) : 2]
+
+        def turn(key, half, pairs, b, copy=nc.scalar.copy, bridge=False):
+            whole = new_bank(b)
+            bank = whole[:].rearrange("p (u j r) -> p u j r", u=2, j=2)
             for j, (t, g) in enumerate(pairs):
-                for u in range(2):
-                    nc.tensor.transpose(bank[:, u, j, :], words(t, g, u), ident[:])
+                if bridge and j == 0:
+                    halves = whole[:].bitcast(BF16)
+                    nc.tensor.matmul(halves[:, :TWO], lhsT=elements(t, g, 0, 1), rhs=spread[:], start=True, stop=True)
+                    nc.tensor.transpose(bank[:, 1, j, :], words(t, g, 1), ident[:])
+                    nc.tensor.matmul(halves[:, 0:TWO:2], lhsT=elements(t, g, 0, 0), rhs=ident_bf[:], start=True, stop=True)
+                else:
+                    for u in range(2):
+                        nc.tensor.transpose(bank[:, u, j, :], words(t, g, u), ident[:])
             if key not in turned:
                 if key[0] == "step":
                     turned[key] = turned_pool.tile([P, 2 * PASS, 4], BF16, name="turned_step", align_bytes=64, bufs=2)
@@ -255,7 +268,7 @@ def tile_aged_key_retrieval_d3_kernel(tc, query, keys_bytes, keys_scale, age, ra
             for q in range(4):
                 z, half = divmod(q, 2)
                 t = 4 * c + 2 * half
-                turn(("step", s), q, [(t, 2 * h + z), (t + 1, 2 * h + z)], q)
+                turn(("step", s), q, [(t, 2 * h + z), (t + 1, 2 * h + z)], q, bridge=(q == 0))
 
         def quantize_step(s, halves=None):
             if ("step", s) not in codes:
@@ -294,7 +307,10 @@ def tile_aged_key_retrieval_d3_kernel(tc, query, keys_bytes, keys_scale, age, ra
             load_keys(2, 1)
             load_query(0)
             load_query(1)
+            nc.vector.memset(spread[:], 0.0)
             make_identity(nc, ident[:])
+            nc.vector.tensor_copy(out=ident_bf[:], in_=ident[:])
+            nc.vector.tensor_copy(out=spread[:, 1:TWO:2], in_=ident[:])
             scale_bank = new_bank(4)
             nc.tensor.transpose(scale_bank[:, :P], scale_rows[:], ident[:])
             nc.vector.tensor_copy(out=scale_sb[:], in_=scale_bank[:, :NT])

@@ -161,18 +161,22 @@ def tile_aged_key_retrieval_d3_kernel(tc, query, keys_bytes, keys_scale, age, ra
             piece, i = parted[t, g]
             return piece[:, u].rearrange("p a x -> p (a x)")[:, TWO * i + e : TWO * (i + 1) : 2]
 
-        def turn(key, half, pairs, b, copy=nc.scalar.copy, bridge=False):
+        def open_run(t, g, b):
             whole = new_bank(b)
+            nc.tensor.matmul(whole[:].bitcast(BF16)[:, :TWO], lhsT=elements(t, g, 0, 1), rhs=spread[:], start=True, stop=True)
+            return whole
+
+        def turn(key, half, pairs, b, copy=nc.scalar.copy, opened=None):
+            whole = new_bank(b) if opened is None else opened
             bank = whole[:].rearrange("p (u j r) -> p u j r", u=2, j=2)
             for j, (t, g) in enumerate(pairs):
-                if bridge and j == 0:
-                    halves = whole[:].bitcast(BF16)
-                    nc.tensor.matmul(halves[:, :TWO], lhsT=elements(t, g, 0, 1), rhs=spread[:], start=True, stop=True)
-                    nc.tensor.transpose(bank[:, 1, j, :], words(t, g, 1), ident[:])
-                    nc.tensor.matmul(halves[:, 0:TWO:2], lhsT=elements(t, g, 0, 0), rhs=ident_bf[:], start=True, stop=True)
-                else:
-                    for u in range(2):
+                for u in range(2):
+                    if opened is None or j + u > 0:
                         nc.tensor.transpose(bank[:, u, j, :], words(t, g, u), ident[:])
+            if opened is not None:
+                t, g = pairs[0]
+                even = whole[:].bitcast(BF16)[:, 0:TWO:2]
+                nc.tensor.matmul(even, lhsT=elements(t, g, 0, 0), rhs=ident_bf[:], start=True, stop=True)
             if key not in turned:
                 if key[0] == "step":
                     turned[key] = turned_pool.tile([P, 2 * PASS, 4], BF16, name="turned_step", align_bytes=64, bufs=2)
@@ -265,10 +269,11 @@ def tile_aged_key_retrieval_d3_kernel(tc, query, keys_bytes, keys_scale, age, ra
 
         def turn_step(s):
             c, h = divmod(s, 2)
-            for q in range(4):
+            opened = open_run(4 * c, 2 * h + 1, 3)
+            for b, q in enumerate((0, 1, 3, 2)):
                 z, half = divmod(q, 2)
                 t = 4 * c + 2 * half
-                turn(("step", s), q, [(t, 2 * h + z), (t + 1, 2 * h + z)], q, bridge=(q == 0))
+                turn(("step", s), q, [(t, 2 * h + z), (t + 1, 2 * h + z)], b, opened=opened if b == 3 else None)
 
         def quantize_step(s, halves=None):
             if ("step", s) not in codes:
@@ -309,8 +314,8 @@ def tile_aged_key_retrieval_d3_kernel(tc, query, keys_bytes, keys_scale, age, ra
             load_query(1)
             nc.vector.memset(spread[:], 0.0)
             make_identity(nc, ident[:])
-            nc.vector.tensor_copy(out=ident_bf[:], in_=ident[:])
             nc.vector.tensor_copy(out=spread[:, 1:TWO:2], in_=ident[:])
+            nc.vector.tensor_copy(out=ident_bf[:], in_=ident[:])
             scale_bank = new_bank(4)
             nc.tensor.transpose(scale_bank[:, :P], scale_rows[:], ident[:])
             nc.vector.tensor_copy(out=scale_sb[:], in_=scale_bank[:, :NT])

@@ -191,12 +191,11 @@ def tile_aged_key_retrieval_d3_kernel(tc, query, keys_bytes, keys_scale, age, ra
             t = 4 * c + 2 * half
             turn(("wide", c, g), half, [(t, g), (t + 1, g)], b)
 
-        def turn_pair(v, g, b, copy=nc.scalar.copy):
-            turn(("pair", v, g // 2), g % 2, [(2 * v, g), (2 * v + 1, g)], b, copy)
+        def turn_pair(v, g, b, opened=None):
+            turn(("pair", v, g // 2), g % 2, [(2 * v, g), (2 * v + 1, g)], b, opened=opened)
 
-        def turn_query(m, b0, b1):
-            for half, b in enumerate((b0, b1)):
-                turn(("query", m), half, [(NT + m, 2 * half), (NT + m, 2 * half + 1)], b)
+        def turn_query(m, half, b, opened=None):
+            turn(("query", m), half, [(NT + m, 2 * half), (NT + m, 2 * half + 1)], b, opened=opened)
 
         def quantize(key, out_codes, out_scales):
             nc.vector.quantize_mx(
@@ -275,6 +274,11 @@ def tile_aged_key_retrieval_d3_kernel(tc, query, keys_bytes, keys_scale, age, ra
                 t = 4 * c + 2 * half
                 turn(("step", s), q, [(t, 2 * h + z), (t + 1, 2 * h + z)], b, opened=opened if b == 3 else None)
 
+        def turn_unit(v, order):
+            opened = open_run(2 * v, order[-1], G - 1)
+            for b, g in enumerate(order):
+                turn_pair(v, g, b, opened=opened if b == G - 1 else None)
+
         def quantize_step(s, halves=None):
             if ("step", s) not in codes:
                 step_codes = code_pool.tile([P, 2 * PASS], U32, name="step_codes", align_bytes=64, bufs=3)
@@ -347,11 +351,13 @@ def tile_aged_key_retrieval_d3_kernel(tc, query, keys_bytes, keys_scale, age, ra
             scale_piece(2, 0, G, "parted_tile")
             part_query(0)
             scale_piece(3, 0, G, "parted_tile")
-            turn_query(0, 4, 5)
+            turn_query(0, 0, 4)
+            turn_query(0, 1, 5)
             part_query(1)
             turn_pair(1, 0, 0)
             turn_pair(1, 1, 1)
-            turn_query(1, 6, 7)
+            turn_query(1, 0, 6)
+            turn_query(1, 1, 7)
             turn_pair(1, 2, 2)
             turn_pair(1, 3, 3)
             quantize_keys("pair", 0, 0)
@@ -364,8 +370,10 @@ def tile_aged_key_retrieval_d3_kernel(tc, query, keys_bytes, keys_scale, age, ra
             sums[0, 0] = new_bank(4)[:]
             multiply_pair(0, 0, sums[0, 0][:, :TWO])
             cast_run(7, 0, HB, "cast_gpsimd")
-            turn_query(2, 0, 1)
-            turn_query(3, 6, 7)
+            turn_query(2, 0, 0)
+            turn_query(2, 1, 1)
+            turn_query(3, 0, 6)
+            turn_query(3, 1, 7)
             sums[0, 1] = new_bank(5)[:]
             multiply_pair(0, 1, sums[0, 1][:, :TWO])
             scale_half(4, 0)
@@ -428,9 +436,9 @@ def tile_aged_key_retrieval_d3_kernel(tc, query, keys_bytes, keys_scale, age, ra
                     for j in range(3):
                         scale_half(t + j, h)
                 else:
+                    scale_half(t, 1)
                     scale_half(t, 0)
                     scale_half(t + 1, 0)
-                    scale_half(t, 1)
                 if h == 0:
                     quantize_step(s + 1)
                 else:
@@ -439,19 +447,17 @@ def tile_aged_key_retrieval_d3_kernel(tc, query, keys_bytes, keys_scale, age, ra
                     quantize_step(s + 1, 1)
 
             v = NS - 2
-            for g in range(G):
-                turn_pair(v, g, g)
+            turn_unit(v, (2, 3, 0, 1))
             for m in range(M):
                 multiply_step(v - 1, m)
             for h in range(2):
                 scale_half(NT - 2, h)
                 scale_half(NT - 1, h)
-            quantize_keys("pair", v, 0)
-            finish_group(NG - 2, 0)
             quantize_keys("pair", v, 1)
+            finish_group(NG - 2, 0)
+            quantize_keys("pair", v, 0)
             finish_group(NG - 2, 1)
-            for g in range(G):
-                turn_pair(v + 1, g, g)
+            turn_unit(v + 1, (0, 1, 2, 3))
             finish_group(NG - 2, 2)
             finish_group(NG - 2, 3)
             first = [new_bank(4 + m)[:, :TWO] for m in range(M)]

from contextlib import ExitStack

import concourse.mybir as mybir
from concourse.masks import make_identity

Q, T, K = 512, 4096, 2048
FLOPS = 2 * Q * T * K

F32 = mybir.dt.float32
BF16 = mybir.dt.bfloat16
U32 = mybir.dt.uint32
U8 = mybir.dt.uint8
FP8 = mybir.dt.float8_e4m3fn
FP8X4 = mybir.dt.float8_e4m3fn_x4
MULT = mybir.AluOpType.mult
ADD = mybir.AluOpType.add
COPY = mybir.ActivationFunctionType.Copy
LN = mybir.ActivationFunctionType.Ln

P = 128
QUAD = 32
PASS = 512
G = K // PASS
M = Q // P
BLOCK = 32
HALF = BLOCK // 2
NB = K // BLOCK
PB = PASS // BLOCK
NT = T // P
GROUP = 4 * P
TWO = 2 * P
NG = T // GROUP
BANKS = 8
NS = NT // 2
HB = NB // 2
LOAD_AHEAD = 6


def tile_aged_key_retrieval_d3_kernel(tc, query, keys_bytes, keys_scale, age, rate, out):
    nc = tc.nc
    with ExitStack() as ctx:
        const = ctx.enter_context(tc.tile_pool(name="const", bufs=1))
        raw_pool = ctx.enter_context(tc.tile_pool(name="raw", bufs=8))
        cast_pool = ctx.enter_context(tc.tile_pool(name="cast", bufs=2))
        parted_pool = ctx.enter_context(tc.tile_pool(name="parted", bufs=2))
        hand_pool = ctx.enter_context(tc.tile_pool(name="hand", bufs=1))
        turned_pool = ctx.enter_context(tc.tile_pool(name="turned", bufs=4))
        code_pool = ctx.enter_context(tc.tile_pool(name="code", bufs=4))
        result_pool = ctx.enter_context(tc.tile_pool(name="result", bufs=12))
        psum = ctx.enter_context(tc.psum_pool(name="psum", bufs=1))

        ident = const.tile([P, P], F32, name="ident")
        ident_bf = const.tile([P, P], BF16, name="ident_bf")
        spread = const.tile([P, TWO], BF16, name="spread")
        scale_rows = const.tile([P, P], F32, name="scale_rows")
        scale_sb = const.tile([P, NT], F32, name="scale_sb", align_bytes=64)
        age_sb = const.tile([P, T // P], BF16, name="age_sb")
        log_sb = const.tile([P, T // P], F32, name="log_sb")
        rate_sb = const.tile([P, M], BF16, name="rate_sb")
        neg_rate = const.tile([P, M], F32, name="neg_rate")
        query_sb = [const.tile([P, K], BF16, name="query_%d" % m) for m in range(M)]
        q_codes = [const.tile([P, G * P], U32, name="q_codes_%d" % m, align_bytes=64) for m in range(M)]
        q_scales = [const.tile([P, G * P], U8, name="q_scales_%d" % m, align_bytes=64) for m in range(M)]
        stale = [const.tile([P, GROUP], F32, name="stale_%d" % c) for c in range(NG)]

        key_view = keys_bytes.rearrange("(t p) k -> p t k", p=P)
        query_view = query.rearrange("(p m) k -> p m k", m=M)
        out_view = out.rearrange("(p m) n -> p m n", m=M)
        park = out[Q - 1 : Q, :]

        raw, cast, parted, turned, codes, sums = {}, {}, {}, {}, {}, {}

        def new_bank(i):
            return psum.tile([P, GROUP], F32, name="bank_%d" % (i % BANKS))


        def load_keys(t, n, g0=0, g1=G, tag="raw_keys", bufs=None):
            width = PASS * (g1 - g0)
            rows = raw_pool.tile([P, n * width], U8, name=tag, bufs=bufs)
            nc.sync.dma_start(
                out=rows[:].rearrange("p (j k) -> p j k", j=n), in_=key_view[:, t : t + n, PASS * g0 : PASS * g1]
            )
            for j in range(n):
                raw.setdefault(t + j, []).append((PB * g0, PB * g1, rows, width * j))

        def load_query(m):
            nc.sync.dma_start(out=query_sb[m][:], in_=query_view[:, m, :])

        def load_stale(c):
            nc.sync.dma_start(out=stale[c][:], in_=park[0, GROUP * c : GROUP * (c + 1)].partition_broadcast(P))

        def find(table, t, a0):
            for first, end, row, at in table.get(t, []):
                if first <= a0 < end:
                    return row, at + BLOCK * (a0 - first), first, end
            return None

        def cast_run(t, a0, n, tag, pool=cast_pool):
            row, at, first, last = find(raw, t, a0)
            values = pool.tile([P, BLOCK * n], BF16, name=tag)
            nc.scalar.copy(out=values[:], in_=row[:, at : at + BLOCK * n].bitcast(FP8))
            done = 0
            while done < n:
                end = min(last, a0 + n - done)
                cast.setdefault(t, []).append((a0, end, values, BLOCK * done))
                done = done + end - a0
                t, a0 = t + 1, first

        def new_piece(t, g0, g1, tag, pool=parted_pool, bufs=None):
            piece = pool.tile([P, 2, PB * (g1 - g0), HALF], BF16, name=tag, bufs=bufs)
            for g in range(g0, g1):
                parted[t, g] = (piece, g - g0)

        def piece_blocks(t, a0, a1):
            piece, i = parted[t, a0 // PB]
            lo = PB * i + a0 % PB
            return piece[:, :, lo : lo + a1 - a0, :]

        def scale(t, a0, a1):
            if find(cast, t, a0) is None:
                row, at = find(raw, t, a0)[:2]
                values = row[:, at : at + BLOCK * (a1 - a0)].bitcast(FP8)
            else:
                row, at = find(cast, t, a0)[:2]
                values = row[:, at : at + BLOCK * (a1 - a0)]
            nc.vector.tensor_scalar(
                out=piece_blocks(t, a0, a1).rearrange("p u a x -> p a u x"),
                in0=values.rearrange("p (a u x) -> p a u x", u=2, x=HALF),
                scalar1=scale_sb[:, t : t + 1],
                scalar2=None,
                op0=MULT,
            )

        def scale_piece(t, g0, g1, tag, bufs=None):
            new_piece(t, g0, g1, tag, bufs=bufs)
            scale(t, PB * g0, PB * g1)

        def scale_on_gpsimd(t, a0, a1):
            row, at = find(cast, t, a0)[:2]
            nc.gpsimd.tensor_scalar(
                out=piece_blocks(t, a0, a1),
                in0=row[:, at : at + BLOCK * (a1 - a0)].rearrange("p (a u x) -> p u a x", u=2, x=HALF),
                scalar1=scale_sb[:, t : t + 1],
                scalar2=0.0,
                op0=MULT,
                op1=ADD,
            )

        def part_query(m):
            new_piece(NT + m, 0, G, "parted_query")
            nc.vector.tensor_copy(
                out=piece_blocks(NT + m, 0, NB).rearrange("p u a x -> p a u x"),
                in_=query_sb[m][:].rearrange("p (a u x) -> p a u x", u=2, x=HALF),
            )

        def words(t, g, u):
            piece, i = parted[t, g]
            return piece[:, u].rearrange("p a x -> p (a x)").bitcast(F32)[:, P * i : P * (i + 1)]

        def elements(t, g, u, e):
            piece, i = parted[t, g]
            return piece[:, u].rearrange("p a x -> p (a x)")[:, TWO * i + e : TWO * (i + 1) : 2]

        def open_run(t, g, b):
            whole = new_bank(b)
            nc.tensor.matmul(whole[:].bitcast(BF16)[:, :TWO], lhsT=elements(t, g, 0, 1), rhs=spread[:], start=True, stop=True)
            return whole

        def turn(key, half, pairs, b, copy=nc.scalar.copy, opened=None):
            whole = new_bank(b) if opened is None else opened
            bank = whole[:].rearrange("p (u j r) -> p u j r", u=2, j=2)
            for j, (t, g) in enumerate(pairs):
                for u in range(2):
                    if opened is None or j + u > 0:
                        nc.tensor.transpose(bank[:, u, j, :], words(t, g, u), ident[:])
            if opened is not None:
                t, g = pairs[0]
                even = whole[:].bitcast(BF16)[:, 0:TWO:2]
                nc.tensor.matmul(even, lhsT=elements(t, g, 0, 0), rhs=ident_bf[:], start=True, stop=True)
            if key not in turned:
                if key[0] == "step":
                    turned[key] = turned_pool.tile([P, 2 * PASS, 4], BF16, name="turned_step", align_bytes=64, bufs=2)
                else:
                    turned[key] = turned_pool.tile([P, PASS, 4], BF16, name="turned_rows", align_bytes=64)
            copy(
                out=turned[key][:, TWO * half : TWO * (half + 1), :].bitcast(F32).rearrange("p (n i) u -> p n u i", i=2),
                in_=bank.rearrange("p u j (r i) -> p (j r) u i", i=2),
            )

        def turn_wide(c, g, half, b):
            t = 4 * c + 2 * half
            turn(("wide", c, g), half, [(t, g), (t + 1, g)], b)

        def turn_pair(v, g, b, opened=None):
            turn(("pair", v, g // 2), g % 2, [(2 * v, g), (2 * v + 1, g)], b, opened=opened)

        def turn_query(m, half, b, opened=None):
            turn(("query", m), half, [(NT + m, 2 * half), (NT + m, 2 * half + 1)], b, opened=opened)

        def quantize(key, out_codes, out_scales):
            nc.vector.quantize_mx(
                out=out_codes[:].bitcast(FP8X4),
                scales=out_scales[:],
                in_=turned[key][:].rearrange("p n t -> p (n t)"),
            )

        def quantize_keys(*key):
            key_codes = code_pool.tile([P, PASS], U32, name="key_codes", align_bytes=64)
            key_scales = code_pool.tile([P, PASS], U8, name="key_scales", align_bytes=64)
            codes[key] = (key_codes, key_scales)
            quantize(key, key_codes, key_scales)

        def quantize_query(m):
            quantize(("query", m), q_codes[m], q_scales[m])

        def product(acc, m, g, key_codes, key_scales):
            nc.tensor.matmul_mx(
                out=acc,
                lhsT=q_codes[m][:, P * g : P * (g + 1)].bitcast(FP8X4),
                lhsT_scale=q_scales[m][:, P * g : P * (g + 1)],
                rhs=key_codes.bitcast(FP8X4),
                rhs_scale=key_scales,
                start=(g == 0),
                stop=(g == G - 1),
            )

        def multiply_wide(c, g, m, b=None):
            if b is not None:
                sums[c, m] = new_bank(b)[:]
            key_codes, key_scales = codes["wide", c, g]
            product(sums[c, m], m, g, key_codes[:], key_scales[:])

        def multiply_pair(v, m, acc, halves=(0, 1), lo=0, hi=TWO):
            for z in halves:
                key_codes, key_scales = codes["pair", v, z]
                for i in range(2):
                    n = slice(TWO * i + lo, TWO * i + hi)
                    product(acc, m, 2 * z + i, key_codes[:, n], key_scales[:, n])

        def finish(acc, first, width, m):
            c, lo = divmod(first, GROUP)
            result = result_pool.tile([P, width], F32, name="scores")
            nc.vector.scalar_tensor_tensor(
                out=result[:],
                in0=stale[c][:, lo : lo + width],
                scalar=neg_rate[:, m : m + 1],
                in1=acc,
                op0=MULT,
                op1=ADD,
            )
            nc.sync.dma_start(out=out_view[:, m, first : first + width], in_=result[:])

        def finish_group(c, m):
            finish(sums[c, m], GROUP * c, GROUP, m)

        def warm_up(n, b):
            rows = ident[:].unsqueeze(1).to_broadcast([P, n, P])
            nc.tensor.matmul(new_bank(b)[:, : P * n], lhsT=ident[:], rhs=rows, start=True, stop=True)

        def load_step(s):
            if s < NS - 2:
                load_keys(4 * (s // 2), 4, 2 * (s % 2), 2 * (s % 2) + 2)
            else:
                load_keys(2 * s, 2)

        def hand(c):
            return "hand_%d" % (c % 2)

        def turn_step(s):
            c, h = divmod(s, 2)
            opened = open_run(4 * c, 2 * h + 1, 3)
            for b, q in enumerate((0, 1, 3, 2)):
                z, half = divmod(q, 2)
                t = 4 * c + 2 * half
                turn(("step", s), q, [(t, 2 * h + z), (t + 1, 2 * h + z)], b, opened=opened if b == 3 else None)

        def turn_unit(v, order):
            opened = open_run(2 * v, order[-1], G - 1)
            for b, g in enumerate(order):
                turn_pair(v, g, b, opened=opened if b == G - 1 else None)

        def quantize_step(s, halves=None):
            if ("step", s) not in codes:
                step_codes = code_pool.tile([P, 2 * PASS], U32, name="step_codes", align_bytes=64, bufs=3)
                step_scales = code_pool.tile([P, 2 * PASS], U8, name="step_scales", align_bytes=64, bufs=3)
                codes["step", s] = (step_codes, step_scales)
            step_codes, step_scales = codes["step", s]
            n = slice(0, 2 * PASS) if halves is None else slice(PASS * halves, PASS * (halves + 1))
            nc.vector.quantize_mx(
                out=step_codes[:, n].bitcast(FP8X4),
                scales=step_scales[:, n],
                in_=turned["step", s][:, n, :].rearrange("p n t -> p (n t)"),
            )

        def multiply_step(s, m):
            c, h = divmod(s, 2)
            if h == 0:
                sums[c, m] = new_bank(4 + m)[:]
            step_codes, step_scales = codes["step", s]
            for z in range(2):
                n = slice(PASS * z, PASS * (z + 1))
                product(sums[c, m], m, 2 * h + z, step_codes[:, n], step_scales[:, n])

        def scale_half(t, h):
            scale_piece(t, 2 * h, 2 * h + 2, "parted_half", bufs=9)

        with tc.manual_schedule():
            nc.sync.dma_start(out=scale_rows[:NT, :], in_=keys_scale.rearrange("(t p) o -> t (p o)", p=P))
            nc.vector.memset(scale_rows[QUAD : 2 * QUAD, :], 0.0)
            nc.vector.memset(scale_rows[2 * QUAD :, :], 0.0)
            load_keys(1, 1, 0, 2)
            nc.sync.dma_start(out=age_sb[:], in_=age.rearrange("(p i) -> p i", p=P))
            load_keys(0, 1, 0, 2)
            load_keys(0, 2, 2, 4)
            load_keys(3, 1)
            load_keys(2, 1)
            load_query(0)
            load_query(1)
            nc.vector.memset(spread[:], 0.0)
            make_identity(nc, ident[:])
            nc.vector.tensor_copy(out=spread[:, 1:TWO:2], in_=ident[:])
            nc.vector.tensor_copy(out=ident_bf[:], in_=ident[:])
            scale_bank = new_bank(4)
            nc.tensor.transpose(scale_bank[:, :P], scale_rows[:], ident[:])
            nc.vector.tensor_copy(out=scale_sb[:], in_=scale_bank[:, :NT])
            warm_up(3, 7)
            nc.scalar.activation(out=log_sb[:], in_=age_sb[:], func=LN, bias=1.0)
            load_query(2)
            load_query(3)
            nc.sync.dma_start(out=park.rearrange("o (p i) -> p (o i)", p=P), in_=log_sb[:])
            load_step(2)
            load_step(3)
            nc.sync.dma_start(out=rate_sb[:], in_=rate.rearrange("(p m) -> p m", m=M))
            load_step(4)
            load_stale(0)
            load_step(5)
            load_stale(1)
            load_step(6)
            load_step(7)

            cast_run(1, 0, HB, "cast_gpsimd")
            cast_run(1, HB, HB, "cast_gpsimd")
            scale_half(0, 0)
            scale_half(1, 0)
            scale_half(0, 1)
            scale_half(1, 1)
            cast_run(3, 0, NB, "cast_step")
            for g in range(G):
                turn_pair(0, g, g)
            warm_up(2, 7)
            scale_piece(2, 0, G, "parted_tile")
            part_query(0)
            scale_piece(3, 0, G, "parted_tile")
            turn_query(0, 0, 4)
            turn_query(0, 1, 5)
            part_query(1)
            turn_pair(1, 0, 0)
            turn_pair(1, 1, 1)
            turn_query(1, 0, 6)
            turn_query(1, 1, 7)
            turn_pair(1, 2, 2)
            turn_pair(1, 3, 3)
            quantize_keys("pair", 0, 0)
            quantize_keys("pair", 0, 1)
            quantize_query(0)
            part_query(2)
            quantize_keys("pair", 1, 0)
            part_query(3)
            quantize_query(1)
            sums[0, 0] = new_bank(4)[:]
            multiply_pair(0, 0, sums[0, 0][:, :TWO])
            cast_run(7, 0, HB, "cast_gpsimd")
            turn_query(2, 0, 0)
            turn_query(2, 1, 1)
            turn_query(3, 0, 6)
            turn_query(3, 1, 7)
            sums[0, 1] = new_bank(5)[:]
            multiply_pair(0, 1, sums[0, 1][:, :TWO])
            scale_half(4, 0)
            quantize_keys("pair", 1, 1)
            scale_half(5, 0)
            scale_half(6, 0)
            scale_half(7, 0)
            quantize_query(2)
            multiply_pair(1, 0, sums[0, 0][:, TWO:])
            multiply_pair(1, 1, sums[0, 1][:, TWO:])
            cast_run(7, HB, HB, hand(0), pool=hand_pool)
            turn_step(2)
            nc.scalar.activation(out=neg_rate[:], in_=rate_sb[:], func=COPY, scale=-1.0)
            cast_run(11, 0, HB, "cast_gpsimd")
            cast_run(9, 0, NB, "cast_step")
            scale_half(4, 1)
            quantize_query(3)
            scale_half(5, 1)
            for m in (2, 3):
                sums[0, m] = new_bank(4 + m)[:]
                multiply_pair(0, m, sums[0, m][:, :TWO])
                multiply_pair(1, m, sums[0, m][:, TWO:])
            scale_half(6, 1)
            quantize_step(2, 0)
            scale_half(7, 1)
            quantize_step(2, 1)

            for s in range(2, NS - 3):
                c, h = divmod(s, 2)
                t = 4 * (c + 1)
                if s + LOAD_AHEAD < NS:
                    load_step(s + LOAD_AHEAD)
                if h == 0 and c + 1 < NG:
                    load_stale(c + 1)
                if s + 1 < NS - 2:
                    turn_step(s + 1)
                if h == 0:
                    if s + 3 < NS - 1:
                        if c % 2 == 1:
                            cast_run(t + 1, HB, 3 * HB, hand(c), pool=hand_pool)
                        else:
                            cast_run(t + 2, HB, NB, hand(c), pool=hand_pool)
                    else:
                        cast_run(NT - 2, HB, NB, "cast_step")
                        cast_run(NT - 1, HB, HB, "cast_gpsimd")
                    gt, ga = (t + 3, 0) if s + 2 < NS - 2 else (t + 1, HB)
                    new_piece(gt, ga // PB, ga // PB + 2, hand(c - 1), pool=hand_pool)
                    scale_on_gpsimd(gt, ga, ga + HB)
                    for m in range(M):
                        finish_group(c - 1, m)
                elif s + 3 < NS - 2:
                    cast_run(t + 7, 0, HB, "cast_gpsimd")
                    cast_run(t + 5, 0, NB, "cast_step")
                else:
                    cast_run(t + 5, HB, HB, "cast_gpsimd")
                    cast_run(t + 4, HB, NB, "cast_step")
                for m in range(M):
                    multiply_step(s, m)
                if s + 2 < NS - 2:
                    for j in range(3):
                        scale_half(t + j, h)
                else:
                    scale_half(t, 1)
                    scale_half(t, 0)
                    scale_half(t + 1, 0)
                if h == 0:
                    quantize_step(s + 1)
                else:
                    quantize_step(s + 1, 0)
                    scale_half(t + 3, h)
                    quantize_step(s + 1, 1)

            v = NS - 2
            turn_unit(v, (2, 3, 0, 1))
            for m in range(M):
                multiply_step(v - 1, m)
            for h in range(2):
                scale_half(NT - 2, h)
                scale_half(NT - 1, h)
            quantize_keys("pair", v, 1)
            finish_group(NG - 2, 0)
            quantize_keys("pair", v, 0)
            finish_group(NG - 2, 1)
            turn_unit(v + 1, (0, 1, 2, 3))
            finish_group(NG - 2, 2)
            finish_group(NG - 2, 3)
            first = [new_bank(4 + m)[:, :TWO] for m in range(M)]
            for m in range(M):
                multiply_pair(v, m, first[m])
            quantize_keys("pair", v + 1, 0)
            finish(first[0], TWO * v, TWO, 0)
            second = [new_bank(m)[:, :TWO] for m in range(M - 1)]
            for m in range(2):
                multiply_pair(v + 1, m, second[m], halves=(0,))
            quantize_keys("pair", v + 1, 1)
            for m in range(1, M):
                finish(first[m], TWO * v, TWO, m)
            for m in range(2):
                multiply_pair(v + 1, m, second[m], halves=(1,))
                finish(second[m], T - TWO, TWO, m)
            multiply_pair(v + 1, 2, second[2])
            finish(second[2], T - TWO, TWO, 2)
            for j in range(2):
                end = new_bank(M - 1 + j)[:, :P]
                multiply_pair(v + 1, M - 1, end, lo=P * j, hi=P * (j + 1))
                finish(end, T - TWO + P * j, P, M - 1)
